import numpy as np
import ml_dtypes


def mxq(x, axis, fmt="e4m3"):
    dtype, down = {"e4m3": (ml_dtypes.float8_e4m3fn, 7), "e5m2": (ml_dtypes.float8_e5m2, 14)}[fmt]
    v = np.moveaxis(np.asarray(x, np.float32).astype(ml_dtypes.bfloat16).astype(np.float64), axis, -1)
    blocks = v.reshape(v.shape[:-1] + (-1, 32))
    amax = np.abs(blocks).max(-1, keepdims=True)
    byte = np.maximum(np.where(amax > 0, np.frexp(amax)[1] - 1 + 127, 0) - down, 1)
    scale = np.exp2(byte - 127.0)
    codes = (blocks / scale).astype(np.float32).astype(dtype).astype(np.float64)
    return np.moveaxis((codes * scale).reshape(v.shape), -1, axis)


WIDE = False


def mx_kscale(k):
    if not WIDE:
        return np.ones(k)
    levels = np.array([10, -10, 5, -5, 0])
    if k % 512:
        return np.exp2(np.random.permutation(np.resize(levels, k // 32))).repeat(32)
    a = np.empty((k // 512, 16))
    for p in range(k // 512):
        a[p, :8] = np.random.permutation(np.resize(levels, 8))
        for g in range(8):
            far = levels[np.abs(levels - a[p, g]) >= 10]
            a[p, g + 8] = far[np.random.randint(len(far))]
    return np.exp2(a.ravel()).repeat(32)


def f64(x):
    return np.asarray(x).astype(np.float64)


def striped(idx):
    return np.tile(idx.reshape(-1, 16).T, (8, 1)).astype(np.uint16)


def unstriped(offs):
    return offs[:16].T.reshape(-1).astype(np.int64)


E2M1 = np.array([0.0, 0.5, 1.0, 1.5, 2.0, 3.0, 4.0, 6.0, -0.0, -0.5, -1.0, -1.5, -2.0, -3.0, -4.0, -6.0])


def pack_weight(w, fmt):
    k, n = w.shape
    w = f64(np.asarray(w, np.float32).astype(ml_dtypes.bfloat16)).reshape(k // 32, 32, n)
    amax = np.abs(w).max(1)
    if fmt == "e4m3":
        byte = np.frexp(amax)[1] - 1 + 127 - 7
    else:
        mant, ex = np.frexp(amax / 6.0)
        byte = np.where(mant > 0.5, ex, ex - 1) + 127
    byte = np.clip(np.where(amax > 0, byte, 1), 1, 254)
    scaled = (w * np.exp2(127.0 - byte)[:, None, :]).reshape(k, n).astype(np.float32)
    by_word = np.ascontiguousarray(scaled.reshape(k // 512, 128, 4, n).transpose(0, 1, 3, 2))
    if fmt == "e4m3":
        words = by_word.astype(ml_dtypes.float8_e4m3fn).view(np.uint8)
    else:
        c = by_word.astype(ml_dtypes.float4_e2m1fn).view(np.uint8) & 0xF
        words = (c[..., 0::2] | (c[..., 1::2] << 4)).reshape(k // 512, 128, 2 * n)
    return np.ascontiguousarray(words), np.ascontiguousarray(byte.astype(np.uint8).reshape(k // 512, 16, n))


def unpack_weight(words, scales, fmt):
    g, _, n = scales.shape
    words = np.ascontiguousarray(words).reshape(g, 128, n, -1)
    if fmt == "e4m3":
        vals = words.view(ml_dtypes.float8_e4m3fn).astype(np.float64)
    else:
        nib = np.empty((g, 128, n, 4), np.uint8)
        nib[..., 0::2] = words & 0xF
        nib[..., 1::2] = words >> 4
        vals = E2M1[nib]
    vals = vals * np.repeat(np.exp2(scales.astype(np.float64) - 127.0), 8, axis=1)[..., None]
    return vals.transpose(0, 1, 3, 2).reshape(g * 512, n)


def gelu(v):
    return 0.5 * v * (1.0 + np.tanh(np.sqrt(2.0 / np.pi) * (v + 0.044715 * v**3)))


def striped8(idx):
    return np.concatenate([v.reshape(-1, 16).T for v in idx]).astype(np.uint16)


def unstriped8(offs):
    return np.stack([offs[16 * g:16 * g + 16].T.reshape(-1) for g in range(8)]).astype(np.int64)


def runs(v, idx8):
    k = np.arange(v.shape[0])
    return v[k[:, None], idx8[k % 512 // 64]]


K, K2, H, N, T, T2, S = 1024, 512, 1024, 512, 2048, 2048, 512

def setup_inputs():
    n = np.random.standard_normal
    s = mx_kscale(K)[:, None]
    s2 = mx_kscale(K2)[:, None]
    u = mx_kscale(H)[:, None]
    tab_words, tab_scales = pack_weight(n((K, T)) * s, "e4m3")
    tab2_words, tab2_scales = pack_weight(n((K2, T2)) * s2, "e4m3")
    wa_words, wa_scales = pack_weight(1.5 * n((K, H)) / np.sqrt(K) / s * u.T, "e2m1")
    wp_words, wp_scales = pack_weight(n((K2, H)) / np.sqrt(K2) / s2 * u.T, "e4m3")
    return {
        "tab_words": tab_words, "tab_scales": tab_scales,
        "tab2_words": tab2_words, "tab2_scales": tab2_scales,
        "offs": striped8(np.stack([np.random.permutation(T)[:S] for _ in range(8)])),
        "offs2": striped(np.random.permutation(T2)[:S]),
        "wa_words": wa_words, "wa_scales": wa_scales,
        "ws": (n((K, H)) / np.sqrt(K) / s).astype(np.float32),
        "base": np.exp(0.3 * n(H)).astype(np.float32),
        "wp_words": wp_words, "wp_scales": wp_scales,
        "wc": (n((H, N)) / np.sqrt(H) / u).astype(np.float32),
    }

def reference(tab_words, tab_scales, tab2_words, tab2_scales, offs, offs2,
              wa_words, wa_scales, ws, base, wp_words, wp_scales, wc):
    v = runs(unpack_weight(tab_words, tab_scales, "e4m3"), unstriped8(offs))
    v2 = unpack_weight(tab2_words, tab2_scales, "e4m3")[:, unstriped(offs2)]
    wa = unpack_weight(wa_words, wa_scales, "e2m1")
    wp = unpack_weight(wp_words, wp_scales, "e4m3")
    a = wa.T @ v
    b = mxq(f64(ws), 0, "e4m3").T @ v
    p = wp.T @ v2
    q = np.abs(a) / (f64(base)[:, None] + np.square(b))
    d = np.abs(q - p)
    return mxq(f64(wc), 0, "e4m3").T @ mxq(d, 0, "e4m3")

@@ -1,0 +1,337 @@
+from contextlib import ExitStack
+
+import concourse.mybir as mybir
+
+K, K2, H, N, T, S = 1024, 512, 1024, 512, 2048, 512
+FLOPS = 2 * S * (2 * K * H + K2 * H + H * N)
+
+F32 = mybir.dt.float32
+BF16 = mybir.dt.bfloat16
+I32 = mybir.dt.int32
+U32 = mybir.dt.uint32
+U16 = mybir.dt.uint16
+U8 = mybir.dt.uint8
+E4M3 = mybir.dt.float8_e4m3fn_x4
+E2M1 = mybir.dt.float4_e2m1fn_x4
+ACT = mybir.ActivationFunctionType
+ALU = mybir.AluOpType
+
+P = 128
+PACK = 4
+KP = P * PACK
+JQ = 128
+NQ = S // JQ
+
+
+def tile_list_tint_adjustment_kernel(
+    tc, tab_words, tab_scales, tab2_words, tab2_scales, offs, offs2,
+    wa_words, wa_scales, ws, base, wp_words, wp_scales, wc, out,
+):
+    nc = tc.nc
+    with ExitStack() as ctx:
+        keep = ctx.enter_context(tc.tile_pool(name="keep", bufs=1))
+        work = ctx.enter_context(tc.tile_pool(name="work", bufs=3))
+        psum = ctx.enter_context(tc.psum_pool(name="psum", bufs=2))
+
+        def held(shape, dtype, name, tag=None):
+            return keep.tile(shape, dtype, name=name, tag=tag or name, align_bytes=64)
+
+        lists = keep.tile([P, S // 16], U16, name="lists")
+        lists2 = keep.tile([P, S // 16], U16, name="lists2")
+
+        tab_rows = [held([P, T], U8, f"tab_rows{x}") for x in range(3)]
+        w_rows = held([P, 3 * H], U8, "w_rows")
+        base_rows = held([P, P], F32, "base_rows")
+        planes = held([P, 3 * S + 3 * H], U8, "planes")
+        warm = held([P, 8], F32, "warm")
+        warm_out = held([P, 8], F32, "warm_out")
+        nc.gpsimd.memset(tab_rows[0][:].bitcast(I32), 0)
+        nc.vector.memset(tab_rows[1][:].bitcast(I32), 0)
+        nc.gpsimd.memset(tab_rows[2][:].bitcast(I32), 0)
+        nc.vector.memset(w_rows[:].bitcast(I32), 0)
+        nc.vector.memset(base_rows[:], 0.0)
+        nc.vector.memset(warm[:], 1.0)
+        nc.gpsimd.memset(planes[:].bitcast(I32), 0)
+
+        ws_raw = {}
+
+        def load_ws(b, a):
+            ws_raw[b, a] = held([P, PACK, KP], F32, f"ws_raw{b}{a}", f"ws_raw{a}")
+            nc.sync.dma_start(
+                out=ws_raw[b, a][:],
+                in_=ws[a * KP:(a + 1) * KP, b * KP:(b + 1) * KP].rearrange("(p j) c -> p j c", j=PACK),
+            )
+
+        windows = {}
+        table_words = [tab_words[0], tab_words[1], tab2_words[0]]
+        table_scales = [tab_scales[0], tab_scales[1], tab2_scales[0]]
+        table_lists = [lists, lists, lists2]
+
+        def load_window(x, tag):
+            windows[x] = held([P, T], I32, f"window{x}", tag)
+            nc.sync.dma_start(out=windows[x][:], in_=table_words[x].rearrange("p t i -> p (t i)").bitcast(I32))
+
+        def load_rows(x):
+            nc.scalar.dma_start(out=tab_rows[x][0:P:8, :].bitcast(I32), in_=table_scales[x].bitcast(I32))
+
+        wa_raw, wp_raw, wc_raw = {}, {}, {}
+
+        def load_wa(b):
+            wa_raw[b] = held([P, 2, KP // 2], I32, f"wa_raw{b}", "wa_raw")
+            nc.sync.dma_start(
+                out=wa_raw[b][:],
+                in_=wa_words.bitcast(I32)[:, :, b * (KP // 2):(b + 1) * (KP // 2)].rearrange("a p c -> p a c"),
+            )
+
+        def load_wp(b):
+            wp_raw[b] = held([P, KP], I32, f"wp_raw{b}", "w_rows")
+            nc.sync.dma_start(
+                out=wp_raw[b][:],
+                in_=wp_words[0].rearrange("p c i -> p (c i)").bitcast(I32)[:, b * KP:(b + 1) * KP],
+            )
+
+        def load_wc(b):
+            wc_raw[b] = held([P, PACK, N], F32, f"wc_raw{b}", f"window{b}")
+            rows = wc[b * KP:(b + 1) * KP, :].rearrange("(h t i) n -> t h i n", t=PACK, i=4)
+            for t in range(PACK):
+                nc.sync.dma_start(out=wc_raw[b][:, t, :], in_=rows[t])
+
+        nc.sync.dma_start(lists[:], offs)
+        load_ws(0, 0)
+        load_rows(0)
+        load_rows(1)
+        nc.sync.dma_start(lists2[:], offs2)
+        load_rows(2)
+        nc.scalar.dma_start(
+            out=w_rows[0:P:8, 0:2 * H].bitcast(I32).rearrange("q (a c) -> q a c", a=2),
+            in_=wa_scales.bitcast(I32).rearrange("a q c -> q a c"),
+        )
+        nc.scalar.dma_start(out=w_rows[0:P:8, 2 * H:3 * H].bitcast(I32), in_=wp_scales[0].bitcast(I32))
+        nc.scalar.activation(out=warm_out[:], in_=warm[:], func=ACT.Abs_reciprocal_sqrt)
+        load_ws(0, 1)
+        load_window(0, "window0")
+        load_window(1, "window1")
+        nc.sync.dma_start(out=base_rows[0:P:16, :], in_=base.rearrange("(b q x) -> q b x", b=2, q=4))
+        load_wa(0)
+
+        picked_rows = held([P, 3 * S], U8, "picked_rows")
+        staged = held([P, 3 * S + 3 * H], U8, "staged")
+        for x in range(3):
+            nc.vector.tensor_copy(out=picked_rows[:, x * S:(x + 1) * S], in_=tab_rows[x][:].indirect(table_lists[x][:]))
+        nc.vector.tensor_copy(
+            out=staged[:, 3 * S:].bitcast(I32).rearrange("p (s t h) -> p s h t", t=PACK, h=32),
+            in_=w_rows[:].bitcast(I32).rearrange("p (s h t) -> p s h t", t=PACK, h=32),
+        )
+        nc.vector.tensor_copy(out=staged[:, 0:3 * S].bitcast(I32), in_=picked_rows[:].bitcast(I32))
+        for d in range(4):
+            nc.scalar.dma_start(
+                out=planes[32 * d:32 * d + 4, :].bitcast(I32),
+                in_=staged[32 * d:32 * d + 32:8, :].bitcast(I32),
+            )
+
+        load_window(2, "picked_rows")
+        load_wp(0)
+
+        def picked_plane(x, cols):
+            return planes[:, x * S + cols.start:x * S + cols.stop]
+
+        def weight_plane(s, b, t):
+            c0 = 3 * S + s * H + b * KP + t * P
+            return planes[:, c0:c0 + P]
+
+        base_sorted = held([P, P], F32, "base_sorted")
+        nc.vector.tensor_copy(
+            out=base_sorted[:].rearrange("p (t h i) -> p t h i", t=PACK, i=4),
+            in_=base_rows[:].rearrange("p (h t i) -> p t h i", t=PACK, i=4),
+        )
+        base_cols = held([P, P], F32, "base_cols")
+        nc.vector.transpose(out=base_cols[:], in_=base_sorted[:])
+
+        ws_codes, ws_plane = {}, {}
+
+        def round_ws(b, a, t, engine_copy, grouped):
+            engine_copy(
+                out=grouped[:, t * KP:(t + 1) * KP].rearrange("p (h i j) -> p h j i", i=4, j=PACK),
+                in_=ws_raw[b, a][:].rearrange("p j (h t i) -> p t h j i", t=PACK, i=4)[:, t],
+            )
+
+        def quantize(grouped, width, name):
+            codes = held([P, width], U32, name + "_codes")
+            plane = held([P, width], U8, name + "_plane")
+            nc.vector.quantize_mx(out=codes[:].bitcast(E4M3), scales=plane[:], in_=grouped)
+            return codes, plane
+
+        picked = [held([P, S], U32, f"picked{x}") for x in range(3)]
+
+        def gather(x, half):
+            nc.vector.tensor_copy(
+                out=picked[x][:, half * 256:(half + 1) * 256],
+                in_=windows[x][:].bitcast(U32).indirect(table_lists[x][:, half * 16:(half + 1) * 16]),
+            )
+
+        wa_codes, wp_codes = {}, {}
+
+        def sort_wa(b):
+            wa_codes[b] = held([P, 2, KP // 2], I32, f"wa_codes{b}")
+            nc.vector.tensor_copy(
+                out=wa_codes[b][:].rearrange("p a (t h w) -> p a h t w", t=PACK, w=2),
+                in_=wa_raw[b][:].rearrange("p a (h t w) -> p a h t w", t=PACK, w=2),
+            )
+
+        def sort_wp(b):
+            wp_codes[b] = held([P, KP], I32, f"wp_codes{b}")
+            nc.vector.tensor_copy(
+                out=wp_codes[b][:].rearrange("p (t h i) -> p h t i", t=PACK, i=4),
+                in_=wp_raw[b][:].rearrange("p (h t i) -> p h t i", t=PACK, i=4),
+            )
+
+        def prepare_ws(b, a, engine_copy):
+            grouped = held([P, PACK * KP], BF16, f"ws_grouped{b}{a}")
+            steps = [lambda t=t: round_ws(b, a, t, engine_copy, grouped) for t in range(PACK)]
+
+            def finish():
+                ws_codes[b, a], ws_plane[b, a] = quantize(grouped[:], KP, f"ws{b}{a}")
+
+            return steps + [finish]
+
+        wc_codes, wc_plane = {}, {}
+
+        def prepare_wc(b):
+            grouped = held([P, PACK * N], BF16, f"wc_grouped{b}")
+
+            def round_wc(n):
+                nc.vector.tensor_copy(
+                    out=grouped[:, n * KP:(n + 1) * KP].rearrange("p (c i t) -> p c t i", i=4, t=PACK),
+                    in_=wc_raw[b][:, :, n * P:(n + 1) * P].rearrange("p t (c i) -> p c t i", i=4),
+                )
+
+            def finish():
+                wc_codes[b], wc_plane[b] = quantize(grouped[:], N, f"wc{b}")
+
+            return [lambda n=n: round_wc(n) for n in range(PACK)] + [finish]
+
+        for step in prepare_ws(0, 0, nc.scalar.copy) + prepare_ws(0, 1, nc.scalar.copy):
+            step()
+        load_ws(1, 0)
+        load_ws(1, 1)
+        gather(0, 0)
+        gather(0, 1)
+        gather(1, 0)
+        sort_wa(0)
+        gather(1, 1)
+        gather(2, 0)
+        sort_wp(0)
+        gather(2, 1)
+        load_wa(1)
+        load_wp(1)
+        load_wc(0)
+        load_wc(1)
+
+        d_codes, d_plane, diffs = {}, {}, {}
+
+        def first_stage(b, j0, width, t0):
+            slots = KP // width
+            scat = psum.tile([P, slots, width], F32, name="scat")
+            absorb = psum.tile([P, slots, width], F32, name="absorb")
+            panel = psum.tile([P, slots, width], F32, name="panel")
+            cols = slice(j0, j0 + width)
+            for a in range(2):
+                for s in range(slots):
+                    t = t0 + s
+                    nc.tensor.matmul_mx(
+                        out=scat[:, s, :],
+                        lhsT=ws_codes[b, a][:, t * P:(t + 1) * P].bitcast(E4M3),
+                        lhsT_scale=ws_plane[b, a][:, t * P:(t + 1) * P],
+                        rhs=picked[a][:, cols].bitcast(E4M3), rhs_scale=picked_plane(a, cols),
+                        start=(a == 0 and s == 0), stop=(a == 1 and s == slots - 1),
+                    )
+            for a in range(2):
+                for s in range(slots):
+                    t = t0 + s
+                    for c0 in range(0, width, JQ):
+                        part = slice(j0 + c0, j0 + c0 + JQ)
+                        nc.tensor.matmul_mx(
+                            out=absorb[:, s, c0:c0 + JQ],
+                            lhsT=wa_codes[b][:, a, t * 64:(t + 1) * 64].bitcast(U8).bitcast(E2M1),
+                            lhsT_scale=weight_plane(a, b, t),
+                            rhs=picked[a][:, part].bitcast(E4M3), rhs_scale=picked_plane(a, part),
+                            start=(a == 0 and s == 0 and c0 == 0),
+                            stop=(a == 1 and s == slots - 1 and c0 + JQ == width),
+                        )
+            for s in range(slots):
+                t = t0 + s
+                nc.tensor.matmul_mx(
+                    out=panel[:, s, :],
+                    lhsT=wp_codes[b][:, t * P:(t + 1) * P].bitcast(E4M3),
+                    lhsT_scale=weight_plane(2, b, t),
+                    rhs=picked[2][:, cols].bitcast(E4M3), rhs_scale=picked_plane(2, cols),
+                    start=True, stop=True,
+                )
+            sq = work.tile([P, slots, width], F32, name="sq")
+            nc.scalar.activation(out=sq[:], in_=scat[:], func=ACT.Square)
+            root = work.tile([P, slots, width], F32, name="root")
+            for s in range(slots):
+                col = 32 * (t0 + s) + 16 * b
+                nc.scalar.activation(out=root[:, s, :], in_=sq[:, s, :], func=ACT.Abs_reciprocal_sqrt, bias=base_cols[:, col:col + 1])
+            recip = work.tile([P, slots, width], F32, name="recip")
+            nc.scalar.activation(out=recip[:], in_=root[:], func=ACT.Square)
+            signed = work.tile([P, slots, width], F32, name="signed")
+            nc.vector.tensor_tensor(out=signed[:], in0=absorb[:], in1=recip[:], op=ALU.mult)
+            quot = work.tile([P, slots, width], F32, name="quot")
+            nc.scalar.activation(out=quot[:], in_=signed[:], func=ACT.Abs)
+            if t0 == 0:
+                diffs[b, j0] = work.tile([P, PACK, width], F32, name="diff")
+            nc.vector.tensor_tensor(out=diffs[b, j0][:, t0:t0 + slots, :], in0=panel[:], in1=quot[:], op=ALU.subtract)
+
+        def quantize_d(b, j0, width):
+            dist = work.tile([P, width * PACK], BF16, name="dist", align_bytes=64)
+            nc.scalar.activation(
+                out=dist[:].rearrange("p (c i t) -> p c t i", i=4, t=PACK),
+                in_=diffs[b, j0][:].rearrange("p t (c i) -> p c t i", i=4),
+                func=ACT.Abs,
+            )
+            codes, plane = quantize(dist[:], width, f"d{b}{j0}")
+            for c0 in range(0, width, JQ):
+                d_codes[b, j0 + c0], d_plane[b, j0 + c0] = codes[:, c0:c0 + JQ], plane[:, c0:c0 + JQ]
+
+        def second_stage(j0):
+            acc = psum.tile([P, PACK, JQ], F32, name="acc")
+            for b in range(2):
+                for n in range(PACK):
+                    nc.tensor.matmul_mx(
+                        out=acc[:, n, :],
+                        lhsT=wc_codes[b][:, n * P:(n + 1) * P].bitcast(E4M3),
+                        lhsT_scale=wc_plane[b][:, n * P:(n + 1) * P],
+                        rhs=d_codes[b, j0].bitcast(E4M3), rhs_scale=d_plane[b, j0],
+                        start=(b == 0 and n == 0), stop=(b == 1 and n == PACK - 1),
+                    )
+            result = work.tile([P, PACK, JQ], F32, name="result")
+            nc.vector.tensor_copy(out=result[:], in_=acc[:])
+            nc.sync.dma_start(
+                out=out[:, j0:j0 + JQ].rearrange("(n p) j -> p n j", p=P),
+                in_=result[:],
+            )
+
+        def columns(b, j0, width):
+            for t0 in range(0, PACK, KP // width):
+                first_stage(b, j0, width, t0)
+            quantize_d(b, j0, width)
+
+        half = S // 2
+        columns(0, 0, half)
+        for step in prepare_ws(1, 0, nc.vector.tensor_copy):
+            step()
+        columns(0, half, half)
+        for step in prepare_ws(1, 1, nc.vector.tensor_copy):
+            step()
+        sort_wa(1)
+        sort_wp(1)
+        columns(1, 0, half)
+        for step in prepare_wc(0) + prepare_wc(1):
+            step()
+        columns(1, half, JQ)
+        second_stage(0)
+        second_stage(JQ)
+        columns(1, half + JQ, JQ)
+        second_stage(half)
+        second_stage(half + JQ)

@@ -42,21 +42,21 @@ def tile_list_tint_adjustment_kernel(
         tab_rows = [held([P, T], U8, f"tab_rows{x}") for x in range(3)]
         w_rows = held([P, 3 * H], U8, "w_rows")
         base_rows = held([P, P], F32, "base_rows")
-        planes = held([P, 3 * S + 3 * H], U8, "planes")
+        planes = held([P, S + 3 * H], U8, "planes")
         warm = held([P, 8], F32, "warm")
         warm_out = held([P, 8], F32, "warm_out")
         nc.gpsimd.memset(tab_rows[0][:].bitcast(I32), 0)
         nc.vector.memset(tab_rows[1][:].bitcast(I32), 0)
+        nc.vector.memset(warm[:], 1.0)
         nc.gpsimd.memset(tab_rows[2][:].bitcast(I32), 0)
         nc.vector.memset(w_rows[:].bitcast(I32), 0)
         nc.vector.memset(base_rows[:], 0.0)
-        nc.vector.memset(warm[:], 1.0)
         nc.gpsimd.memset(planes[:].bitcast(I32), 0)
 
         ws_raw = {}
 
         def load_ws(b, a):
-            ws_raw[b, a] = held([P, PACK, KP], F32, f"ws_raw{b}{a}", f"ws_raw{a}")
+            ws_raw[b, a] = held([P, PACK, KP], F32, f"ws_raw{b}{a}")
             nc.sync.dma_start(
                 out=ws_raw[b, a][:],
                 in_=ws[a * KP:(a + 1) * KP, b * KP:(b + 1) * KP].rearrange("(p j) c -> p j c", j=PACK),
@@ -67,8 +67,8 @@ def tile_list_tint_adjustment_kernel(
         table_scales = [tab_scales[0], tab_scales[1], tab2_scales[0]]
         table_lists = [lists, lists, lists2]
 
-        def load_window(x, tag):
-            windows[x] = held([P, T], I32, f"window{x}", tag)
+        def load_window(x):
+            windows[x] = held([P, T], I32, f"window{x}")
             nc.sync.dma_start(out=windows[x][:], in_=table_words[x].rearrange("p t i -> p (t i)").bitcast(I32))
 
         def load_rows(x):
@@ -77,66 +77,68 @@ def tile_list_tint_adjustment_kernel(
         wa_raw, wp_raw, wc_raw = {}, {}, {}
 
         def load_wa(b):
-            wa_raw[b] = held([P, 2, KP // 2], I32, f"wa_raw{b}", "wa_raw")
+            wa_raw[b] = held([P, 2, KP // 2], I32, f"wa_raw{b}")
             nc.sync.dma_start(
                 out=wa_raw[b][:],
                 in_=wa_words.bitcast(I32)[:, :, b * (KP // 2):(b + 1) * (KP // 2)].rearrange("a p c -> p a c"),
             )
 
         def load_wp(b):
-            wp_raw[b] = held([P, KP], I32, f"wp_raw{b}", "w_rows")
+            wp_raw[b] = held([P, KP], I32, f"wp_raw{b}")
             nc.sync.dma_start(
                 out=wp_raw[b][:],
                 in_=wp_words[0].rearrange("p c i -> p (c i)").bitcast(I32)[:, b * KP:(b + 1) * KP],
             )
 
         def load_wc(b):
-            wc_raw[b] = held([P, PACK, N], F32, f"wc_raw{b}", f"window{b}")
+            wc_raw[b] = held([P, PACK, N], F32, f"wc_raw{b}")
             rows = wc[b * KP:(b + 1) * KP, :].rearrange("(h t i) n -> t h i n", t=PACK, i=4)
             for t in range(PACK):
                 nc.sync.dma_start(out=wc_raw[b][:, t, :], in_=rows[t])
 
         nc.sync.dma_start(lists[:], offs)
         load_ws(0, 0)
+        nc.sync.dma_start(lists2[:], offs2)
+        load_ws(0, 1)
+        load_window(0)
+        load_window(1)
+        load_wa(0)
+        load_ws(1, 0)
+        load_window(2)
+        load_wp(0)
+        load_ws(1, 1)
+        load_wa(1)
+        load_wp(1)
+        load_wc(0)
+        load_wc(1)
         load_rows(0)
         load_rows(1)
-        nc.sync.dma_start(lists2[:], offs2)
+        nc.scalar.activation(out=warm_out[:], in_=warm[:], func=ACT.Abs_reciprocal_sqrt)
         load_rows(2)
         nc.scalar.dma_start(
             out=w_rows[0:P:8, 0:2 * H].bitcast(I32).rearrange("q (a c) -> q a c", a=2),
             in_=wa_scales.bitcast(I32).rearrange("a q c -> q a c"),
         )
         nc.scalar.dma_start(out=w_rows[0:P:8, 2 * H:3 * H].bitcast(I32), in_=wp_scales[0].bitcast(I32))
-        nc.scalar.activation(out=warm_out[:], in_=warm[:], func=ACT.Abs_reciprocal_sqrt)
-        load_ws(0, 1)
-        load_window(0, "window0")
-        load_window(1, "window1")
-        nc.sync.dma_start(out=base_rows[0:P:16, :], in_=base.rearrange("(b q x) -> q b x", b=2, q=4))
-        load_wa(0)
+        nc.scalar.dma_start(out=base_rows[0:P:16, :], in_=base.rearrange("(b q x) -> q b x", b=2, q=4))
 
-        picked_rows = held([P, 3 * S], U8, "picked_rows")
-        staged = held([P, 3 * S + 3 * H], U8, "staged")
-        for x in range(3):
-            nc.vector.tensor_copy(out=picked_rows[:, x * S:(x + 1) * S], in_=tab_rows[x][:].indirect(table_lists[x][:]))
+        picked_rows = held([P, 2 * S], U8, "picked_rows")
+        picked_rows2 = held([P, S], U8, "picked_rows2")
+        for x in range(2):
+            nc.vector.tensor_copy(out=picked_rows[:, x * S:(x + 1) * S], in_=tab_rows[x][:].indirect(lists[:]))
+        nc.vector.tensor_copy(out=picked_rows2[:], in_=tab_rows[2][:].indirect(lists2[:]))
+        staged = held([P, S + 3 * H], U8, "staged")
+        nc.vector.tensor_copy(out=staged[:, 0:S].bitcast(I32), in_=picked_rows2[:].bitcast(I32))
         nc.vector.tensor_copy(
-            out=staged[:, 3 * S:].bitcast(I32).rearrange("p (s t h) -> p s h t", t=PACK, h=32),
-            in_=w_rows[:].bitcast(I32).rearrange("p (s h t) -> p s h t", t=PACK, h=32),
+            out=staged[:, S:].bitcast(I32).rearrange("p (s t g h) -> p s g t h", t=PACK, g=8, h=4),
+            in_=w_rows[:].bitcast(I32).rearrange("p (s g h t) -> p s g t h", t=PACK, g=8, h=4),
         )
-        nc.vector.tensor_copy(out=staged[:, 0:3 * S].bitcast(I32), in_=picked_rows[:].bitcast(I32))
-        for d in range(4):
-            nc.scalar.dma_start(
-                out=planes[32 * d:32 * d + 4, :].bitcast(I32),
-                in_=staged[32 * d:32 * d + 32:8, :].bitcast(I32),
-            )
-
-        load_window(2, "picked_rows")
-        load_wp(0)
 
         def picked_plane(x, cols):
-            return planes[:, x * S + cols.start:x * S + cols.stop]
+            return tab_planes[:, x * S + cols.start:x * S + cols.stop] if x < 2 else planes[:, cols]
 
         def weight_plane(s, b, t):
-            c0 = 3 * S + s * H + b * KP + t * P
+            c0 = S + s * H + b * KP + t * P
             return planes[:, c0:c0 + P]
 
         base_sorted = held([P, P], F32, "base_sorted")
@@ -148,11 +150,12 @@ def tile_list_tint_adjustment_kernel(
         nc.vector.transpose(out=base_cols[:], in_=base_sorted[:])
 
         ws_codes, ws_plane = {}, {}
+        on_scalar, on_vector = nc.scalar.copy, nc.vector.tensor_copy
 
-        def round_ws(b, a, t, engine_copy, grouped):
+        def round_ws(b, a, t0, engine_copy, grouped):
             engine_copy(
-                out=grouped[:, t * KP:(t + 1) * KP].rearrange("p (h i j) -> p h j i", i=4, j=PACK),
-                in_=ws_raw[b, a][:].rearrange("p j (h t i) -> p t h j i", t=PACK, i=4)[:, t],
+                out=grouped[:, t0 * KP:(t0 + 2) * KP].rearrange("p (t h i j) -> p t h j i", t=2, i=4, j=PACK),
+                in_=ws_raw[b, a][:].rearrange("p j (h t i) -> p t h j i", t=PACK, i=4)[:, t0:t0 + 2],
             )
 
         def quantize(grouped, width, name):
@@ -171,23 +174,23 @@ def tile_list_tint_adjustment_kernel(
 
         wa_codes, wp_codes = {}, {}
 
-        def sort_wa(b):
-            wa_codes[b] = held([P, 2, KP // 2], I32, f"wa_codes{b}")
+        def sort_wa(b, tag=None):
+            wa_codes[b] = held([P, 2, KP // 2], I32, f"wa_codes{b}", tag)
             nc.vector.tensor_copy(
-                out=wa_codes[b][:].rearrange("p a (t h w) -> p a h t w", t=PACK, w=2),
-                in_=wa_raw[b][:].rearrange("p a (h t w) -> p a h t w", t=PACK, w=2),
+                out=wa_codes[b][:].rearrange("p a (t h w) -> p a t h w", t=PACK, w=2),
+                in_=wa_raw[b][:].rearrange("p a (h t w) -> p a t h w", t=PACK, w=2),
             )
 
-        def sort_wp(b):
-            wp_codes[b] = held([P, KP], I32, f"wp_codes{b}")
+        def sort_wp(b, tag=None):
+            wp_codes[b] = held([P, KP], I32, f"wp_codes{b}", tag)
             nc.vector.tensor_copy(
                 out=wp_codes[b][:].rearrange("p (t h i) -> p h t i", t=PACK, i=4),
                 in_=wp_raw[b][:].rearrange("p (h t i) -> p h t i", t=PACK, i=4),
             )
 
-        def prepare_ws(b, a, engine_copy):
-            grouped = held([P, PACK * KP], BF16, f"ws_grouped{b}{a}")
-            steps = [lambda t=t: round_ws(b, a, t, engine_copy, grouped) for t in range(PACK)]
+        def prepare_ws(b, a, copies, tag=None):
+            grouped = held([P, PACK * KP], BF16, f"ws_grouped{b}{a}", tag)
+            steps = [lambda x=x: round_ws(b, a, 2 * x, copies[x], grouped) for x in range(2)]
 
             def finish():
                 ws_codes[b, a], ws_plane[b, a] = quantize(grouped[:], KP, f"ws{b}{a}")
@@ -201,137 +204,200 @@ def tile_list_tint_adjustment_kernel(
 
             def round_wc(n):
                 nc.vector.tensor_copy(
-                    out=grouped[:, n * KP:(n + 1) * KP].rearrange("p (c i t) -> p c t i", i=4, t=PACK),
-                    in_=wc_raw[b][:, :, n * P:(n + 1) * P].rearrange("p t (c i) -> p c t i", i=4),
+                    out=grouped[:, n * KP:(n + 2) * KP].rearrange("p (c i t) -> p c t i", i=4, t=PACK),
+                    in_=wc_raw[b][:, :, n * P:(n + 2) * P].rearrange("p t (c i) -> p c t i", i=4),
                 )
 
             def finish():
                 wc_codes[b], wc_plane[b] = quantize(grouped[:], N, f"wc{b}")
 
-            return [lambda n=n: round_wc(n) for n in range(PACK)] + [finish]
+            return [lambda n=n: round_wc(n) for n in (0, 2)] + [finish]
 
-        for step in prepare_ws(0, 0, nc.scalar.copy) + prepare_ws(0, 1, nc.scalar.copy):
+        def move_rows(dst, src):
+            for d in range(4):
+                nc.scalar.dma_start(out=dst[32 * d:32 * d + 4, :].bitcast(I32), in_=src[32 * d:32 * d + 32:8, :].bitcast(I32))
+
+        for step in prepare_ws(0, 0, [on_scalar] * 2):
             step()
-        load_ws(1, 0)
-        load_ws(1, 1)
+        tab_planes = held([P, 2 * S], U8, "tab_planes", "ws_raw00")
+        nc.vector.memset(tab_planes[:].bitcast(I32), 0)
+        move_rows(tab_planes, picked_rows)
         gather(0, 0)
         gather(0, 1)
+        for step in prepare_ws(0, 1, [on_scalar] * 2):
+            step()
+        move_rows(planes, staged)
         gather(1, 0)
         sort_wa(0)
         gather(1, 1)
         gather(2, 0)
         sort_wp(0)
         gather(2, 1)
-        load_wa(1)
-        load_wp(1)
-        load_wc(0)
-        load_wc(1)
 
-        d_codes, d_plane, diffs = {}, {}, {}
+        half = S // 2
+        units = [(0, j0, half, t0) for j0 in (0, half) for t0 in (0, 2)] + [(1, 0, half, 0), (1, 0, half, 2), (1, half, JQ, 0), (1, half + JQ, JQ, 0)]
+        scat, absorb, panel, sq, root, recip, signed, quot = {}, {}, {}, {}, {}, {}, {}, {}
+        diffs, dist, d_codes, d_plane = {}, {}, {}, {}
 
-        def first_stage(b, j0, width, t0):
+        def shape_of(u):
+            width = units[u][2]
+            return [P, KP // width, width]
+
+        def scat_products(u):
+            b, j0, width, t0 = units[u]
             slots = KP // width
-            scat = psum.tile([P, slots, width], F32, name="scat")
-            absorb = psum.tile([P, slots, width], F32, name="absorb")
-            panel = psum.tile([P, slots, width], F32, name="panel")
             cols = slice(j0, j0 + width)
+            scat[u] = psum.tile(shape_of(u), F32, name="scat")
             for a in range(2):
                 for s in range(slots):
                     t = t0 + s
                     nc.tensor.matmul_mx(
-                        out=scat[:, s, :],
+                        out=scat[u][:, s, :],
                         lhsT=ws_codes[b, a][:, t * P:(t + 1) * P].bitcast(E4M3),
                         lhsT_scale=ws_plane[b, a][:, t * P:(t + 1) * P],
                         rhs=picked[a][:, cols].bitcast(E4M3), rhs_scale=picked_plane(a, cols),
                         start=(a == 0 and s == 0), stop=(a == 1 and s == slots - 1),
                     )
+
+        def absorb_products(u):
+            b, j0, width, t0 = units[u]
+            slots = KP // width
+            absorb[u] = psum.tile(shape_of(u), F32, name="absorb")
             for a in range(2):
                 for s in range(slots):
                     t = t0 + s
                     for c0 in range(0, width, JQ):
                         part = slice(j0 + c0, j0 + c0 + JQ)
                         nc.tensor.matmul_mx(
-                            out=absorb[:, s, c0:c0 + JQ],
+                            out=absorb[u][:, s, c0:c0 + JQ],
                             lhsT=wa_codes[b][:, a, t * 64:(t + 1) * 64].bitcast(U8).bitcast(E2M1),
                             lhsT_scale=weight_plane(a, b, t),
                             rhs=picked[a][:, part].bitcast(E4M3), rhs_scale=picked_plane(a, part),
                             start=(a == 0 and s == 0 and c0 == 0),
                             stop=(a == 1 and s == slots - 1 and c0 + JQ == width),
                         )
-            for s in range(slots):
+
+        def panel_products(u):
+            b, j0, width, t0 = units[u]
+            cols = slice(j0, j0 + width)
+            panel[u] = psum.tile(shape_of(u), F32, name="panel")
+            for s in range(KP // width):
                 t = t0 + s
                 nc.tensor.matmul_mx(
-                    out=panel[:, s, :],
+                    out=panel[u][:, s, :],
                     lhsT=wp_codes[b][:, t * P:(t + 1) * P].bitcast(E4M3),
                     lhsT_scale=weight_plane(2, b, t),
                     rhs=picked[2][:, cols].bitcast(E4M3), rhs_scale=picked_plane(2, cols),
                     start=True, stop=True,
                 )
-            sq = work.tile([P, slots, width], F32, name="sq")
-            nc.scalar.activation(out=sq[:], in_=scat[:], func=ACT.Square)
-            root = work.tile([P, slots, width], F32, name="root")
-            for s in range(slots):
+
+        def square_scat(u):
+            sq[u] = work.tile(shape_of(u), F32, name="sq")
+            nc.scalar.activation(out=sq[u][:], in_=scat[u][:], func=ACT.Square)
+
+        def inverse_root(u):
+            b, j0, width, t0 = units[u]
+            root[u] = work.tile(shape_of(u), F32, name="root")
+            for s in range(KP // width):
                 col = 32 * (t0 + s) + 16 * b
-                nc.scalar.activation(out=root[:, s, :], in_=sq[:, s, :], func=ACT.Abs_reciprocal_sqrt, bias=base_cols[:, col:col + 1])
-            recip = work.tile([P, slots, width], F32, name="recip")
-            nc.scalar.activation(out=recip[:], in_=root[:], func=ACT.Square)
-            signed = work.tile([P, slots, width], F32, name="signed")
-            nc.vector.tensor_tensor(out=signed[:], in0=absorb[:], in1=recip[:], op=ALU.mult)
-            quot = work.tile([P, slots, width], F32, name="quot")
-            nc.scalar.activation(out=quot[:], in_=signed[:], func=ACT.Abs)
+                nc.scalar.activation(
+                    out=root[u][:, s, :], in_=sq[u][:, s, :], func=ACT.Abs_reciprocal_sqrt, bias=base_cols[:, col:col + 1]
+                )
+
+        def square_root(u):
+            recip[u] = work.tile(shape_of(u), F32, name="recip")
+            nc.scalar.activation(out=recip[u][:], in_=root[u][:], func=ACT.Square)
+
+        def divide(u):
+            signed[u] = work.tile(shape_of(u), F32, name="signed")
+            nc.vector.tensor_tensor(out=signed[u][:], in0=absorb[u][:], in1=recip[u][:], op=ALU.mult)
+
+        def drop_sign(u):
+            quot[u] = work.tile(shape_of(u), F32, name="quot", bufs=4)
+            nc.scalar.activation(out=quot[u][:], in_=signed[u][:], func=ACT.Abs)
+
+        finished = []
+
+        def subtract(u):
+            b, j0, width, t0 = units[u]
+            slots = KP // width
             if t0 == 0:
                 diffs[b, j0] = work.tile([P, PACK, width], F32, name="diff")
-            nc.vector.tensor_tensor(out=diffs[b, j0][:, t0:t0 + slots, :], in0=panel[:], in1=quot[:], op=ALU.subtract)
+            nc.vector.tensor_tensor(out=diffs[b, j0][:, t0:t0 + slots, :], in0=panel[u][:], in1=quot[u][:], op=ALU.subtract)
+            if t0 + slots == PACK:
+                finished.extend((b, j0, c0) for c0 in range(0, width, JQ))
 
-        def quantize_d(b, j0, width):
-            dist = work.tile([P, width * PACK], BF16, name="dist", align_bytes=64)
+        def distance(b, j0, c0):
+            dist[b, j0 + c0] = work.tile([P, JQ * PACK], BF16, name="dist", align_bytes=64)
             nc.scalar.activation(
-                out=dist[:].rearrange("p (c i t) -> p c t i", i=4, t=PACK),
-                in_=diffs[b, j0][:].rearrange("p t (c i) -> p c t i", i=4),
+                out=dist[b, j0 + c0][:].rearrange("p (c i t) -> p c t i", i=4, t=PACK),
+                in_=diffs[b, j0][:, :, c0:c0 + JQ].rearrange("p t (c i) -> p c t i", i=4),
                 func=ACT.Abs,
             )
-            codes, plane = quantize(dist[:], width, f"d{b}{j0}")
-            for c0 in range(0, width, JQ):
-                d_codes[b, j0 + c0], d_plane[b, j0 + c0] = codes[:, c0:c0 + JQ], plane[:, c0:c0 + JQ]
 
-        def second_stage(j0):
-            acc = psum.tile([P, PACK, JQ], F32, name="acc")
+        def quantize_d(b, j0, c0):
+            d_codes[b, j0 + c0], d_plane[b, j0 + c0] = quantize(dist[b, j0 + c0][:], JQ, f"d{b}{j0 + c0}")
+
+        def second_stage(j0, n0, count, bank, copy):
+            acc = psum.tile([P, count, JQ], F32, name="acc", tag=bank)
             for b in range(2):
-                for n in range(PACK):
+                for n in range(n0, n0 + count):
                     nc.tensor.matmul_mx(
-                        out=acc[:, n, :],
+                        out=acc[:, n - n0, :],
                         lhsT=wc_codes[b][:, n * P:(n + 1) * P].bitcast(E4M3),
                         lhsT_scale=wc_plane[b][:, n * P:(n + 1) * P],
-                        rhs=d_codes[b, j0].bitcast(E4M3), rhs_scale=d_plane[b, j0],
-                        start=(b == 0 and n == 0), stop=(b == 1 and n == PACK - 1),
+                        rhs=d_codes[b, j0][:].bitcast(E4M3), rhs_scale=d_plane[b, j0][:],
+                        start=(b == 0 and n == n0), stop=(b == 1 and n == n0 + count - 1),
                     )
-            result = work.tile([P, PACK, JQ], F32, name="result")
-            nc.vector.tensor_copy(out=result[:], in_=acc[:])
+            result = work.tile([P, count, JQ], F32, name="result")
+            copy(out=result[:], in_=acc[:])
             nc.sync.dma_start(
-                out=out[:, j0:j0 + JQ].rearrange("(n p) j -> p n j", p=P),
+                out=out[n0 * P:(n0 + count) * P, j0:j0 + JQ].rearrange("(n p) j -> p n j", p=P),
                 in_=result[:],
             )
 
-        def columns(b, j0, width):
-            for t0 in range(0, PACK, KP // width):
-                first_stage(b, j0, width, t0)
-            quantize_d(b, j0, width)
+        def run(stage, u):
+            if 0 <= u < len(units):
+                stage(u)
 
-        half = S // 2
-        columns(0, 0, half)
-        for step in prepare_ws(1, 0, nc.vector.tensor_copy):
-            step()
-        columns(0, half, half)
-        for step in prepare_ws(1, 1, nc.vector.tensor_copy):
-            step()
-        sort_wa(1)
-        sort_wp(1)
-        columns(1, 0, half)
-        for step in prepare_wc(0) + prepare_wc(1):
-            step()
-        columns(1, half, JQ)
-        second_stage(0)
-        second_stage(JQ)
-        columns(1, half + JQ, JQ)
-        second_stage(half)
-        second_stage(half + JQ)
+        taken = 0
+        second = []
+        scat_products(0)
+        for k in range(len(units) + 2):
+            run(square_scat, k)
+            run(subtract, k - 2)
+            if k == 4:
+                sort_wa(1)
+            if k == 5:
+                sort_wp(1)
+            if k != 3:
+                run(scat_products, k + 1)
+            run(absorb_products, k)
+            run(panel_products, k - 1)
+            run(square_root, k - 1)
+            run(divide, k - 1)
+            run(inverse_root, k)
+            ready = finished[taken:taken + (1 if k < 8 else 2)]
+            taken = taken + len(ready)
+            for piece in ready:
+                distance(*piece)
+            run(drop_sign, k - 1)
+            for piece in ready:
+                quantize_d(*piece)
+                if piece[0] == 1:
+                    second.append(piece[1] + piece[2])
+            if k == 3:
+                for step in prepare_ws(1, 0, [on_vector] * 2) + prepare_ws(1, 1, [on_vector] * 2):
+                    step()
+                scat_products(4)
+            if k == 7:
+                for step in prepare_wc(0) + prepare_wc(1):
+                    step()
+            if k >= 7:
+                for j0 in second:
+                    if j0 + JQ < S:
+                        second_stage(j0, 0, PACK, "acc", on_vector)
+                    else:
+                        second_stage(j0, 0, 2, "scat", on_vector)
+                        second_stage(j0, 2, 2, "absorb", on_scalar)
+                second = []

@@ -20,7 +20,13 @@ P = 128
 PACK = 4
 KP = P * PACK
 JQ = 128
-NQ = S // JQ
+QB = 5
+LINE = "tpmAPcC"
+NS = 2
+RECIP_V = ()
+ON_VECTOR = ()
+COPY_V = (0, 128, 256)
+WCK = 6
 
 
 def tile_list_tint_adjustment_kernel(
@@ -40,27 +46,30 @@ def tile_list_tint_adjustment_kernel(
         lists2 = keep.tile([P, S // 16], U16, name="lists2")
 
         tab_rows = [held([P, T], U8, f"tab_rows{x}") for x in range(3)]
-        w_rows = held([P, 3 * H], U8, "w_rows")
+        wa_rows = held([P, 2 * H], U8, "wa_rows")
+        wp_rows = held([P, H], U8, "wp_rows")
         base_rows = held([P, P], F32, "base_rows")
-        planes = held([P, S + 3 * H], U8, "planes")
+        late_planes = held([P, S + 2 * H], U8, "late_planes")
+        early_planes = held([P, 2 * S + H], U8, "early_planes")
         warm = held([P, 8], F32, "warm")
         warm_out = held([P, 8], F32, "warm_out")
         nc.gpsimd.memset(tab_rows[0][:].bitcast(I32), 0)
         nc.vector.memset(tab_rows[1][:].bitcast(I32), 0)
+        nc.gpsimd.memset(wa_rows[:].bitcast(I32), 0)
         nc.vector.memset(warm[:], 1.0)
-        nc.gpsimd.memset(tab_rows[2][:].bitcast(I32), 0)
-        nc.vector.memset(w_rows[:].bitcast(I32), 0)
+        nc.vector.memset(tab_rows[2][:].bitcast(I32), 0)
+        nc.vector.memset(wp_rows[:].bitcast(I32), 0)
         nc.vector.memset(base_rows[:], 0.0)
-        nc.gpsimd.memset(planes[:].bitcast(I32), 0)
+        nc.gpsimd.memset(early_planes[:].bitcast(I32), 0)
+        nc.gpsimd.memset(late_planes[:].bitcast(I32), 0)
 
         ws_raw = {}
 
-        def load_ws(b, a):
-            ws_raw[b, a] = held([P, PACK, KP], F32, f"ws_raw{b}{a}")
-            nc.sync.dma_start(
-                out=ws_raw[b, a][:],
-                in_=ws[a * KP:(a + 1) * KP, b * KP:(b + 1) * KP].rearrange("(p j) c -> p j c", j=PACK),
-            )
+        def load_ws(b, a, j0=0, count=PACK):
+            if j0 == 0:
+                ws_raw[b, a] = held([P, PACK, KP], F32, f"ws_raw{b}{a}")
+            rows = ws[a * KP:(a + 1) * KP, b * KP:(b + 1) * KP].rearrange("(p j) c -> p j c", j=PACK)
+            nc.sync.dma_start(out=ws_raw[b, a][:, j0:j0 + count, :], in_=rows[:, j0:j0 + count, :])
 
         windows = {}
         table_words = [tab_words[0], tab_words[1], tab2_words[0]]
@@ -71,8 +80,8 @@ def tile_list_tint_adjustment_kernel(
             windows[x] = held([P, T], I32, f"window{x}")
             nc.sync.dma_start(out=windows[x][:], in_=table_words[x].rearrange("p t i -> p (t i)").bitcast(I32))
 
-        def load_rows(x):
-            nc.scalar.dma_start(out=tab_rows[x][0:P:8, :].bitcast(I32), in_=table_scales[x].bitcast(I32))
+        def load_rows(x, queue):
+            queue.dma_start(out=tab_rows[x][0:P:8, :].bitcast(I32), in_=table_scales[x].bitcast(I32))
 
         wa_raw, wp_raw, wc_raw = {}, {}, {}
 
@@ -96,50 +105,79 @@ def tile_list_tint_adjustment_kernel(
             for t in range(PACK):
                 nc.sync.dma_start(out=wc_raw[b][:, t, :], in_=rows[t])
 
+        def move_rows(dst, src, queue):
+            for d in range(4):
+                queue.dma_start(out=dst[32 * d:32 * d + 4, :].bitcast(I32), in_=src[32 * d:32 * d + 32:8, :].bitcast(I32))
+
         nc.sync.dma_start(lists[:], offs)
-        load_ws(0, 0)
         nc.sync.dma_start(lists2[:], offs2)
-        load_ws(0, 1)
+        load_ws(0, 0, 0, 2)
+        load_rows(0, nc.sync)
+        load_rows(1, nc.sync)
+        nc.sync.dma_start(
+            out=wa_rows[0:P:8, :].bitcast(I32).rearrange("q (a c) -> q a c", a=2),
+            in_=wa_scales.bitcast(I32).rearrange("a q c -> q a c"),
+        )
+        load_rows(2, nc.sync)
+        load_ws(0, 0, 2, 2)
         load_window(0)
+        load_ws(0, 1)
+        nc.sync.dma_start(out=wp_rows[0:P:8, :].bitcast(I32), in_=wp_scales[0].bitcast(I32))
+        nc.sync.dma_start(out=base_rows[0:P:16, :], in_=base.rearrange("(b q x) -> q b x", b=2, q=4))
+        nc.scalar.activation(out=warm_out[:], in_=warm[:], func=ACT.Abs_reciprocal_sqrt)
+
+        def sort_rows(dst, src):
+            nc.vector.tensor_copy(
+                out=dst.bitcast(I32).rearrange("p s (t g h) -> p s g t h", t=PACK, h=4),
+                in_=src.bitcast(I32).rearrange("p s (g h t) -> p s g t h", t=PACK, h=4),
+            )
+
+        wa_halves = wa_rows[:].rearrange("p (a b c) -> p b a c", a=2, b=2)
+        picked_rows = held([P, 2 * S], U8, "picked_rows")
+        picked_rows2 = held([P, S], U8, "picked_rows2")
+        early_rows = held([P, 2 * S + H], U8, "early_rows")
+        late_rows = held([P, S + 2 * H], U8, "late_rows")
+        for x in range(2):
+            nc.vector.tensor_copy(out=picked_rows[:, x * S:(x + 1) * S], in_=tab_rows[x][:].indirect(lists[:]))
+        sort_rows(early_rows[:, 2 * S:].rearrange("p (s c) -> p s c", s=2), wa_halves[:, 0])
+        nc.vector.tensor_copy(out=early_rows[:, 0:2 * S].bitcast(I32), in_=picked_rows[:].bitcast(I32))
+        move_rows(early_planes, early_rows, nc.sync)
         load_window(1)
         load_wa(0)
         load_ws(1, 0)
-        load_window(2)
-        load_wp(0)
         load_ws(1, 1)
-        load_wa(1)
-        load_wp(1)
-        load_wc(0)
-        load_wc(1)
-        load_rows(0)
-        load_rows(1)
-        nc.scalar.activation(out=warm_out[:], in_=warm[:], func=ACT.Abs_reciprocal_sqrt)
-        load_rows(2)
-        nc.scalar.dma_start(
-            out=w_rows[0:P:8, 0:2 * H].bitcast(I32).rearrange("q (a c) -> q a c", a=2),
-            in_=wa_scales.bitcast(I32).rearrange("a q c -> q a c"),
-        )
-        nc.scalar.dma_start(out=w_rows[0:P:8, 2 * H:3 * H].bitcast(I32), in_=wp_scales[0].bitcast(I32))
-        nc.scalar.dma_start(out=base_rows[0:P:16, :], in_=base.rearrange("(b q x) -> q b x", b=2, q=4))
-
-        picked_rows = held([P, 2 * S], U8, "picked_rows")
-        picked_rows2 = held([P, S], U8, "picked_rows2")
-        for x in range(2):
-            nc.vector.tensor_copy(out=picked_rows[:, x * S:(x + 1) * S], in_=tab_rows[x][:].indirect(lists[:]))
         nc.vector.tensor_copy(out=picked_rows2[:], in_=tab_rows[2][:].indirect(lists2[:]))
-        staged = held([P, S + 3 * H], U8, "staged")
-        nc.vector.tensor_copy(out=staged[:, 0:S].bitcast(I32), in_=picked_rows2[:].bitcast(I32))
-        nc.vector.tensor_copy(
-            out=staged[:, S:].bitcast(I32).rearrange("p (s t g h) -> p s g t h", t=PACK, g=8, h=4),
-            in_=w_rows[:].bitcast(I32).rearrange("p (s g h t) -> p s g t h", t=PACK, g=8, h=4),
-        )
+        sort_rows(late_rows[:, S:S + H].rearrange("p (s c) -> p s c", s=2), wa_halves[:, 1])
+        sort_rows(late_rows[:, S + H:].rearrange("p (s c) -> p s c", s=2), wp_rows[:].rearrange("p (s c) -> p s c", s=2))
+        nc.vector.tensor_copy(out=late_rows[:, 0:S].bitcast(I32), in_=picked_rows2[:].bitcast(I32))
+        for what in LINE:
+            if what == "m":
+                move_rows(late_planes, late_rows, nc.sync)
+            elif what == "M":
+                move_rows(late_planes, late_rows, nc.scalar)
+            elif what == "t":
+                load_window(2)
+            elif what == "p":
+                load_wp(0)
+            elif what == "P":
+                load_wp(1)
+            elif what == "A":
+                load_wa(1)
+            elif what == "c":
+                load_wc(0)
+            elif what == "C":
+                load_wc(1)
 
         def picked_plane(x, cols):
-            return tab_planes[:, x * S + cols.start:x * S + cols.stop] if x < 2 else planes[:, cols]
+            return early_planes[:, x * S + cols.start:x * S + cols.stop] if x < 2 else late_planes[:, cols]
 
-        def weight_plane(s, b, t):
-            c0 = S + s * H + b * KP + t * P
-            return planes[:, c0:c0 + P]
+        def wa_plane(b, a, t):
+            c0 = a * KP + t * P
+            return early_planes[:, 2 * S + c0:2 * S + c0 + P] if b == 0 else late_planes[:, S + c0:S + c0 + P]
+
+        def wp_plane(b, t):
+            c0 = S + H + b * KP + t * P
+            return late_planes[:, c0:c0 + P]
 
         base_sorted = held([P, P], F32, "base_sorted")
         nc.vector.tensor_copy(
@@ -152,10 +190,10 @@ def tile_list_tint_adjustment_kernel(
         ws_codes, ws_plane = {}, {}
         on_scalar, on_vector = nc.scalar.copy, nc.vector.tensor_copy
 
-        def round_ws(b, a, t0, engine_copy, grouped):
+        def round_ws(b, a, t, engine_copy, grouped):
             engine_copy(
-                out=grouped[:, t0 * KP:(t0 + 2) * KP].rearrange("p (t h i j) -> p t h j i", t=2, i=4, j=PACK),
-                in_=ws_raw[b, a][:].rearrange("p j (h t i) -> p t h j i", t=PACK, i=4)[:, t0:t0 + 2],
+                out=grouped[:, t * KP:(t + 1) * KP].rearrange("p (h e i j) -> p h e j i", e=2, i=2, j=PACK),
+                in_=ws_raw[b, a][:].rearrange("p j (h t e i) -> p t h e j i", t=PACK, e=2, i=2)[:, t],
             )
 
         def quantize(grouped, width, name):
@@ -190,7 +228,7 @@ def tile_list_tint_adjustment_kernel(
 
         def prepare_ws(b, a, copies, tag=None):
             grouped = held([P, PACK * KP], BF16, f"ws_grouped{b}{a}", tag)
-            steps = [lambda x=x: round_ws(b, a, 2 * x, copies[x], grouped) for x in range(2)]
+            steps = [lambda t=t: round_ws(b, a, t, copies[t], grouped) for t in range(PACK)]
 
             def finish():
                 ws_codes[b, a], ws_plane[b, a] = quantize(grouped[:], KP, f"ws{b}{a}")
@@ -204,8 +242,8 @@ def tile_list_tint_adjustment_kernel(
 
             def round_wc(n):
                 nc.vector.tensor_copy(
-                    out=grouped[:, n * KP:(n + 2) * KP].rearrange("p (c i t) -> p c t i", i=4, t=PACK),
-                    in_=wc_raw[b][:, :, n * P:(n + 2) * P].rearrange("p t (c i) -> p c t i", i=4),
+                    out=grouped[:, n * KP:(n + 2) * KP].rearrange("p (c i t) -> p c t i", i=2, t=PACK),
+                    in_=wc_raw[b][:, :, n * P:(n + 2) * P].rearrange("p t (c i) -> p c t i", i=2),
                 )
 
             def finish():
@@ -213,20 +251,12 @@ def tile_list_tint_adjustment_kernel(
 
             return [lambda n=n: round_wc(n) for n in (0, 2)] + [finish]
 
-        def move_rows(dst, src):
-            for d in range(4):
-                nc.scalar.dma_start(out=dst[32 * d:32 * d + 4, :].bitcast(I32), in_=src[32 * d:32 * d + 32:8, :].bitcast(I32))
-
-        for step in prepare_ws(0, 0, [on_scalar] * 2):
+        for step in prepare_ws(0, 0, [on_scalar] * 4):
             step()
-        tab_planes = held([P, 2 * S], U8, "tab_planes", "ws_raw00")
-        nc.vector.memset(tab_planes[:].bitcast(I32), 0)
-        move_rows(tab_planes, picked_rows)
         gather(0, 0)
         gather(0, 1)
-        for step in prepare_ws(0, 1, [on_scalar] * 2):
+        for step in prepare_ws(0, 1, [on_scalar] * NS + [on_vector] * (4 - NS)):
             step()
-        move_rows(planes, staged)
         gather(1, 0)
         sort_wa(0)
         gather(1, 1)
@@ -271,7 +301,7 @@ def tile_list_tint_adjustment_kernel(
                         nc.tensor.matmul_mx(
                             out=absorb[u][:, s, c0:c0 + JQ],
                             lhsT=wa_codes[b][:, a, t * 64:(t + 1) * 64].bitcast(U8).bitcast(E2M1),
-                            lhsT_scale=weight_plane(a, b, t),
+                            lhsT_scale=wa_plane(b, a, t),
                             rhs=picked[a][:, part].bitcast(E4M3), rhs_scale=picked_plane(a, part),
                             start=(a == 0 and s == 0 and c0 == 0),
                             stop=(a == 1 and s == slots - 1 and c0 + JQ == width),
@@ -286,7 +316,7 @@ def tile_list_tint_adjustment_kernel(
                 nc.tensor.matmul_mx(
                     out=panel[u][:, s, :],
                     lhsT=wp_codes[b][:, t * P:(t + 1) * P].bitcast(E4M3),
-                    lhsT_scale=weight_plane(2, b, t),
+                    lhsT_scale=wp_plane(b, t),
                     rhs=picked[2][:, cols].bitcast(E4M3), rhs_scale=picked_plane(2, cols),
                     start=True, stop=True,
                 )
@@ -305,15 +335,24 @@ def tile_list_tint_adjustment_kernel(
                 )
 
         def square_root(u):
+            if u in RECIP_V:
+                return
             recip[u] = work.tile(shape_of(u), F32, name="recip")
             nc.scalar.activation(out=recip[u][:], in_=root[u][:], func=ACT.Square)
 
         def divide(u):
-            signed[u] = work.tile(shape_of(u), F32, name="signed")
+            signed[u] = work.tile(shape_of(u), F32, name="signed", bufs=QB)
+            if u in RECIP_V:
+                once = work.tile(shape_of(u), F32, name="recip")
+                nc.vector.tensor_tensor(out=once[:], in0=absorb[u][:], in1=root[u][:], op=ALU.mult)
+                nc.vector.tensor_tensor(out=signed[u][:], in0=once[:], in1=root[u][:], op=ALU.mult)
+                return
             nc.vector.tensor_tensor(out=signed[u][:], in0=absorb[u][:], in1=recip[u][:], op=ALU.mult)
 
         def drop_sign(u):
-            quot[u] = work.tile(shape_of(u), F32, name="quot", bufs=4)
+            if u in ON_VECTOR:
+                return
+            quot[u] = work.tile(shape_of(u), F32, name="quot", bufs=QB)
             nc.scalar.activation(out=quot[u][:], in_=signed[u][:], func=ACT.Abs)
 
         finished = []
@@ -323,15 +362,20 @@ def tile_list_tint_adjustment_kernel(
             slots = KP // width
             if t0 == 0:
                 diffs[b, j0] = work.tile([P, PACK, width], F32, name="diff")
-            nc.vector.tensor_tensor(out=diffs[b, j0][:, t0:t0 + slots, :], in0=panel[u][:], in1=quot[u][:], op=ALU.subtract)
+            if u in ON_VECTOR:
+                low = work.tile(shape_of(u), F32, name="low")
+                nc.vector.scalar_tensor_tensor(out=low[:], in0=signed[u][:], scalar=0.0, in1=panel[u][:], op0=ALU.min, op1=ALU.add)
+                nc.vector.scalar_tensor_tensor(out=diffs[b, j0][:, t0:t0 + slots, :], in0=signed[u][:], scalar=0.0, in1=low[:], op0=ALU.max, op1=ALU.subtract)
+            else:
+                nc.vector.tensor_tensor(out=diffs[b, j0][:, t0:t0 + slots, :], in0=panel[u][:], in1=quot[u][:], op=ALU.subtract)
             if t0 + slots == PACK:
                 finished.extend((b, j0, c0) for c0 in range(0, width, JQ))
 
         def distance(b, j0, c0):
             dist[b, j0 + c0] = work.tile([P, JQ * PACK], BF16, name="dist", align_bytes=64)
             nc.scalar.activation(
-                out=dist[b, j0 + c0][:].rearrange("p (c i t) -> p c t i", i=4, t=PACK),
-                in_=diffs[b, j0][:, :, c0:c0 + JQ].rearrange("p t (c i) -> p c t i", i=4),
+                out=dist[b, j0 + c0][:].rearrange("p (c i t) -> p c t i", i=2, t=PACK),
+                in_=diffs[b, j0][:, :, c0:c0 + JQ].rearrange("p t (c i) -> p c t i", i=2),
                 func=ACT.Abs,
             )
 
@@ -387,16 +431,16 @@ def tile_list_tint_adjustment_kernel(
                 if piece[0] == 1:
                     second.append(piece[1] + piece[2])
             if k == 3:
-                for step in prepare_ws(1, 0, [on_vector] * 2) + prepare_ws(1, 1, [on_vector] * 2):
+                for step in prepare_ws(1, 0, [on_vector] * 4) + prepare_ws(1, 1, [on_vector] * 4):
                     step()
                 scat_products(4)
-            if k == 7:
+            if k == WCK:
                 for step in prepare_wc(0) + prepare_wc(1):
                     step()
             if k >= 7:
                 for j0 in second:
                     if j0 + JQ < S:
-                        second_stage(j0, 0, PACK, "acc", on_vector)
+                        second_stage(j0, 0, PACK, "acc" if j0 < half else "panel", on_vector if j0 in COPY_V else on_scalar)
                     else:
                         second_stage(j0, 0, 2, "scat", on_vector)
                         second_stage(j0, 2, 2, "absorb", on_scalar)

@@ -19,14 +19,18 @@ ALU = mybir.AluOpType
 P = 128
 PACK = 4
 KP = P * PACK
-JQ = 128
-QB = 5
-LINE = "tpmAPcC"
-NS = 2
-RECIP_V = ()
-ON_VECTOR = ()
-COPY_V = (0, 128, 256)
-WCK = 6
+BANK = 512
+HALF = S // 2
+QUARTER = S // 4
+
+UNITS = (
+    [(0, 0, S, t) for t in range(PACK)]
+    + [(1, 0, HALF, 0), (1, 0, HALF, 2)]
+    + [(1, HALF, QUARTER, 0), (1, HALF + QUARTER, QUARTER, 0)]
+)
+QUOT_BUFS = 6
+WC_STEP = 5
+DRAIN_STEP = 7
 
 
 def tile_list_tint_adjustment_kernel(
@@ -45,138 +49,94 @@ def tile_list_tint_adjustment_kernel(
         lists = keep.tile([P, S // 16], U16, name="lists")
         lists2 = keep.tile([P, S // 16], U16, name="lists2")
 
+        table_words = [tab_words[0], tab_words[1], tab2_words[0]]
+        table_scales = [tab_scales[0], tab_scales[1], tab2_scales[0]]
+        table_lists = [lists, lists, lists2]
+
         tab_rows = [held([P, T], U8, f"tab_rows{x}") for x in range(3)]
         wa_rows = held([P, 2 * H], U8, "wa_rows")
         wp_rows = held([P, H], U8, "wp_rows")
         base_rows = held([P, P], F32, "base_rows")
-        late_planes = held([P, S + 2 * H], U8, "late_planes")
-        early_planes = held([P, 2 * S + H], U8, "early_planes")
-        warm = held([P, 8], F32, "warm")
-        warm_out = held([P, 8], F32, "warm_out")
+        late_planes = held([P, S + H], U8, "late_planes")
+        early_planes = held([P, 2 * S + 2 * H], U8, "early_planes")
         nc.gpsimd.memset(tab_rows[0][:].bitcast(I32), 0)
         nc.vector.memset(tab_rows[1][:].bitcast(I32), 0)
         nc.gpsimd.memset(wa_rows[:].bitcast(I32), 0)
-        nc.vector.memset(warm[:], 1.0)
         nc.vector.memset(tab_rows[2][:].bitcast(I32), 0)
         nc.vector.memset(wp_rows[:].bitcast(I32), 0)
         nc.vector.memset(base_rows[:], 0.0)
         nc.gpsimd.memset(early_planes[:].bitcast(I32), 0)
         nc.gpsimd.memset(late_planes[:].bitcast(I32), 0)
 
-        ws_raw = {}
+        windows = [held([P, T], I32, f"window{x}") for x in range(3)]
+        wa_raw = held([P, 2, H // 2], I32, "wa_raw")
+        wp_raw = held([P, H], I32, "wp_raw")
+        ws_raw = {(b, a): held([P, PACK, KP], F32, f"ws_raw{b}{a}") for b in range(2) for a in range(2)}
+        wc_raw = {}
 
-        def load_ws(b, a, j0=0, count=PACK):
-            if j0 == 0:
-                ws_raw[b, a] = held([P, PACK, KP], F32, f"ws_raw{b}{a}")
-            rows = ws[a * KP:(a + 1) * KP, b * KP:(b + 1) * KP].rearrange("(p j) c -> p j c", j=PACK)
-            nc.sync.dma_start(out=ws_raw[b, a][:, j0:j0 + count, :], in_=rows[:, j0:j0 + count, :])
+        def load_window(x, c0, count):
+            words = table_words[x].rearrange("p t i -> p (t i)").bitcast(I32)
+            nc.sync.dma_start(out=windows[x][:, c0:c0 + count], in_=words[:, c0:c0 + count])
 
-        windows = {}
-        table_words = [tab_words[0], tab_words[1], tab2_words[0]]
-        table_scales = [tab_scales[0], tab_scales[1], tab2_scales[0]]
-        table_lists = [lists, lists, lists2]
+        def load_rows(x):
+            nc.sync.dma_start(out=tab_rows[x][0:P:8, :].bitcast(I32), in_=table_scales[x].bitcast(I32))
 
-        def load_window(x):
-            windows[x] = held([P, T], I32, f"window{x}")
-            nc.sync.dma_start(out=windows[x][:], in_=table_words[x].rearrange("p t i -> p (t i)").bitcast(I32))
+        def move_rows(planes, rows):
+            for r in range(4):
+                nc.sync.dma_start(out=planes[r:P:32, :].bitcast(I32), in_=rows[8 * r:P:32, :].bitcast(I32))
 
-        def load_rows(x, queue):
-            queue.dma_start(out=tab_rows[x][0:P:8, :].bitcast(I32), in_=table_scales[x].bitcast(I32))
-
-        wa_raw, wp_raw, wc_raw = {}, {}, {}
-
-        def load_wa(b):
-            wa_raw[b] = held([P, 2, KP // 2], I32, f"wa_raw{b}")
-            nc.sync.dma_start(
-                out=wa_raw[b][:],
-                in_=wa_words.bitcast(I32)[:, :, b * (KP // 2):(b + 1) * (KP // 2)].rearrange("a p c -> p a c"),
+        def sort_rows(sorted_rows, rows):
+            nc.vector.tensor_copy(
+                out=sorted_rows.bitcast(I32).rearrange("p (s t g e) -> p s g t e", t=PACK, g=8, e=4),
+                in_=rows.bitcast(I32).rearrange("p (s g e t) -> p s g t e", t=PACK, g=8, e=4),
             )
-
-        def load_wp(b):
-            wp_raw[b] = held([P, KP], I32, f"wp_raw{b}")
-            nc.sync.dma_start(
-                out=wp_raw[b][:],
-                in_=wp_words[0].rearrange("p c i -> p (c i)").bitcast(I32)[:, b * KP:(b + 1) * KP],
-            )
-
-        def load_wc(b):
-            wc_raw[b] = held([P, PACK, N], F32, f"wc_raw{b}")
-            rows = wc[b * KP:(b + 1) * KP, :].rearrange("(h t i) n -> t h i n", t=PACK, i=4)
-            for t in range(PACK):
-                nc.sync.dma_start(out=wc_raw[b][:, t, :], in_=rows[t])
-
-        def move_rows(dst, src, queue):
-            for d in range(4):
-                queue.dma_start(out=dst[32 * d:32 * d + 4, :].bitcast(I32), in_=src[32 * d:32 * d + 32:8, :].bitcast(I32))
 
         nc.sync.dma_start(lists[:], offs)
         nc.sync.dma_start(lists2[:], offs2)
-        load_ws(0, 0, 0, 2)
-        load_rows(0, nc.sync)
-        load_rows(1, nc.sync)
+        load_window(0, 0, T // 2)
+        load_rows(0)
+        load_rows(1)
         nc.sync.dma_start(
             out=wa_rows[0:P:8, :].bitcast(I32).rearrange("q (a c) -> q a c", a=2),
             in_=wa_scales.bitcast(I32).rearrange("a q c -> q a c"),
         )
-        load_rows(2, nc.sync)
-        load_ws(0, 0, 2, 2)
-        load_window(0)
-        load_ws(0, 1)
-        nc.sync.dma_start(out=wp_rows[0:P:8, :].bitcast(I32), in_=wp_scales[0].bitcast(I32))
-        nc.sync.dma_start(out=base_rows[0:P:16, :], in_=base.rearrange("(b q x) -> q b x", b=2, q=4))
-        nc.scalar.activation(out=warm_out[:], in_=warm[:], func=ACT.Abs_reciprocal_sqrt)
+        nc.sync.dma_start(out=base_rows[0:P:16, :], in_=base.rearrange("(b d x) -> d b x", b=2, d=4))
+        load_window(0, T // 2, T // 2)
+        load_window(1, 0, T)
+        nc.sync.dma_start(out=wa_raw[:], in_=wa_words.bitcast(I32).rearrange("a p c -> p a c"))
 
-        def sort_rows(dst, src):
-            nc.vector.tensor_copy(
-                out=dst.bitcast(I32).rearrange("p s (t g h) -> p s g t h", t=PACK, h=4),
-                in_=src.bitcast(I32).rearrange("p s (g h t) -> p s g t h", t=PACK, h=4),
-            )
-
-        wa_halves = wa_rows[:].rearrange("p (a b c) -> p b a c", a=2, b=2)
         picked_rows = held([P, 2 * S], U8, "picked_rows")
         picked_rows2 = held([P, S], U8, "picked_rows2")
-        early_rows = held([P, 2 * S + H], U8, "early_rows")
-        late_rows = held([P, S + 2 * H], U8, "late_rows")
+        early_rows = held([P, 2 * S + 2 * H], U8, "early_rows")
+        late_rows = held([P, S + H], U8, "late_rows")
         for x in range(2):
             nc.vector.tensor_copy(out=picked_rows[:, x * S:(x + 1) * S], in_=tab_rows[x][:].indirect(lists[:]))
-        sort_rows(early_rows[:, 2 * S:].rearrange("p (s c) -> p s c", s=2), wa_halves[:, 0])
+        sort_rows(early_rows[:, 2 * S:], wa_rows[:])
         nc.vector.tensor_copy(out=early_rows[:, 0:2 * S].bitcast(I32), in_=picked_rows[:].bitcast(I32))
-        move_rows(early_planes, early_rows, nc.sync)
-        load_window(1)
-        load_wa(0)
-        load_ws(1, 0)
-        load_ws(1, 1)
+        move_rows(early_planes, early_rows)
+
+        load_rows(2)
+        nc.sync.dma_start(out=wp_rows[0:P:8, :].bitcast(I32), in_=wp_scales[0].bitcast(I32))
+        for b in range(2):
+            for a in range(2):
+                rows = ws[a * KP:(a + 1) * KP, b * KP:(b + 1) * KP]
+                nc.sync.dma_start(out=ws_raw[b, a][:], in_=rows.rearrange("(p j) c -> p j c", j=PACK))
+        load_window(2, 0, T)
+        nc.sync.dma_start(out=wp_raw[:], in_=wp_words[0].rearrange("p c i -> p (c i)").bitcast(I32))
         nc.vector.tensor_copy(out=picked_rows2[:], in_=tab_rows[2][:].indirect(lists2[:]))
-        sort_rows(late_rows[:, S:S + H].rearrange("p (s c) -> p s c", s=2), wa_halves[:, 1])
-        sort_rows(late_rows[:, S + H:].rearrange("p (s c) -> p s c", s=2), wp_rows[:].rearrange("p (s c) -> p s c", s=2))
+        sort_rows(late_rows[:, S:], wp_rows[:])
         nc.vector.tensor_copy(out=late_rows[:, 0:S].bitcast(I32), in_=picked_rows2[:].bitcast(I32))
-        for what in LINE:
-            if what == "m":
-                move_rows(late_planes, late_rows, nc.sync)
-            elif what == "M":
-                move_rows(late_planes, late_rows, nc.scalar)
-            elif what == "t":
-                load_window(2)
-            elif what == "p":
-                load_wp(0)
-            elif what == "P":
-                load_wp(1)
-            elif what == "A":
-                load_wa(1)
-            elif what == "c":
-                load_wc(0)
-            elif what == "C":
-                load_wc(1)
+        move_rows(late_planes, late_rows)
 
         def picked_plane(x, cols):
             return early_planes[:, x * S + cols.start:x * S + cols.stop] if x < 2 else late_planes[:, cols]
 
         def wa_plane(b, a, t):
-            c0 = a * KP + t * P
-            return early_planes[:, 2 * S + c0:2 * S + c0 + P] if b == 0 else late_planes[:, S + c0:S + c0 + P]
+            c0 = 2 * S + a * H + b * KP + t * P
+            return early_planes[:, c0:c0 + P]
 
         def wp_plane(b, t):
-            c0 = S + H + b * KP + t * P
+            c0 = S + b * KP + t * P
             return late_planes[:, c0:c0 + P]
 
         base_sorted = held([P, P], F32, "base_sorted")
@@ -186,96 +146,103 @@ def tile_list_tint_adjustment_kernel(
         )
         base_cols = held([P, P], F32, "base_cols")
         nc.vector.transpose(out=base_cols[:], in_=base_sorted[:])
+        inv_root = held([P, 2 * PACK], F32, "inv_root")
+        nc.scalar.activation(out=inv_root[:], in_=base_cols[:, 0:P:16], func=ACT.Abs_reciprocal_sqrt)
+        inv_base = held([P, 2 * PACK], F32, "inv_base")
+        nc.scalar.activation(out=inv_base[:], in_=inv_root[:], func=ACT.Square)
 
-        ws_codes, ws_plane = {}, {}
-        on_scalar, on_vector = nc.scalar.copy, nc.vector.tensor_copy
-
-        def round_ws(b, a, t, engine_copy, grouped):
-            engine_copy(
-                out=grouped[:, t * KP:(t + 1) * KP].rearrange("p (h e i j) -> p h e j i", e=2, i=2, j=PACK),
-                in_=ws_raw[b, a][:].rearrange("p j (h t e i) -> p t h e j i", t=PACK, e=2, i=2)[:, t],
-            )
-
-        def quantize(grouped, width, name):
+        def quantize(rounded, width, name):
             codes = held([P, width], U32, name + "_codes")
             plane = held([P, width], U8, name + "_plane")
-            nc.vector.quantize_mx(out=codes[:].bitcast(E4M3), scales=plane[:], in_=grouped)
+            nc.vector.quantize_mx(out=codes[:].bitcast(E4M3), scales=plane[:], in_=rounded)
             return codes, plane
 
         picked = [held([P, S], U32, f"picked{x}") for x in range(3)]
 
-        def gather(x, half):
+        def gather(x, c0, count):
             nc.vector.tensor_copy(
-                out=picked[x][:, half * 256:(half + 1) * 256],
-                in_=windows[x][:].bitcast(U32).indirect(table_lists[x][:, half * 16:(half + 1) * 16]),
+                out=picked[x][:, c0:c0 + count],
+                in_=windows[x][:].bitcast(U32).indirect(table_lists[x][:, c0 // 16:(c0 + count) // 16]),
             )
 
-        wa_codes, wp_codes = {}, {}
+        wa_codes, wp_codes, ws_codes, ws_plane, wc_codes, wc_plane = {}, {}, {}, {}, {}, {}
 
-        def sort_wa(b, tag=None):
-            wa_codes[b] = held([P, 2, KP // 2], I32, f"wa_codes{b}", tag)
+        def sort_wa(b):
+            wa_codes[b] = held([P, 2, KP // 2], I32, f"wa_codes{b}")
             nc.vector.tensor_copy(
                 out=wa_codes[b][:].rearrange("p a (t h w) -> p a t h w", t=PACK, w=2),
-                in_=wa_raw[b][:].rearrange("p a (h t w) -> p a t h w", t=PACK, w=2),
+                in_=wa_raw[:, :, b * (KP // 2):(b + 1) * (KP // 2)].rearrange("p a (h t w) -> p a t h w", t=PACK, w=2),
             )
 
-        def sort_wp(b, tag=None):
-            wp_codes[b] = held([P, KP], I32, f"wp_codes{b}", tag)
+        def sort_wp(b):
+            wp_codes[b] = held([P, KP], I32, f"wp_codes{b}")
             nc.vector.tensor_copy(
                 out=wp_codes[b][:].rearrange("p (t h i) -> p h t i", t=PACK, i=4),
-                in_=wp_raw[b][:].rearrange("p (h t i) -> p h t i", t=PACK, i=4),
+                in_=wp_raw[:, b * KP:(b + 1) * KP].rearrange("p (h t i) -> p h t i", t=PACK, i=4),
             )
 
-        def prepare_ws(b, a, copies, tag=None):
-            grouped = held([P, PACK * KP], BF16, f"ws_grouped{b}{a}", tag)
-            steps = [lambda t=t: round_ws(b, a, t, copies[t], grouped) for t in range(PACK)]
-
-            def finish():
-                ws_codes[b, a], ws_plane[b, a] = quantize(grouped[:], KP, f"ws{b}{a}")
-
-            return steps + [finish]
-
-        wc_codes, wc_plane = {}, {}
-
-        def prepare_wc(b):
-            grouped = held([P, PACK * N], BF16, f"wc_grouped{b}")
-
-            def round_wc(n):
+        def prepare_ws(b, a):
+            rounded = held([P, PACK * KP], BF16, f"ws_rounded{b}{a}")
+            for t in range(PACK):
                 nc.vector.tensor_copy(
-                    out=grouped[:, n * KP:(n + 2) * KP].rearrange("p (c i t) -> p c t i", i=2, t=PACK),
-                    in_=wc_raw[b][:, :, n * P:(n + 2) * P].rearrange("p t (c i) -> p c t i", i=2),
+                    out=rounded[:, t * KP:(t + 1) * KP].rearrange("p (h e f j) -> p h e j f", e=2, f=2, j=PACK),
+                    in_=ws_raw[b, a][:].rearrange("p j (h t e f) -> p t h e j f", t=PACK, e=2, f=2)[:, t],
                 )
+            ws_codes[b, a], ws_plane[b, a] = quantize(rounded[:], KP, f"ws{b}{a}")
 
-            def finish():
-                wc_codes[b], wc_plane[b] = quantize(grouped[:], N, f"wc{b}")
+        def prepare_wc(b, copies):
+            rounded = held([P, PACK * N], BF16, f"wc_rounded{b}")
+            for x, copy in enumerate(copies):
+                n0, n1 = x * (N // 2), (x + 1) * (N // 2)
+                copy(
+                    out=rounded[:, n0 * PACK:n1 * PACK].rearrange("p (c f t) -> p c t f", f=2, t=PACK),
+                    in_=wc_raw[b][:, :, n0:n1].rearrange("p t (c f) -> p c t f", f=2),
+                )
+            wc_codes[b], wc_plane[b] = quantize(rounded[:], N, f"wc{b}")
 
-            return [lambda n=n: round_wc(n) for n in (0, 2)] + [finish]
+        gather(0, 0, S)
+        gather(1, 0, S)
+        for b in range(2):
+            wc_raw[b] = held([P, PACK, N], F32, f"wc_raw{b}", f"window{b}")
+            rows = wc[b * KP:(b + 1) * KP, :].rearrange("(h t i) n -> t h i n", t=PACK, i=4)
+            for t in range(PACK):
+                nc.sync.dma_start(out=wc_raw[b][:, t, :], in_=rows[t])
+        absorbed = [held([P, PACK, S], F32, f"absorbed{b}") for b in range(2)]
 
-        for step in prepare_ws(0, 0, [on_scalar] * 4):
-            step()
-        gather(0, 0)
-        gather(0, 1)
-        for step in prepare_ws(0, 1, [on_scalar] * NS + [on_vector] * (4 - NS)):
-            step()
-        gather(1, 0)
-        sort_wa(0)
-        gather(1, 1)
-        gather(2, 0)
+        def absorption(b):
+            sort_wa(b)
+            for t in range(PACK):
+                absorb = psum.tile([P, S], F32, name="absorb", tag="absorb" if t % 2 == 0 else "acc")
+                for a in range(2):
+                    nc.tensor.matmul_mx(
+                        out=absorb[:],
+                        lhsT=wa_codes[b][:, a, t * (P // 2):(t + 1) * (P // 2)].bitcast(U8).bitcast(E2M1),
+                        lhsT_scale=wa_plane(b, a, t),
+                        rhs=picked[a][:].bitcast(E4M3), rhs_scale=picked_plane(a, slice(0, S)),
+                        start=(a == 0), stop=(a == 1),
+                    )
+                col = 2 * t + b
+                nc.scalar.activation(out=absorbed[b][:, t, :], in_=absorb[:], func=ACT.Abs, scale=inv_base[:, col:col + 1])
+
+        absorption(0)
+        prepare_ws(0, 0)
+        prepare_ws(0, 1)
+        absorption(1)
+        gather(2, 0, HALF)
         sort_wp(0)
-        gather(2, 1)
+        gather(2, HALF, HALF)
 
-        half = S // 2
-        units = [(0, j0, half, t0) for j0 in (0, half) for t0 in (0, 2)] + [(1, 0, half, 0), (1, 0, half, 2), (1, half, JQ, 0), (1, half + JQ, JQ, 0)]
-        scat, absorb, panel, sq, root, recip, signed, quot = {}, {}, {}, {}, {}, {}, {}, {}
+        scat, panel, sq, root, recip, quot = {}, {}, {}, {}, {}, {}
         diffs, dist, d_codes, d_plane = {}, {}, {}, {}
+        finished = []
 
         def shape_of(u):
-            width = units[u][2]
-            return [P, KP // width, width]
+            width = UNITS[u][2]
+            return [P, BANK // width, width]
 
         def scat_products(u):
-            b, j0, width, t0 = units[u]
-            slots = KP // width
+            b, j0, width, t0 = UNITS[u]
+            slots = BANK // width
             cols = slice(j0, j0 + width)
             scat[u] = psum.tile(shape_of(u), F32, name="scat")
             for a in range(2):
@@ -289,29 +256,11 @@ def tile_list_tint_adjustment_kernel(
                         start=(a == 0 and s == 0), stop=(a == 1 and s == slots - 1),
                     )
 
-        def absorb_products(u):
-            b, j0, width, t0 = units[u]
-            slots = KP // width
-            absorb[u] = psum.tile(shape_of(u), F32, name="absorb")
-            for a in range(2):
-                for s in range(slots):
-                    t = t0 + s
-                    for c0 in range(0, width, JQ):
-                        part = slice(j0 + c0, j0 + c0 + JQ)
-                        nc.tensor.matmul_mx(
-                            out=absorb[u][:, s, c0:c0 + JQ],
-                            lhsT=wa_codes[b][:, a, t * 64:(t + 1) * 64].bitcast(U8).bitcast(E2M1),
-                            lhsT_scale=wa_plane(b, a, t),
-                            rhs=picked[a][:, part].bitcast(E4M3), rhs_scale=picked_plane(a, part),
-                            start=(a == 0 and s == 0 and c0 == 0),
-                            stop=(a == 1 and s == slots - 1 and c0 + JQ == width),
-                        )
-
         def panel_products(u):
-            b, j0, width, t0 = units[u]
+            b, j0, width, t0 = UNITS[u]
             cols = slice(j0, j0 + width)
             panel[u] = psum.tile(shape_of(u), F32, name="panel")
-            for s in range(KP // width):
+            for s in range(BANK // width):
                 t = t0 + s
                 nc.tensor.matmul_mx(
                     out=panel[u][:, s, :],
@@ -322,68 +271,46 @@ def tile_list_tint_adjustment_kernel(
                 )
 
         def square_scat(u):
+            b, j0, width, t0 = UNITS[u]
             sq[u] = work.tile(shape_of(u), F32, name="sq")
-            nc.scalar.activation(out=sq[u][:], in_=scat[u][:], func=ACT.Square)
+            for s in range(BANK // width):
+                col = 2 * (t0 + s) + b
+                nc.scalar.activation(out=sq[u][:, s, :], in_=scat[u][:, s, :], func=ACT.Square, scale=inv_root[:, col:col + 1])
 
         def inverse_root(u):
-            b, j0, width, t0 = units[u]
             root[u] = work.tile(shape_of(u), F32, name="root")
-            for s in range(KP // width):
-                col = 32 * (t0 + s) + 16 * b
-                nc.scalar.activation(
-                    out=root[u][:, s, :], in_=sq[u][:, s, :], func=ACT.Abs_reciprocal_sqrt, bias=base_cols[:, col:col + 1]
-                )
+            nc.scalar.activation(out=root[u][:], in_=sq[u][:], func=ACT.Abs_reciprocal_sqrt, bias=1.0)
 
         def square_root(u):
-            if u in RECIP_V:
-                return
             recip[u] = work.tile(shape_of(u), F32, name="recip")
             nc.scalar.activation(out=recip[u][:], in_=root[u][:], func=ACT.Square)
 
         def divide(u):
-            signed[u] = work.tile(shape_of(u), F32, name="signed", bufs=QB)
-            if u in RECIP_V:
-                once = work.tile(shape_of(u), F32, name="recip")
-                nc.vector.tensor_tensor(out=once[:], in0=absorb[u][:], in1=root[u][:], op=ALU.mult)
-                nc.vector.tensor_tensor(out=signed[u][:], in0=once[:], in1=root[u][:], op=ALU.mult)
-                return
-            nc.vector.tensor_tensor(out=signed[u][:], in0=absorb[u][:], in1=recip[u][:], op=ALU.mult)
-
-        def drop_sign(u):
-            if u in ON_VECTOR:
-                return
-            quot[u] = work.tile(shape_of(u), F32, name="quot", bufs=QB)
-            nc.scalar.activation(out=quot[u][:], in_=signed[u][:], func=ACT.Abs)
-
-        finished = []
+            b, j0, width, t0 = UNITS[u]
+            quot[u] = work.tile(shape_of(u), F32, name="quot", bufs=QUOT_BUFS)
+            nc.vector.tensor_tensor(
+                out=quot[u][:], in0=absorbed[b][:, t0:t0 + BANK // width, j0:j0 + width], in1=recip[u][:], op=ALU.mult
+            )
 
         def subtract(u):
-            b, j0, width, t0 = units[u]
-            slots = KP // width
+            b, j0, width, t0 = UNITS[u]
+            slots = BANK // width
             if t0 == 0:
                 diffs[b, j0] = work.tile([P, PACK, width], F32, name="diff")
-            if u in ON_VECTOR:
-                low = work.tile(shape_of(u), F32, name="low")
-                nc.vector.scalar_tensor_tensor(out=low[:], in0=signed[u][:], scalar=0.0, in1=panel[u][:], op0=ALU.min, op1=ALU.add)
-                nc.vector.scalar_tensor_tensor(out=diffs[b, j0][:, t0:t0 + slots, :], in0=signed[u][:], scalar=0.0, in1=low[:], op0=ALU.max, op1=ALU.subtract)
-            else:
-                nc.vector.tensor_tensor(out=diffs[b, j0][:, t0:t0 + slots, :], in0=panel[u][:], in1=quot[u][:], op=ALU.subtract)
+            nc.vector.tensor_tensor(out=diffs[b, j0][:, t0:t0 + slots, :], in0=panel[u][:], in1=quot[u][:], op=ALU.subtract)
             if t0 + slots == PACK:
-                finished.extend((b, j0, c0) for c0 in range(0, width, JQ))
+                finished.extend((b, j0, c0) for c0 in range(0, width, QUARTER))
 
         def distance(b, j0, c0):
-            dist[b, j0 + c0] = work.tile([P, JQ * PACK], BF16, name="dist", align_bytes=64)
+            dist[b, j0 + c0] = work.tile([P, QUARTER * PACK], BF16, name="dist", align_bytes=64)
             nc.scalar.activation(
-                out=dist[b, j0 + c0][:].rearrange("p (c i t) -> p c t i", i=2, t=PACK),
-                in_=diffs[b, j0][:, :, c0:c0 + JQ].rearrange("p t (c i) -> p c t i", i=2),
+                out=dist[b, j0 + c0][:].rearrange("p (c f t) -> p c t f", f=2, t=PACK),
+                in_=diffs[b, j0][:, :, c0:c0 + QUARTER].rearrange("p t (c f) -> p c t f", f=2),
                 func=ACT.Abs,
             )
 
-        def quantize_d(b, j0, c0):
-            d_codes[b, j0 + c0], d_plane[b, j0 + c0] = quantize(dist[b, j0 + c0][:], JQ, f"d{b}{j0 + c0}")
-
         def second_stage(j0, n0, count, bank, copy):
-            acc = psum.tile([P, count, JQ], F32, name="acc", tag=bank)
+            acc = psum.tile([P, count, QUARTER], F32, name="acc", tag=bank)
             for b in range(2):
                 for n in range(n0, n0 + count):
                     nc.tensor.matmul_mx(
@@ -393,55 +320,43 @@ def tile_list_tint_adjustment_kernel(
                         rhs=d_codes[b, j0][:].bitcast(E4M3), rhs_scale=d_plane[b, j0][:],
                         start=(b == 0 and n == n0), stop=(b == 1 and n == n0 + count - 1),
                     )
-            result = work.tile([P, count, JQ], F32, name="result")
+            result = work.tile([P, count, QUARTER], F32, name="result", bufs=5)
             copy(out=result[:], in_=acc[:])
             nc.sync.dma_start(
-                out=out[n0 * P:(n0 + count) * P, j0:j0 + JQ].rearrange("(n p) j -> p n j", p=P),
+                out=out[n0 * P:(n0 + count) * P, j0:j0 + QUARTER].rearrange("(n p) j -> p n j", p=P),
                 in_=result[:],
             )
 
         def run(stage, u):
-            if 0 <= u < len(units):
+            if 0 <= u < len(UNITS):
                 stage(u)
 
         taken = 0
-        second = []
         scat_products(0)
-        for k in range(len(units) + 2):
+        for k in range(len(UNITS) + 2):
+            if k in (1, 2):
+                prepare_ws(1, k - 1)
             run(square_scat, k)
             run(subtract, k - 2)
-            if k == 4:
-                sort_wa(1)
-            if k == 5:
+            if k == PACK + 1:
                 sort_wp(1)
-            if k != 3:
-                run(scat_products, k + 1)
-            run(absorb_products, k)
+            run(scat_products, k + 1)
             run(panel_products, k - 1)
             run(square_root, k - 1)
             run(divide, k - 1)
             run(inverse_root, k)
-            ready = finished[taken:taken + (1 if k < 8 else 2)]
+            ready = finished[taken:taken + (1 if k < DRAIN_STEP else 2)]
             taken = taken + len(ready)
-            for piece in ready:
-                distance(*piece)
-            run(drop_sign, k - 1)
-            for piece in ready:
-                quantize_d(*piece)
-                if piece[0] == 1:
-                    second.append(piece[1] + piece[2])
-            if k == 3:
-                for step in prepare_ws(1, 0, [on_vector] * 4) + prepare_ws(1, 1, [on_vector] * 4):
-                    step()
-                scat_products(4)
-            if k == WCK:
-                for step in prepare_wc(0) + prepare_wc(1):
-                    step()
-            if k >= 7:
-                for j0 in second:
-                    if j0 + JQ < S:
-                        second_stage(j0, 0, PACK, "acc" if j0 < half else "panel", on_vector if j0 in COPY_V else on_scalar)
-                    else:
-                        second_stage(j0, 0, 2, "scat", on_vector)
-                        second_stage(j0, 2, 2, "absorb", on_scalar)
-                second = []
+            for b, j0, c0 in ready:
+                distance(b, j0, c0)
+            for b, j0, c0 in ready:
+                d_codes[b, j0 + c0], d_plane[b, j0 + c0] = quantize(dist[b, j0 + c0][:], QUARTER, f"d{b}{j0 + c0}")
+            if k == WC_STEP:
+                prepare_wc(0, [nc.vector.tensor_copy, nc.vector.tensor_copy])
+                prepare_wc(1, [nc.vector.tensor_copy, nc.scalar.copy])
+            for j in [j0 + c0 for b, j0, c0 in ready if b == 1]:
+                if j + QUARTER < S:
+                    second_stage(j, 0, PACK, "acc" if j < HALF else "absorb", nc.vector.tensor_copy)
+                else:
+                    second_stage(j, 0, 2, "scat", nc.vector.tensor_copy)
+                    second_stage(j, 2, 2, "scat", nc.scalar.copy)

@@ -59,14 +59,11 @@ def tile_list_tint_adjustment_kernel(
         base_rows = held([P, P], F32, "base_rows")
         late_planes = held([P, S + H], U8, "late_planes")
         early_planes = held([P, 2 * S + 2 * H], U8, "early_planes")
-        nc.gpsimd.memset(tab_rows[0][:].bitcast(I32), 0)
-        nc.vector.memset(tab_rows[1][:].bitcast(I32), 0)
-        nc.gpsimd.memset(wa_rows[:].bitcast(I32), 0)
-        nc.vector.memset(tab_rows[2][:].bitcast(I32), 0)
-        nc.vector.memset(wp_rows[:].bitcast(I32), 0)
+        for cleared in (tab_rows[0], tab_rows[1], wa_rows):
+            nc.vector.memset(cleared[:].bitcast(I32), 0)
         nc.vector.memset(base_rows[:], 0.0)
-        nc.gpsimd.memset(early_planes[:].bitcast(I32), 0)
-        nc.gpsimd.memset(late_planes[:].bitcast(I32), 0)
+        for cleared in (early_planes, tab_rows[2], wp_rows, late_planes):
+            nc.vector.memset(cleared[:].bitcast(I32), 0)
 
         windows = [held([P, T], I32, f"window{x}") for x in range(3)]
         wa_raw = held([P, 2, H // 2], I32, "wa_raw")
@@ -185,8 +182,8 @@ def tile_list_tint_adjustment_kernel(
             rounded = held([P, PACK * KP], BF16, f"ws_rounded{b}{a}")
             for t in range(PACK):
                 nc.vector.tensor_copy(
-                    out=rounded[:, t * KP:(t + 1) * KP].rearrange("p (h e f j) -> p h e j f", e=2, f=2, j=PACK),
-                    in_=ws_raw[b, a][:].rearrange("p j (h t e f) -> p t h e j f", t=PACK, e=2, f=2)[:, t],
+                    out=rounded[:, t * KP:(t + 1) * KP].rearrange("p (h i j) -> p h i j", i=4, j=PACK),
+                    in_=ws_raw[b, a][:].rearrange("p j (h t i) -> p t h i j", t=PACK, i=4)[:, t],
                 )
             ws_codes[b, a], ws_plane[b, a] = quantize(rounded[:], KP, f"ws{b}{a}")
 
@@ -195,8 +192,8 @@ def tile_list_tint_adjustment_kernel(
             for x, copy in enumerate(copies):
                 n0, n1 = x * (N // 2), (x + 1) * (N // 2)
                 copy(
-                    out=rounded[:, n0 * PACK:n1 * PACK].rearrange("p (c f t) -> p c t f", f=2, t=PACK),
-                    in_=wc_raw[b][:, :, n0:n1].rearrange("p t (c f) -> p c t f", f=2),
+                    out=rounded[:, n0 * PACK:n1 * PACK].rearrange("p (c t) -> p c t", t=PACK),
+                    in_=wc_raw[b][:, :, n0:n1].rearrange("p t c -> p c t"),
                 )
             wc_codes[b], wc_plane[b] = quantize(rounded[:], N, f"wc{b}")
 
@@ -304,8 +301,8 @@ def tile_list_tint_adjustment_kernel(
         def distance(b, j0, c0):
             dist[b, j0 + c0] = work.tile([P, QUARTER * PACK], BF16, name="dist", align_bytes=64)
             nc.scalar.activation(
-                out=dist[b, j0 + c0][:].rearrange("p (c f t) -> p c t f", f=2, t=PACK),
-                in_=diffs[b, j0][:, :, c0:c0 + QUARTER].rearrange("p t (c f) -> p c t f", f=2),
+                out=dist[b, j0 + c0][:].rearrange("p (c t) -> p c t", t=PACK),
+                in_=diffs[b, j0][:, :, c0:c0 + QUARTER].rearrange("p t c -> p c t"),
                 func=ACT.Abs,
             )
 

@@ -23,15 +23,6 @@ BANK = 512
 HALF = S // 2
 QUARTER = S // 4
 
-UNITS = (
-    [(0, 0, S, t) for t in range(PACK)]
-    + [(1, 0, HALF, 0), (1, 0, HALF, 2)]
-    + [(1, HALF, QUARTER, 0), (1, HALF + QUARTER, QUARTER, 0)]
-)
-QUOT_BUFS = 6
-WC_STEP = 5
-DRAIN_STEP = 7
-
 
 def tile_list_tint_adjustment_kernel(
     tc, tab_words, tab_scales, tab2_words, tab2_scales, offs, offs2,
@@ -40,11 +31,13 @@ def tile_list_tint_adjustment_kernel(
     nc = tc.nc
     with ExitStack() as ctx:
         keep = ctx.enter_context(tc.tile_pool(name="keep", bufs=1))
-        work = ctx.enter_context(tc.tile_pool(name="work", bufs=3))
-        psum = ctx.enter_context(tc.psum_pool(name="psum", bufs=2))
+        psum = ctx.enter_context(tc.psum_pool(name="psum", bufs=1))
 
         def held(shape, dtype, name, tag=None):
             return keep.tile(shape, dtype, name=name, tag=tag or name, align_bytes=64)
+
+        def bank(number, shape):
+            return psum.tile(shape, F32, name="bank%d" % number, tag="bank%d" % number)
 
         lists = keep.tile([P, S // 16], U16, name="lists")
         lists2 = keep.tile([P, S // 16], U16, name="lists2")
@@ -57,12 +50,13 @@ def tile_list_tint_adjustment_kernel(
         wa_rows = held([P, 2 * H], U8, "wa_rows")
         wp_rows = held([P, H], U8, "wp_rows")
         base_rows = held([P, P], F32, "base_rows")
+        early_planes = held([P, 2 * S], U8, "early_planes")
+        wa_planes = held([P, 2 * H], U8, "wa_planes")
         late_planes = held([P, S + H], U8, "late_planes")
-        early_planes = held([P, 2 * S + 2 * H], U8, "early_planes")
         for cleared in (tab_rows[0], tab_rows[1], wa_rows):
             nc.vector.memset(cleared[:].bitcast(I32), 0)
         nc.vector.memset(base_rows[:], 0.0)
-        for cleared in (early_planes, tab_rows[2], wp_rows, late_planes):
+        for cleared in (tab_rows[2], wp_rows, early_planes, late_planes):
             nc.vector.memset(cleared[:].bitcast(I32), 0)
 
         windows = [held([P, T], I32, f"window{x}") for x in range(3)]
@@ -75,12 +69,16 @@ def tile_list_tint_adjustment_kernel(
             words = table_words[x].rearrange("p t i -> p (t i)").bitcast(I32)
             nc.sync.dma_start(out=windows[x][:, c0:c0 + count], in_=words[:, c0:c0 + count])
 
-        def load_rows(x):
-            nc.sync.dma_start(out=tab_rows[x][0:P:8, :].bitcast(I32), in_=table_scales[x].bitcast(I32))
+        def load_rows(queue, x):
+            queue.dma_start(out=tab_rows[x][0:P:8, :].bitcast(I32), in_=table_scales[x].bitcast(I32))
 
-        def move_rows(planes, rows):
+        def load_ws(b, a):
+            rows = ws[a * KP:(a + 1) * KP, b * KP:(b + 1) * KP]
+            nc.sync.dma_start(out=ws_raw[b, a][:], in_=rows.rearrange("(p j) c -> p j c", j=PACK))
+
+        def move_rows(queue, planes, rows):
             for r in range(4):
-                nc.sync.dma_start(out=planes[r:P:32, :].bitcast(I32), in_=rows[8 * r:P:32, :].bitcast(I32))
+                queue.dma_start(out=planes[r:P:32, :].bitcast(I32), in_=rows[8 * r:P:32, :].bitcast(I32))
 
         def sort_rows(sorted_rows, rows):
             nc.vector.tensor_copy(
@@ -89,54 +87,50 @@ def tile_list_tint_adjustment_kernel(
             )
 
         nc.sync.dma_start(lists[:], offs)
-        nc.sync.dma_start(lists2[:], offs2)
-        load_window(0, 0, T // 2)
-        load_rows(0)
-        load_rows(1)
-        nc.sync.dma_start(
-            out=wa_rows[0:P:8, :].bitcast(I32).rearrange("q (a c) -> q a c", a=2),
-            in_=wa_scales.bitcast(I32).rearrange("a q c -> q a c"),
-        )
-        nc.sync.dma_start(out=base_rows[0:P:16, :], in_=base.rearrange("(b d x) -> d b x", b=2, d=4))
-        load_window(0, T // 2, T // 2)
-        load_window(1, 0, T)
+        load_window(0, 0, T // 4)
+        load_rows(nc.sync, 0)
+        load_rows(nc.sync, 1)
+        for d in range(4):
+            nc.scalar.dma_start(
+                out=wa_rows[32 * d:32 * d + 4, :].bitcast(I32).rearrange("q (a c) -> q a c", a=2),
+                in_=wa_scales[:, 4 * d:4 * d + 4, :].bitcast(I32).rearrange("a q c -> q a c"),
+            )
+        nc.gpsimd.dma_start(out=base_rows[0:P:16, :], in_=base.rearrange("(b d x) -> d b x", b=2, d=4))
+        load_window(0, T // 4, T - T // 4)
         nc.sync.dma_start(out=wa_raw[:], in_=wa_words.bitcast(I32).rearrange("a p c -> p a c"))
+        load_window(1, 0, T)
+        nc.sync.dma_start(lists2[:], offs2)
+        load_rows(nc.sync, 2)
 
         picked_rows = held([P, 2 * S], U8, "picked_rows")
-        picked_rows2 = held([P, S], U8, "picked_rows2")
-        early_rows = held([P, 2 * S + 2 * H], U8, "early_rows")
-        late_rows = held([P, S + H], U8, "late_rows")
         for x in range(2):
             nc.vector.tensor_copy(out=picked_rows[:, x * S:(x + 1) * S], in_=tab_rows[x][:].indirect(lists[:]))
-        sort_rows(early_rows[:, 2 * S:], wa_rows[:])
-        nc.vector.tensor_copy(out=early_rows[:, 0:2 * S].bitcast(I32), in_=picked_rows[:].bitcast(I32))
-        move_rows(early_planes, early_rows)
-
-        load_rows(2)
+        move_rows(nc.scalar, early_planes, picked_rows)
+        load_ws(0, 0)
+        load_ws(0, 1)
         nc.sync.dma_start(out=wp_rows[0:P:8, :].bitcast(I32), in_=wp_scales[0].bitcast(I32))
-        for b in range(2):
-            for a in range(2):
-                rows = ws[a * KP:(a + 1) * KP, b * KP:(b + 1) * KP]
-                nc.sync.dma_start(out=ws_raw[b, a][:], in_=rows.rearrange("(p j) c -> p j c", j=PACK))
-        load_window(2, 0, T)
-        nc.sync.dma_start(out=wp_raw[:], in_=wp_words[0].rearrange("p c i -> p (c i)").bitcast(I32))
-        nc.vector.tensor_copy(out=picked_rows2[:], in_=tab_rows[2][:].indirect(lists2[:]))
-        sort_rows(late_rows[:, S:], wp_rows[:])
-        nc.vector.tensor_copy(out=late_rows[:, 0:S].bitcast(I32), in_=picked_rows2[:].bitcast(I32))
-        move_rows(late_planes, late_rows)
+        load_ws(1, 0)
+        load_ws(1, 1)
 
         def picked_plane(x, cols):
             return early_planes[:, x * S + cols.start:x * S + cols.stop] if x < 2 else late_planes[:, cols]
 
         def wa_plane(b, a, t):
-            c0 = 2 * S + a * H + b * KP + t * P
-            return early_planes[:, c0:c0 + P]
+            c0 = a * H + b * KP + t * P
+            return wa_planes[:, c0:c0 + P]
 
         def wp_plane(b, t):
             c0 = S + b * KP + t * P
             return late_planes[:, c0:c0 + P]
 
-        base_sorted = held([P, P], F32, "base_sorted")
+        picked = [held([P, S], U32, f"picked{x}") for x in range(3)]
+
+        def gather(x):
+            nc.vector.tensor_copy(out=picked[x][:], in_=windows[x][:].bitcast(U32).indirect(table_lists[x][:]))
+
+        gather(0)
+        sort_rows(wa_planes[:], wa_rows[:])
+        base_sorted = held([P, P], F32, "base_sorted", "window0")
         nc.vector.tensor_copy(
             out=base_sorted[:].rearrange("p (t h i) -> p t h i", t=PACK, i=4),
             in_=base_rows[:].rearrange("p (h t i) -> p t h i", t=PACK, i=4),
@@ -148,24 +142,11 @@ def tile_list_tint_adjustment_kernel(
         inv_base = held([P, 2 * PACK], F32, "inv_base")
         nc.scalar.activation(out=inv_base[:], in_=inv_root[:], func=ACT.Square)
 
-        def quantize(rounded, width, name):
-            codes = held([P, width], U32, name + "_codes")
-            plane = held([P, width], U8, name + "_plane")
-            nc.vector.quantize_mx(out=codes[:].bitcast(E4M3), scales=plane[:], in_=rounded)
-            return codes, plane
 
-        picked = [held([P, S], U32, f"picked{x}") for x in range(3)]
-
-        def gather(x, c0, count):
-            nc.vector.tensor_copy(
-                out=picked[x][:, c0:c0 + count],
-                in_=windows[x][:].bitcast(U32).indirect(table_lists[x][:, c0 // 16:(c0 + count) // 16]),
-            )
-
-        wa_codes, wp_codes, ws_codes, ws_plane, wc_codes, wc_plane = {}, {}, {}, {}, {}, {}
+        wa_codes, wp_codes = {}, {}
 
         def sort_wa(b):
-            wa_codes[b] = held([P, 2, KP // 2], I32, f"wa_codes{b}")
+            wa_codes[b] = held([P, 2, KP // 2], I32, f"wa_codes{b}", "window1" if b else None)
             nc.vector.tensor_copy(
                 out=wa_codes[b][:].rearrange("p a (t h w) -> p a t h w", t=PACK, w=2),
                 in_=wa_raw[:, :, b * (KP // 2):(b + 1) * (KP // 2)].rearrange("p a (h t w) -> p a t h w", t=PACK, w=2),
@@ -178,182 +159,217 @@ def tile_list_tint_adjustment_kernel(
                 in_=wp_raw[:, b * KP:(b + 1) * KP].rearrange("p (h t i) -> p h t i", t=PACK, i=4),
             )
 
-        def prepare_ws(b, a):
-            rounded = held([P, PACK * KP], BF16, f"ws_rounded{b}{a}")
-            for t in range(PACK):
-                nc.vector.tensor_copy(
-                    out=rounded[:, t * KP:(t + 1) * KP].rearrange("p (h i j) -> p h i j", i=4, j=PACK),
-                    in_=ws_raw[b, a][:].rearrange("p j (h t i) -> p t h i j", t=PACK, i=4)[:, t],
-                )
-            ws_codes[b, a], ws_plane[b, a] = quantize(rounded[:], KP, f"ws{b}{a}")
-
-        def prepare_wc(b, copies):
-            rounded = held([P, PACK * N], BF16, f"wc_rounded{b}")
-            for x, copy in enumerate(copies):
-                n0, n1 = x * (N // 2), (x + 1) * (N // 2)
-                copy(
-                    out=rounded[:, n0 * PACK:n1 * PACK].rearrange("p (c t) -> p c t", t=PACK),
-                    in_=wc_raw[b][:, :, n0:n1].rearrange("p t c -> p c t"),
-                )
-            wc_codes[b], wc_plane[b] = quantize(rounded[:], N, f"wc{b}")
-
-        gather(0, 0, S)
-        gather(1, 0, S)
-        for b in range(2):
-            wc_raw[b] = held([P, PACK, N], F32, f"wc_raw{b}", f"window{b}")
-            rows = wc[b * KP:(b + 1) * KP, :].rearrange("(h t i) n -> t h i n", t=PACK, i=4)
-            for t in range(PACK):
-                nc.sync.dma_start(out=wc_raw[b][:, t, :], in_=rows[t])
         absorbed = [held([P, PACK, S], F32, f"absorbed{b}") for b in range(2)]
+        everything = slice(0, S)
+
+        def absorb_pass(absorb, b, a, t):
+            nc.tensor.matmul_mx(
+                out=absorb[:],
+                lhsT=wa_codes[b][:, a, t * (P // 2):(t + 1) * (P // 2)].bitcast(U8).bitcast(E2M1),
+                lhsT_scale=wa_plane(b, a, t),
+                rhs=picked[a][:].bitcast(E4M3), rhs_scale=picked_plane(a, everything),
+                start=(a == 0), stop=(a == 1),
+            )
 
         def absorption(b):
-            sort_wa(b)
+            banks = [bank(PACK * b + t, [P, S]) for t in range(PACK)]
             for t in range(PACK):
-                absorb = psum.tile([P, S], F32, name="absorb", tag="absorb" if t % 2 == 0 else "acc")
-                for a in range(2):
-                    nc.tensor.matmul_mx(
-                        out=absorb[:],
-                        lhsT=wa_codes[b][:, a, t * (P // 2):(t + 1) * (P // 2)].bitcast(U8).bitcast(E2M1),
-                        lhsT_scale=wa_plane(b, a, t),
-                        rhs=picked[a][:].bitcast(E4M3), rhs_scale=picked_plane(a, slice(0, S)),
-                        start=(a == 0), stop=(a == 1),
-                    )
+                absorb_pass(banks[t], b, 0, t)
+            for t in range(PACK):
+                absorb_pass(banks[t], b, 1, t)
                 col = 2 * t + b
-                nc.scalar.activation(out=absorbed[b][:, t, :], in_=absorb[:], func=ACT.Abs, scale=inv_base[:, col:col + 1])
+                nc.scalar.activation(out=absorbed[b][:, t, :], in_=banks[t][:], func=ACT.Abs, scale=inv_base[:, col:col + 1])
 
+        sort_wa(0)
+        gather(1)
         absorption(0)
-        prepare_ws(0, 0)
-        prepare_ws(0, 1)
-        absorption(1)
-        gather(2, 0, HALF)
-        sort_wp(0)
-        gather(2, HALF, HALF)
+        sort_wa(1)
+        picked_rows2 = held([P, S], U8, "picked_rows2", "wa_raw")
+        late_rows = held([P, S + H], U8, "late_rows")
+        nc.vector.tensor_copy(out=picked_rows2[:], in_=tab_rows[2][:].indirect(lists2[:]))
+        nc.vector.tensor_copy(out=late_rows[:, 0:S].bitcast(I32), in_=picked_rows2[:].bitcast(I32))
+        load_window(2, 0, T)
+        nc.sync.dma_start(out=wp_raw[:], in_=wp_words[0].rearrange("p c i -> p (c i)").bitcast(I32))
 
-        scat, panel, sq, root, recip, quot = {}, {}, {}, {}, {}, {}
-        diffs, dist, d_codes, d_plane = {}, {}, {}, {}
-        finished = []
+        ws_rounded, ws_codes, ws_plane = {}, {}, {}
+        wc_rounded, wc_codes, wc_plane = {}, {}, {}
 
-        def shape_of(u):
-            width = UNITS[u][2]
-            return [P, BANK // width, width]
+        def round_ws(b, a, t0, slots):
+            ws_rounded[b, a, t0] = held([P, slots * KP], BF16, f"ws_rounded{b}{a}{t0}")
+            nc.vector.tensor_copy(
+                out=ws_rounded[b, a, t0][:].rearrange("p (t h i j) -> p t h i j", t=slots, i=4, j=PACK),
+                in_=ws_raw[b, a][:].rearrange("p j (h t i) -> p t h i j", t=PACK, i=4)[:, t0:t0 + slots],
+            )
 
-        def scat_products(u):
-            b, j0, width, t0 = UNITS[u]
-            slots = BANK // width
-            cols = slice(j0, j0 + width)
-            scat[u] = psum.tile(shape_of(u), F32, name="scat")
+        def quantize(rounded, width, name, tag=None):
+            codes = held([P, width], U32, name + "_codes", tag)
+            plane = held([P, width], U8, name + "_plane")
+            nc.vector.quantize_mx(out=codes[:].bitcast(E4M3), scales=plane[:], in_=rounded[:])
+            return codes, plane
+
+        def quantize_ws(b, a, t0, slots):
+            codes, plane = quantize(ws_rounded[b, a, t0], slots * P, f"ws{b}{a}{t0}")
+            for s in range(slots):
+                ws_codes[b, a, t0 + s] = codes[:, s * P:(s + 1) * P]
+                ws_plane[b, a, t0 + s] = plane[:, s * P:(s + 1) * P]
+
+        def round_wc(b, x, copy):
+            wc_rounded[b, x] = held([P, PACK * N // 2], BF16, f"wc_rounded{b}{x}")
+            copy(
+                out=wc_rounded[b, x][:].rearrange("p (c t) -> p c t", t=PACK),
+                in_=wc_raw[b][:, :, x * (N // 2):(x + 1) * (N // 2)].rearrange("p t c -> p c t"),
+            )
+
+        def quantize_wc(b, x):
+            codes, plane = quantize(wc_rounded[b, x], N // 2, f"wc{b}{x}")
+            for s in range(2):
+                wc_codes[b, 2 * x + s] = codes[:, s * P:(s + 1) * P]
+                wc_plane[b, 2 * x + s] = plane[:, s * P:(s + 1) * P]
+
+        squares = [held([P, PACK, S], F32, f"squares{b}") for b in range(2)]
+
+        def scattering(b, t):
+            scat = bank(PACK * b + t, [P, S])
             for a in range(2):
-                for s in range(slots):
-                    t = t0 + s
-                    nc.tensor.matmul_mx(
-                        out=scat[u][:, s, :],
-                        lhsT=ws_codes[b, a][:, t * P:(t + 1) * P].bitcast(E4M3),
-                        lhsT_scale=ws_plane[b, a][:, t * P:(t + 1) * P],
-                        rhs=picked[a][:, cols].bitcast(E4M3), rhs_scale=picked_plane(a, cols),
-                        start=(a == 0 and s == 0), stop=(a == 1 and s == slots - 1),
-                    )
-
-        def panel_products(u):
-            b, j0, width, t0 = UNITS[u]
-            cols = slice(j0, j0 + width)
-            panel[u] = psum.tile(shape_of(u), F32, name="panel")
-            for s in range(BANK // width):
-                t = t0 + s
                 nc.tensor.matmul_mx(
-                    out=panel[u][:, s, :],
-                    lhsT=wp_codes[b][:, t * P:(t + 1) * P].bitcast(E4M3),
-                    lhsT_scale=wp_plane(b, t),
-                    rhs=picked[2][:, cols].bitcast(E4M3), rhs_scale=picked_plane(2, cols),
+                    out=scat[:],
+                    lhsT=ws_codes[b, a, t].bitcast(E4M3), lhsT_scale=ws_plane[b, a, t],
+                    rhs=picked[a][:].bitcast(E4M3), rhs_scale=picked_plane(a, everything),
+                    start=(a == 0), stop=(a == 1),
+                )
+            col = 2 * t + b
+            nc.scalar.activation(out=squares[b][:, t, :], in_=scat[:], func=ACT.Square, scale=inv_root[:, col:col + 1])
+
+        quot = [held([P, PACK, QUARTER], F32, f"quot{q}") for q in range(4)]
+
+        def cols_of(q):
+            return slice(q * QUARTER, (q + 1) * QUARTER)
+
+        def pair(tile, x):
+            return tile[:, 2 * x:2 * x + 2, :]
+
+        def inverse_root(target, source):
+            nc.scalar.activation(out=target, in_=source, func=ACT.Abs_reciprocal_sqrt, bias=1.0)
+
+        def square_root(target):
+            nc.scalar.activation(out=target, in_=target, func=ACT.Square)
+
+        def divide(target, numerator, inverse):
+            nc.vector.tensor_tensor(out=target, in0=numerator, in1=inverse, op=ALU.mult)
+
+        diffs, dist, d_codes, d_plane = {}, {}, {}, {}
+
+        def subtract(b, q):
+            panel = bank(PACK * b + q, [P, PACK, QUARTER])
+            for t in range(PACK):
+                nc.tensor.matmul_mx(
+                    out=panel[:, t, :],
+                    lhsT=wp_codes[b][:, t * P:(t + 1) * P].bitcast(E4M3), lhsT_scale=wp_plane(b, t),
+                    rhs=picked[2][:, cols_of(q)].bitcast(E4M3), rhs_scale=picked_plane(2, cols_of(q)),
                     start=True, stop=True,
                 )
+            tag = None
+            diffs[b, q] = held([P, PACK, QUARTER], F32, f"diffs{b}{q}", tag)
+            nc.vector.tensor_tensor(out=diffs[b, q][:], in0=panel[:], in1=quotients_of[b][:, :, cols_of(q)], op=ALU.subtract)
 
-        def square_scat(u):
-            b, j0, width, t0 = UNITS[u]
-            sq[u] = work.tile(shape_of(u), F32, name="sq")
-            for s in range(BANK // width):
-                col = 2 * (t0 + s) + b
-                nc.scalar.activation(out=sq[u][:, s, :], in_=scat[u][:, s, :], func=ACT.Square, scale=inv_root[:, col:col + 1])
-
-        def inverse_root(u):
-            root[u] = work.tile(shape_of(u), F32, name="root")
-            nc.scalar.activation(out=root[u][:], in_=sq[u][:], func=ACT.Abs_reciprocal_sqrt, bias=1.0)
-
-        def square_root(u):
-            recip[u] = work.tile(shape_of(u), F32, name="recip")
-            nc.scalar.activation(out=recip[u][:], in_=root[u][:], func=ACT.Square)
-
-        def divide(u):
-            b, j0, width, t0 = UNITS[u]
-            quot[u] = work.tile(shape_of(u), F32, name="quot", bufs=QUOT_BUFS)
-            nc.vector.tensor_tensor(
-                out=quot[u][:], in0=absorbed[b][:, t0:t0 + BANK // width, j0:j0 + width], in1=recip[u][:], op=ALU.mult
-            )
-
-        def subtract(u):
-            b, j0, width, t0 = UNITS[u]
-            slots = BANK // width
-            if t0 == 0:
-                diffs[b, j0] = work.tile([P, PACK, width], F32, name="diff")
-            nc.vector.tensor_tensor(out=diffs[b, j0][:, t0:t0 + slots, :], in0=panel[u][:], in1=quot[u][:], op=ALU.subtract)
-            if t0 + slots == PACK:
-                finished.extend((b, j0, c0) for c0 in range(0, width, QUARTER))
-
-        def distance(b, j0, c0):
-            dist[b, j0 + c0] = work.tile([P, QUARTER * PACK], BF16, name="dist", align_bytes=64)
+        def distance(b, q):
+            if b == 1 or q % 2 == 0:
+                dist[b, q] = held([P, (2 - b) * QUARTER * PACK], BF16, f"dist{b}{q}")
+            target = dist[b, q][:] if b == 1 else dist[b, q - q % 2][:, (q % 2) * KP:(q % 2 + 1) * KP]
             nc.scalar.activation(
-                out=dist[b, j0 + c0][:].rearrange("p (c t) -> p c t", t=PACK),
-                in_=diffs[b, j0][:, :, c0:c0 + QUARTER].rearrange("p t c -> p c t"),
-                func=ACT.Abs,
+                out=target.rearrange("p (c t) -> p c t", t=PACK),
+                in_=diffs[b, q][:].rearrange("p t c -> p c t"), func=ACT.Abs,
             )
 
-        def second_stage(j0, n0, count, bank, copy):
-            acc = psum.tile([P, count, QUARTER], F32, name="acc", tag=bank)
+        def quantize_d(b, q):
+            codes, plane = quantize(dist[b, q], (2 - b) * QUARTER, f"d{b}{q}", None if b else f"wc_rounded1{q // 2}")
+            for s in range(2 - b):
+                d_codes[b, (q + s) * QUARTER] = codes[:, s * QUARTER:(s + 1) * QUARTER]
+                d_plane[b, (q + s) * QUARTER] = plane[:, s * QUARTER:(s + 1) * QUARTER]
+
+        def second_stage(q, n0, count, number, copy):
+            j0 = q * QUARTER
+            acc = bank(number, [P, count, QUARTER])
             for b in range(2):
                 for n in range(n0, n0 + count):
                     nc.tensor.matmul_mx(
                         out=acc[:, n - n0, :],
-                        lhsT=wc_codes[b][:, n * P:(n + 1) * P].bitcast(E4M3),
-                        lhsT_scale=wc_plane[b][:, n * P:(n + 1) * P],
-                        rhs=d_codes[b, j0][:].bitcast(E4M3), rhs_scale=d_plane[b, j0][:],
+                        lhsT=wc_codes[b, n].bitcast(E4M3), lhsT_scale=wc_plane[b, n],
+                        rhs=d_codes[b, j0].bitcast(E4M3), rhs_scale=d_plane[b, j0],
                         start=(b == 0 and n == n0), stop=(b == 1 and n == n0 + count - 1),
                     )
-            result = work.tile([P, count, QUARTER], F32, name="result", bufs=5)
+            result = held([P, count, QUARTER], F32, f"result{q}{n0}")
             copy(out=result[:], in_=acc[:])
             nc.sync.dma_start(
                 out=out[n0 * P:(n0 + count) * P, j0:j0 + QUARTER].rearrange("(n p) j -> p n j", p=P),
                 in_=result[:],
             )
 
-        def run(stage, u):
-            if 0 <= u < len(UNITS):
-                stage(u)
+        round_ws(0, 0, 0, 2)
+        round_ws(0, 0, 2, 2)
+        quantize_ws(0, 0, 0, 2)
+        quantize_ws(0, 0, 2, 2)
+        round_ws(0, 1, 0, 1)
+        for t in range(PACK):
+            if t + 1 < PACK:
+                round_ws(0, 1, t + 1, 1)
+            quantize_ws(0, 1, t, 1)
+            scattering(0, t)
+        sort_rows(late_rows[:, S:], wp_rows[:])
+        move_rows(nc.sync, late_planes, late_rows)
+        for b in range(2):
+            wc_raw[b] = held([P, PACK, N], F32, f"wc_raw{b}", f"window{b}")
+            rows = wc[b * KP:(b + 1) * KP, :].rearrange("(h t i) n -> t h i n", t=PACK, i=4)
+            for t in range(PACK):
+                nc.sync.dma_start(out=wc_raw[b][:, t, :], in_=rows[t])
 
-        taken = 0
-        scat_products(0)
-        for k in range(len(UNITS) + 2):
-            if k in (1, 2):
-                prepare_ws(1, k - 1)
-            run(square_scat, k)
-            run(subtract, k - 2)
-            if k == PACK + 1:
-                sort_wp(1)
-            run(scat_products, k + 1)
-            run(panel_products, k - 1)
-            run(square_root, k - 1)
-            run(divide, k - 1)
-            run(inverse_root, k)
-            ready = finished[taken:taken + (1 if k < DRAIN_STEP else 2)]
-            taken = taken + len(ready)
-            for b, j0, c0 in ready:
-                distance(b, j0, c0)
-            for b, j0, c0 in ready:
-                d_codes[b, j0 + c0], d_plane[b, j0 + c0] = quantize(dist[b, j0 + c0][:], QUARTER, f"d{b}{j0 + c0}")
-            if k == WC_STEP:
-                prepare_wc(0, [nc.vector.tensor_copy, nc.vector.tensor_copy])
-                prepare_wc(1, [nc.vector.tensor_copy, nc.scalar.copy])
-            for j in [j0 + c0 for b, j0, c0 in ready if b == 1]:
-                if j + QUARTER < S:
-                    second_stage(j, 0, PACK, "acc" if j < HALF else "absorb", nc.vector.tensor_copy)
-                else:
-                    second_stage(j, 0, 2, "scat", nc.vector.tensor_copy)
-                    second_stage(j, 2, 2, "scat", nc.scalar.copy)
+        for x in range(2):
+            inverse_root(pair(squares[0], x), pair(squares[0], x))
+        for x in range(2):
+            square_root(pair(squares[0], x))
+        absorption(1)
+        for a in range(2):
+            round_ws(1, a, 0, 2)
+            round_ws(1, a, 2, 2)
+            quantize_ws(1, a, 0, 2)
+            quantize_ws(1, a, 2, 2)
+        for t in range(PACK):
+            scattering(1, t)
+        gather(2)
+        sort_wp(0)
+        sort_wp(1)
+        quotient = held([P, PACK, S], F32, "quotient", "wp_raw")
+        for x in range(2):
+            divide(pair(quotient, x), pair(absorbed[0], x), pair(squares[0], x))
+
+        def quotients(q):
+            inverse_root(quot[q][:], squares[1][:, :, cols_of(q)])
+
+        quotients(0)
+        for q in range(4):
+            if q + 1 < 4:
+                quotients(q + 1)
+            square_root(quot[q][:])
+        quotients_of = [quotient]
+        for q in range(4):
+            subtract(0, q)
+            distance(0, q)
+        for b in range(2):
+            for x in range(2):
+                round_wc(b, x, nc.vector.tensor_copy)
+            for x in range(2):
+                quantize_wc(b, x)
+        quotients_of.append(held([P, PACK, S], F32, "quotient1", "window1"))
+        for q in range(4):
+            divide(quotients_of[1][:, :, cols_of(q)], absorbed[1][:, :, cols_of(q)], quot[q][:])
+            if q % 2 == 0:
+                quantize_d(0, q)
+            subtract(1, q)
+            if q > 0:
+                quantize_d(1, q - 1)
+            distance(1, q)
+            if q > 0:
+                second_stage(q - 1, 0, PACK, q - 1, nc.scalar.copy if q == 1 else nc.vector.tensor_copy)
+        quantize_d(1, 3)
+        second_stage(3, 0, 2, 3, nc.vector.tensor_copy)
+        second_stage(3, 2, 2, 4, nc.scalar.copy)

@@ -197,8 +197,8 @@ def tile_list_tint_adjustment_kernel(
         def round_ws(b, a, t0, slots):
             ws_rounded[b, a, t0] = held([P, slots * KP], BF16, f"ws_rounded{b}{a}{t0}")
             nc.vector.tensor_copy(
-                out=ws_rounded[b, a, t0][:].rearrange("p (t h i j) -> p t h i j", t=slots, i=4, j=PACK),
-                in_=ws_raw[b, a][:].rearrange("p j (h t i) -> p t h i j", t=PACK, i=4)[:, t0:t0 + slots],
+                out=ws_rounded[b, a, t0][:].rearrange("p (t h i j) -> p t h j i", t=slots, i=4, j=PACK),
+                in_=ws_raw[b, a][:].rearrange("p j (h t i) -> p t h j i", t=PACK, i=4)[:, t0:t0 + slots],
             )
 
         def quantize(rounded, width, name, tag=None):
@@ -216,8 +216,8 @@ def tile_list_tint_adjustment_kernel(
         def round_wc(b, x, copy):
             wc_rounded[b, x] = held([P, PACK * N // 2], BF16, f"wc_rounded{b}{x}")
             copy(
-                out=wc_rounded[b, x][:].rearrange("p (c t) -> p c t", t=PACK),
-                in_=wc_raw[b][:, :, x * (N // 2):(x + 1) * (N // 2)].rearrange("p t c -> p c t"),
+                out=wc_rounded[b, x][:].rearrange("p (c i t) -> p c t i", t=PACK, i=4),
+                in_=wc_raw[b][:, :, x * (N // 2):(x + 1) * (N // 2)].rearrange("p t (c i) -> p c t i", i=4),
             )
 
         def quantize_wc(b, x):
@@ -277,8 +277,8 @@ def tile_list_tint_adjustment_kernel(
                 dist[b, q] = held([P, (2 - b) * QUARTER * PACK], BF16, f"dist{b}{q}")
             target = dist[b, q][:] if b == 1 else dist[b, q - q % 2][:, (q % 2) * KP:(q % 2 + 1) * KP]
             nc.scalar.activation(
-                out=target.rearrange("p (c t) -> p c t", t=PACK),
-                in_=diffs[b, q][:].rearrange("p t c -> p c t"), func=ACT.Abs,
+                out=target.rearrange("p (c i t) -> p c t i", t=PACK, i=4),
+                in_=diffs[b, q][:].rearrange("p t (c i) -> p c t i", i=4), func=ACT.Abs,
             )
 
         def quantize_d(b, q):

@@ -97,10 +97,10 @@ def tile_list_tint_adjustment_kernel(
             )
         nc.gpsimd.dma_start(out=base_rows[0:P:16, :], in_=base.rearrange("(b d x) -> d b x", b=2, d=4))
         load_window(0, T // 4, T - T // 4)
-        nc.sync.dma_start(out=wa_raw[:], in_=wa_words.bitcast(I32).rearrange("a p c -> p a c"))
         load_window(1, 0, T)
+        nc.sync.dma_start(out=wa_raw[:], in_=wa_words.bitcast(I32).rearrange("a p c -> p a c"))
         nc.sync.dma_start(lists2[:], offs2)
-        load_rows(nc.sync, 2)
+        load_rows(nc.gpsimd, 2)
 
         picked_rows = held([P, 2 * S], U8, "picked_rows")
         for x in range(2):
@@ -146,7 +146,7 @@ def tile_list_tint_adjustment_kernel(
         wa_codes, wp_codes = {}, {}
 
         def sort_wa(b):
-            wa_codes[b] = held([P, 2, KP // 2], I32, f"wa_codes{b}", "window1" if b else None)
+            wa_codes[b] = held([P, 2, KP // 2], I32, f"wa_codes{b}")
             nc.vector.tensor_copy(
                 out=wa_codes[b][:].rearrange("p a (t h w) -> p a t h w", t=PACK, w=2),
                 in_=wa_raw[:, :, b * (KP // 2):(b + 1) * (KP // 2)].rearrange("p a (h t w) -> p a t h w", t=PACK, w=2),
@@ -175,13 +175,18 @@ def tile_list_tint_adjustment_kernel(
             banks = [bank(PACK * b + t, [P, S]) for t in range(PACK)]
             for t in range(PACK):
                 absorb_pass(banks[t], b, 0, t)
-            for t in range(PACK):
                 absorb_pass(banks[t], b, 1, t)
                 col = 2 * t + b
                 nc.scalar.activation(out=absorbed[b][:, t, :], in_=banks[t][:], func=ACT.Abs, scale=inv_base[:, col:col + 1])
 
-        sort_wa(0)
         gather(1)
+        unread = bank(7, [P, S])
+        for x in range(4):
+            nc.tensor.matmul_mx(
+                out=unread[:], lhsT=picked[0][:, 0:P].bitcast(E4M3), lhsT_scale=picked_rows[:, 0:P],
+                rhs=picked[0][:].bitcast(E4M3), rhs_scale=picked_rows[:, 0:S], start=True, stop=True,
+            )
+        sort_wa(0)
         absorption(0)
         sort_wa(1)
         picked_rows2 = held([P, S], U8, "picked_rows2", "wa_raw")

@@ -21,6 +21,8 @@ PACK = 4
 KP = P * PACK
 BANK = 512
 HALF = S // 2
+ROW0 = 4
+LATE0 = 8
 QUARTER = S // 4
 
 
@@ -50,12 +52,12 @@ def tile_list_tint_adjustment_kernel(
         wa_rows = held([P, 2 * H], U8, "wa_rows")
         wp_rows = held([P, H], U8, "wp_rows")
         base_rows = held([P, P], F32, "base_rows")
-        early_planes = held([P, 2 * S], U8, "early_planes")
-        wa_planes = held([P, 2 * H], U8, "wa_planes")
+        early_planes = held([P, 2 * S + 2 * H], U8, "early_planes")
         late_planes = held([P, S + H], U8, "late_planes")
-        for cleared in (tab_rows[0], tab_rows[1], wa_rows):
-            nc.vector.memset(cleared[:].bitcast(I32), 0)
+        nc.vector.memset(tab_rows[0][:].bitcast(I32), 0)
         nc.vector.memset(base_rows[:], 0.0)
+        for cleared in (tab_rows[1], wa_rows):
+            nc.vector.memset(cleared[:].bitcast(I32), 0)
         for cleared in (tab_rows[2], wp_rows, early_planes, late_planes):
             nc.vector.memset(cleared[:].bitcast(I32), 0)
 
@@ -70,15 +72,15 @@ def tile_list_tint_adjustment_kernel(
             nc.sync.dma_start(out=windows[x][:, c0:c0 + count], in_=words[:, c0:c0 + count])
 
         def load_rows(queue, x):
-            queue.dma_start(out=tab_rows[x][0:P:8, :].bitcast(I32), in_=table_scales[x].bitcast(I32))
+            queue.dma_start(out=tab_rows[x][ROW0:P:8, :].bitcast(I32), in_=table_scales[x].bitcast(I32))
 
         def load_ws(b, a):
             rows = ws[a * KP:(a + 1) * KP, b * KP:(b + 1) * KP]
             nc.sync.dma_start(out=ws_raw[b, a][:], in_=rows.rearrange("(p j) c -> p j c", j=PACK))
 
-        def move_rows(queue, planes, rows):
+        def move_rows(queue, planes, rows, first):
             for r in range(4):
-                queue.dma_start(out=planes[r:P:32, :].bitcast(I32), in_=rows[8 * r:P:32, :].bitcast(I32))
+                queue.dma_start(out=planes[first + r:P:32, :].bitcast(I32), in_=rows[ROW0 + 8 * r:P:32, :].bitcast(I32))
 
         def sort_rows(sorted_rows, rows):
             nc.vector.tensor_copy(
@@ -89,39 +91,55 @@ def tile_list_tint_adjustment_kernel(
         nc.sync.dma_start(lists[:], offs)
         load_window(0, 0, T // 4)
         load_rows(nc.sync, 0)
+        nc.sync.dma_start(out=base_rows[0:P:16, :], in_=base.rearrange("(b d x) -> d b x", b=2, d=4))
         load_rows(nc.sync, 1)
-        for d in range(4):
-            nc.scalar.dma_start(
-                out=wa_rows[32 * d:32 * d + 4, :].bitcast(I32).rearrange("q (a c) -> q a c", a=2),
-                in_=wa_scales[:, 4 * d:4 * d + 4, :].bitcast(I32).rearrange("a q c -> q a c"),
-            )
-        nc.gpsimd.dma_start(out=base_rows[0:P:16, :], in_=base.rearrange("(b d x) -> d b x", b=2, d=4))
+        nc.sync.dma_start(
+            out=wa_rows[ROW0:P:8, :].bitcast(I32).rearrange("q (a c) -> q a c", a=2),
+            in_=wa_scales.bitcast(I32).rearrange("a q c -> q a c"),
+        )
         load_window(0, T // 4, T - T // 4)
         load_window(1, 0, T)
         nc.sync.dma_start(out=wa_raw[:], in_=wa_words.bitcast(I32).rearrange("a p c -> p a c"))
         nc.sync.dma_start(lists2[:], offs2)
-        load_rows(nc.gpsimd, 2)
+        load_rows(nc.sync, 2)
 
         picked_rows = held([P, 2 * S], U8, "picked_rows")
         for x in range(2):
             nc.vector.tensor_copy(out=picked_rows[:, x * S:(x + 1) * S], in_=tab_rows[x][:].indirect(lists[:]))
-        move_rows(nc.scalar, early_planes, picked_rows)
+        base_sorted = held([P, P], F32, "base_sorted")
+        nc.vector.tensor_copy(
+            out=base_sorted[:].rearrange("p (t h i) -> p t h i", t=PACK, i=4),
+            in_=base_rows[:].rearrange("p (h t i) -> p t h i", t=PACK, i=4),
+        )
+        base_cols = held([P, P], F32, "base_cols", "tab_rows1")
+        nc.vector.transpose(out=base_cols[:], in_=base_sorted[:])
+        inv_root = held([P, 2 * PACK], F32, "inv_root")
+        nc.scalar.activation(out=inv_root[:], in_=base_cols[:, 0:P:16], func=ACT.Abs_reciprocal_sqrt)
+        inv_base = held([P, 2 * PACK], F32, "inv_base")
+        nc.scalar.activation(out=inv_base[:], in_=inv_root[:], func=ACT.Square)
+
+
+        early_rows = held([P, 2 * S + 2 * H], U8, "early_rows")
+        sort_rows(early_rows[:, 2 * S:], wa_rows[:])
+        nc.vector.tensor_copy(out=early_rows[:, 0:2 * S].bitcast(I32), in_=picked_rows[:].bitcast(I32))
+        move_rows(nc.sync, early_planes, early_rows, 0)
         load_ws(0, 0)
         load_ws(0, 1)
-        nc.sync.dma_start(out=wp_rows[0:P:8, :].bitcast(I32), in_=wp_scales[0].bitcast(I32))
+        nc.sync.dma_start(out=wp_rows[ROW0:P:8, :].bitcast(I32), in_=wp_scales[0].bitcast(I32))
         load_ws(1, 0)
+        nc.sync.dma_start(out=wp_raw[:], in_=wp_words[0].rearrange("p c i -> p (c i)").bitcast(I32))
         load_ws(1, 1)
 
         def picked_plane(x, cols):
-            return early_planes[:, x * S + cols.start:x * S + cols.stop] if x < 2 else late_planes[:, cols]
+            return early_planes[:, x * S + cols.start:x * S + cols.stop] if x < 2 else late_planes[LATE0:P, cols]
 
         def wa_plane(b, a, t):
-            c0 = a * H + b * KP + t * P
-            return wa_planes[:, c0:c0 + P]
+            c0 = 2 * S + a * H + b * KP + t * P
+            return early_planes[:, c0:c0 + P]
 
         def wp_plane(b, t):
             c0 = S + b * KP + t * P
-            return late_planes[:, c0:c0 + P]
+            return late_planes[LATE0:P, c0:c0 + P]
 
         picked = [held([P, S], U32, f"picked{x}") for x in range(3)]
 
@@ -129,19 +147,6 @@ def tile_list_tint_adjustment_kernel(
             nc.vector.tensor_copy(out=picked[x][:], in_=windows[x][:].bitcast(U32).indirect(table_lists[x][:]))
 
         gather(0)
-        sort_rows(wa_planes[:], wa_rows[:])
-        base_sorted = held([P, P], F32, "base_sorted", "window0")
-        nc.vector.tensor_copy(
-            out=base_sorted[:].rearrange("p (t h i) -> p t h i", t=PACK, i=4),
-            in_=base_rows[:].rearrange("p (h t i) -> p t h i", t=PACK, i=4),
-        )
-        base_cols = held([P, P], F32, "base_cols")
-        nc.vector.transpose(out=base_cols[:], in_=base_sorted[:])
-        inv_root = held([P, 2 * PACK], F32, "inv_root")
-        nc.scalar.activation(out=inv_root[:], in_=base_cols[:, 0:P:16], func=ACT.Abs_reciprocal_sqrt)
-        inv_base = held([P, 2 * PACK], F32, "inv_base")
-        nc.scalar.activation(out=inv_base[:], in_=inv_root[:], func=ACT.Square)
-
 
         wa_codes, wp_codes = {}, {}
 
@@ -183,8 +188,8 @@ def tile_list_tint_adjustment_kernel(
         unread = bank(7, [P, S])
         for x in range(4):
             nc.tensor.matmul_mx(
-                out=unread[:], lhsT=picked[0][:, 0:P].bitcast(E4M3), lhsT_scale=picked_rows[:, 0:P],
-                rhs=picked[0][:].bitcast(E4M3), rhs_scale=picked_rows[:, 0:S], start=True, stop=True,
+                out=unread[:], lhsT=windows[0][:, 0:P].bitcast(E4M3), lhsT_scale=early_rows[:, 0:P],
+                rhs=windows[0][:, 0:S].bitcast(E4M3), rhs_scale=early_rows[:, 0:S], start=True, stop=True,
             )
         sort_wa(0)
         absorption(0)
@@ -194,7 +199,6 @@ def tile_list_tint_adjustment_kernel(
         nc.vector.tensor_copy(out=picked_rows2[:], in_=tab_rows[2][:].indirect(lists2[:]))
         nc.vector.tensor_copy(out=late_rows[:, 0:S].bitcast(I32), in_=picked_rows2[:].bitcast(I32))
         load_window(2, 0, T)
-        nc.sync.dma_start(out=wp_raw[:], in_=wp_words[0].rearrange("p c i -> p (c i)").bitcast(I32))
 
         ws_rounded, ws_codes, ws_plane = {}, {}, {}
         wc_rounded, wc_codes, wc_plane = {}, {}, {}
@@ -264,33 +268,26 @@ def tile_list_tint_adjustment_kernel(
 
         diffs, dist, d_codes, d_plane = {}, {}, {}, {}
 
-        def subtract(b, q):
-            panel = bank(PACK * b + q, [P, PACK, QUARTER])
-            for t in range(PACK):
-                nc.tensor.matmul_mx(
-                    out=panel[:, t, :],
-                    lhsT=wp_codes[b][:, t * P:(t + 1) * P].bitcast(E4M3), lhsT_scale=wp_plane(b, t),
-                    rhs=picked[2][:, cols_of(q)].bitcast(E4M3), rhs_scale=picked_plane(2, cols_of(q)),
-                    start=True, stop=True,
-                )
-            tag = None
-            diffs[b, q] = held([P, PACK, QUARTER], F32, f"diffs{b}{q}", tag)
-            nc.vector.tensor_tensor(out=diffs[b, q][:], in0=panel[:], in1=quotients_of[b][:, :, cols_of(q)], op=ALU.subtract)
-
-        def distance(b, q):
-            if b == 1 or q % 2 == 0:
-                dist[b, q] = held([P, (2 - b) * QUARTER * PACK], BF16, f"dist{b}{q}")
-            target = dist[b, q][:] if b == 1 else dist[b, q - q % 2][:, (q % 2) * KP:(q % 2 + 1) * KP]
-            nc.scalar.activation(
-                out=target.rearrange("p (c i t) -> p c t i", t=PACK, i=4),
-                in_=diffs[b, q][:].rearrange("p t (c i) -> p c t i", i=4), func=ACT.Abs,
+        def panel_pass(target, b, t, cols):
+            nc.tensor.matmul_mx(
+                out=target,
+                lhsT=wp_codes[b][:, t * P:(t + 1) * P].bitcast(E4M3), lhsT_scale=wp_plane(b, t),
+                rhs=picked[2][:, cols].bitcast(E4M3), rhs_scale=picked_plane(2, cols),
+                start=True, stop=True,
             )
 
-        def quantize_d(b, q):
-            codes, plane = quantize(dist[b, q], (2 - b) * QUARTER, f"d{b}{q}", None if b else f"wc_rounded1{q // 2}")
-            for s in range(2 - b):
-                d_codes[b, (q + s) * QUARTER] = codes[:, s * QUARTER:(s + 1) * QUARTER]
-                d_plane[b, (q + s) * QUARTER] = plane[:, s * QUARTER:(s + 1) * QUARTER]
+        def distance(b, j0, source):
+            dist[b, j0] = held([P, source.shape[2] * PACK], BF16, f"dist{b}{j0}")
+            nc.scalar.activation(
+                out=dist[b, j0][:].rearrange("p (c i t) -> p c t i", t=PACK, i=4),
+                in_=source.rearrange("p t (c i) -> p c t i", i=4), func=ACT.Abs,
+            )
+
+        def quantize_d(b, j0, width, tag=None):
+            codes, plane = quantize(dist[b, j0], width, f"d{b}{j0}", tag)
+            for c0 in range(0, width, QUARTER):
+                d_codes[b, j0 + c0] = codes[:, c0:c0 + QUARTER]
+                d_plane[b, j0 + c0] = plane[:, c0:c0 + QUARTER]
 
         def second_stage(q, n0, count, number, copy):
             j0 = q * QUARTER
@@ -320,61 +317,79 @@ def tile_list_tint_adjustment_kernel(
                 round_ws(0, 1, t + 1, 1)
             quantize_ws(0, 1, t, 1)
             scattering(0, t)
+            if t > 1:
+                square_root(squares[0][:, t - 2, :])
+            if t > 0:
+                inverse_root(squares[0][:, t - 1, :], squares[0][:, t - 1, :])
         sort_rows(late_rows[:, S:], wp_rows[:])
-        move_rows(nc.sync, late_planes, late_rows)
+        move_rows(nc.sync, late_planes, late_rows, LATE0)
         for b in range(2):
             wc_raw[b] = held([P, PACK, N], F32, f"wc_raw{b}", f"window{b}")
             rows = wc[b * KP:(b + 1) * KP, :].rearrange("(h t i) n -> t h i n", t=PACK, i=4)
             for t in range(PACK):
                 nc.sync.dma_start(out=wc_raw[b][:, t, :], in_=rows[t])
 
-        for x in range(2):
-            inverse_root(pair(squares[0], x), pair(squares[0], x))
-        for x in range(2):
-            square_root(pair(squares[0], x))
+        inverse_root(squares[0][:, PACK - 1, :], squares[0][:, PACK - 1, :])
+        for t in (PACK - 2, PACK - 1):
+            square_root(squares[0][:, t, :])
         absorption(1)
+        slot_quot = []
+
+        def divide_slot(tag):
+            t = len(slot_quot)
+            slot_quot.append(held([P, S], F32, f"slot_quot{t}", tag)[:])
+            divide(slot_quot[t], absorbed[0][:, t, :], squares[0][:, t, :])
+
         for a in range(2):
             round_ws(1, a, 0, 2)
             round_ws(1, a, 2, 2)
             quantize_ws(1, a, 0, 2)
             quantize_ws(1, a, 2, 2)
+            if a == 0:
+                sort_wp(0)
+                sort_wp(1)
+            divide_slot("ws_raw11" if a else "wp_raw")
         for t in range(PACK):
             scattering(1, t)
         gather(2)
-        sort_wp(0)
-        sort_wp(1)
-        quotient = held([P, PACK, S], F32, "quotient", "wp_raw")
-        for x in range(2):
-            divide(pair(quotient, x), pair(absorbed[0], x), pair(squares[0], x))
+        last_two = held([P, 2, S], F32, "last_two", "window2")
+        for t in (2, 3):
+            slot_quot.append(last_two[:, t - 2, :])
+            divide(slot_quot[t], absorbed[0][:, t, :], squares[0][:, t, :])
+        diffs0 = held([P, PACK, S], F32, "diffs_all")
+        for t in range(PACK):
+            panel = bank(t, [P, S])
+            panel_pass(panel[:], 0, t, everything)
+            nc.vector.tensor_tensor(out=diffs0[:, t, :], in0=panel[:], in1=slot_quot[t], op=ALU.subtract)
 
-        def quotients(q):
-            inverse_root(quot[q][:], squares[1][:, :, cols_of(q)])
-
-        quotients(0)
-        for q in range(4):
-            if q + 1 < 4:
-                quotients(q + 1)
-            square_root(quot[q][:])
-        quotients_of = [quotient]
-        for q in range(4):
-            subtract(0, q)
-            distance(0, q)
+        for q in range(4 + 1):
+            if q < 4:
+                inverse_root(quot[q][:], squares[1][:, :, cols_of(q)])
+            if q > 0:
+                square_root(quot[q - 1][:])
+            if q in (2, 4):
+                distance(0, (q - 2) * QUARTER, diffs0[:, :, (q - 2) * QUARTER:q * QUARTER])
         for b in range(2):
             for x in range(2):
                 round_wc(b, x, nc.vector.tensor_copy)
             for x in range(2):
                 quantize_wc(b, x)
-        quotients_of.append(held([P, PACK, S], F32, "quotient1", "window1"))
+        quotient = held([P, PACK, S], F32, "quotient", "window1")
         for q in range(4):
-            divide(quotients_of[1][:, :, cols_of(q)], absorbed[1][:, :, cols_of(q)], quot[q][:])
-            if q % 2 == 0:
-                quantize_d(0, q)
-            subtract(1, q)
-            if q > 0:
-                quantize_d(1, q - 1)
-            distance(1, q)
-            if q > 0:
-                second_stage(q - 1, 0, PACK, q - 1, nc.scalar.copy if q == 1 else nc.vector.tensor_copy)
-        quantize_d(1, 3)
+            divide(quotient[:, :, cols_of(q)], absorbed[1][:, :, cols_of(q)], quot[q][:])
+            panel = bank(PACK + q, [P, PACK, QUARTER])
+            for t in range(PACK):
+                panel_pass(panel[:, t, :], 1, t, cols_of(q))
+            diffs[q] = held([P, PACK, QUARTER], F32, f"diffs{q}")
+            nc.vector.tensor_tensor(out=diffs[q][:], in0=panel[:], in1=quotient[:, :, cols_of(q)], op=ALU.subtract)
+            if q < 2:
+                quantize_d(0, q * HALF, HALF, f"wc_rounded1{q}")
+            distance(1, q * QUARTER, diffs[q][:])
+            if q > 1:
+                quantize_d(1, (q - 2) * QUARTER, QUARTER)
+                second_stage(q - 2, 0, PACK, q - 2, nc.scalar.copy)
+        quantize_d(1, 2 * QUARTER, QUARTER)
+        quantize_d(1, 3 * QUARTER, QUARTER)
+        second_stage(2, 0, PACK, 2, nc.vector.tensor_copy)
         second_stage(3, 0, 2, 3, nc.vector.tensor_copy)
         second_stage(3, 2, 2, 4, nc.scalar.copy)

@@ -91,13 +91,14 @@ def tile_list_tint_adjustment_kernel(
         nc.sync.dma_start(lists[:], offs)
         load_window(0, 0, T // 4)
         load_rows(nc.sync, 0)
+        load_window(0, T // 4, T // 4)
         nc.sync.dma_start(out=base_rows[0:P:16, :], in_=base.rearrange("(b d x) -> d b x", b=2, d=4))
         load_rows(nc.sync, 1)
         nc.sync.dma_start(
             out=wa_rows[ROW0:P:8, :].bitcast(I32).rearrange("q (a c) -> q a c", a=2),
             in_=wa_scales.bitcast(I32).rearrange("a q c -> q a c"),
         )
-        load_window(0, T // 4, T - T // 4)
+        load_window(0, T // 2, T // 2)
         load_window(1, 0, T)
         nc.sync.dma_start(out=wa_raw[:], in_=wa_words.bitcast(I32).rearrange("a p c -> p a c"))
         nc.sync.dma_start(lists2[:], offs2)
@@ -111,18 +112,17 @@ def tile_list_tint_adjustment_kernel(
             out=base_sorted[:].rearrange("p (t h i) -> p t h i", t=PACK, i=4),
             in_=base_rows[:].rearrange("p (h t i) -> p t h i", t=PACK, i=4),
         )
-        base_cols = held([P, P], F32, "base_cols", "tab_rows1")
-        nc.vector.transpose(out=base_cols[:], in_=base_sorted[:])
-        inv_root = held([P, 2 * PACK], F32, "inv_root")
-        nc.scalar.activation(out=inv_root[:], in_=base_cols[:, 0:P:16], func=ACT.Abs_reciprocal_sqrt)
-        inv_base = held([P, 2 * PACK], F32, "inv_base")
-        nc.scalar.activation(out=inv_base[:], in_=inv_root[:], func=ACT.Square)
-
 
         early_rows = held([P, 2 * S + 2 * H], U8, "early_rows")
         sort_rows(early_rows[:, 2 * S:], wa_rows[:])
         nc.vector.tensor_copy(out=early_rows[:, 0:2 * S].bitcast(I32), in_=picked_rows[:].bitcast(I32))
         move_rows(nc.sync, early_planes, early_rows, 0)
+        base_cols = held([P, P], F32, "base_cols", "wa_rows")
+        nc.vector.transpose(out=base_cols[:], in_=base_sorted[:])
+        inv_root = held([P, 2 * PACK], F32, "inv_root")
+        nc.scalar.activation(out=inv_root[:], in_=base_cols[:, 0:P:16], func=ACT.Abs_reciprocal_sqrt)
+        inv_base = held([P, 2 * PACK], F32, "inv_base")
+        nc.scalar.activation(out=inv_base[:], in_=inv_root[:], func=ACT.Square)
         load_ws(0, 0)
         load_ws(0, 1)
         nc.sync.dma_start(out=wp_rows[ROW0:P:8, :].bitcast(I32), in_=wp_scales[0].bitcast(I32))
@@ -249,7 +249,6 @@ def tile_list_tint_adjustment_kernel(
             col = 2 * t + b
             nc.scalar.activation(out=squares[b][:, t, :], in_=scat[:], func=ACT.Square, scale=inv_root[:, col:col + 1])
 
-        quot = [held([P, PACK, QUARTER], F32, f"quot{q}") for q in range(4)]
 
         def cols_of(q):
             return slice(q * QUARTER, (q + 1) * QUARTER)
@@ -362,6 +361,8 @@ def tile_list_tint_adjustment_kernel(
             panel_pass(panel[:], 0, t, everything)
             nc.vector.tensor_tensor(out=diffs0[:, t, :], in0=panel[:], in1=slot_quot[t], op=ALU.subtract)
 
+        all_quot = held([P, 4, PACK, QUARTER], F32, "all_quot", None)
+        quot = [all_quot[:, q] for q in range(4)]
         for q in range(4 + 1):
             if q < 4:
                 inverse_root(quot[q][:], squares[1][:, :, cols_of(q)])
@@ -371,12 +372,15 @@ def tile_list_tint_adjustment_kernel(
                 distance(0, (q - 2) * QUARTER, diffs0[:, :, (q - 2) * QUARTER:q * QUARTER])
         for b in range(2):
             for x in range(2):
-                round_wc(b, x, nc.vector.tensor_copy)
+                if (b, x) not in wc_rounded:
+                    round_wc(b, x, nc.vector.tensor_copy)
             for x in range(2):
                 quantize_wc(b, x)
         quotient = held([P, PACK, S], F32, "quotient", "window1")
         for q in range(4):
             divide(quotient[:, :, cols_of(q)], absorbed[1][:, :, cols_of(q)], quot[q][:])
+            if q == 3:
+                quantize_d(1, QUARTER, QUARTER)
             panel = bank(PACK + q, [P, PACK, QUARTER])
             for t in range(PACK):
                 panel_pass(panel[:, t, :], 1, t, cols_of(q))
@@ -385,11 +389,12 @@ def tile_list_tint_adjustment_kernel(
             if q < 2:
                 quantize_d(0, q * HALF, HALF, f"wc_rounded1{q}")
             distance(1, q * QUARTER, diffs[q][:])
-            if q > 1:
-                quantize_d(1, (q - 2) * QUARTER, QUARTER)
-                second_stage(q - 2, 0, PACK, q - 2, nc.scalar.copy)
+            if q == 2:
+                quantize_d(1, 0, QUARTER)
+                second_stage(0, 0, PACK, 0, nc.scalar.copy)
+        second_stage(1, 0, PACK, 1, nc.scalar.copy)
         quantize_d(1, 2 * QUARTER, QUARTER)
         quantize_d(1, 3 * QUARTER, QUARTER)
         second_stage(2, 0, PACK, 2, nc.vector.tensor_copy)
         second_stage(3, 0, 2, 3, nc.vector.tensor_copy)
-        second_stage(3, 2, 2, 4, nc.scalar.copy)
+        second_stage(3, 2, 2, 6, nc.scalar.copy)

@@ -50,15 +50,12 @@ def tile_list_tint_adjustment_kernel(
 
         tab_rows = [held([P, T], U8, f"tab_rows{x}") for x in range(3)]
         wa_rows = held([P, 2 * H], U8, "wa_rows")
-        wp_rows = held([P, H], U8, "wp_rows")
         base_rows = held([P, P], F32, "base_rows")
         early_planes = held([P, 2 * S + 2 * H], U8, "early_planes")
-        late_planes = held([P, S + H], U8, "late_planes")
-        nc.vector.memset(tab_rows[0][:].bitcast(I32), 0)
-        nc.vector.memset(base_rows[:], 0.0)
-        for cleared in (tab_rows[1], wa_rows):
+        for cleared in (tab_rows[0], tab_rows[1], wa_rows):
             nc.vector.memset(cleared[:].bitcast(I32), 0)
-        for cleared in (tab_rows[2], wp_rows, early_planes, late_planes):
+        nc.vector.memset(base_rows[:], 0.0)
+        for cleared in (early_planes, tab_rows[2]):
             nc.vector.memset(cleared[:].bitcast(I32), 0)
 
         windows = [held([P, T], I32, f"window{x}") for x in range(3)]
@@ -89,35 +86,33 @@ def tile_list_tint_adjustment_kernel(
             )
 
         nc.sync.dma_start(lists[:], offs)
+        nc.sync.dma_start(lists2[:], offs2)
         load_window(0, 0, T // 4)
         load_rows(nc.sync, 0)
-        load_window(0, T // 4, T // 4)
-        nc.sync.dma_start(out=base_rows[0:P:16, :], in_=base.rearrange("(b d x) -> d b x", b=2, d=4))
         load_rows(nc.sync, 1)
         nc.sync.dma_start(
             out=wa_rows[ROW0:P:8, :].bitcast(I32).rearrange("q (a c) -> q a c", a=2),
             in_=wa_scales.bitcast(I32).rearrange("a q c -> q a c"),
         )
-        load_window(0, T // 2, T // 2)
+        load_window(0, T // 4, T - T // 4)
+        nc.sync.dma_start(out=base_rows[0:P:16, :], in_=base.rearrange("(b d x) -> d b x", b=2, d=4))
         load_window(1, 0, T)
         nc.sync.dma_start(out=wa_raw[:], in_=wa_words.bitcast(I32).rearrange("a p c -> p a c"))
-        nc.sync.dma_start(lists2[:], offs2)
         load_rows(nc.sync, 2)
 
         picked_rows = held([P, 2 * S], U8, "picked_rows")
         for x in range(2):
             nc.vector.tensor_copy(out=picked_rows[:, x * S:(x + 1) * S], in_=tab_rows[x][:].indirect(lists[:]))
+        early_rows = held([P, 2 * S + 2 * H], U8, "early_rows")
+        sort_rows(early_rows[:, 2 * S:], wa_rows[:])
+        nc.vector.tensor_copy(out=early_rows[:, 0:2 * S].bitcast(I32), in_=picked_rows[:].bitcast(I32))
+        move_rows(nc.sync, early_planes, early_rows, 0)
         base_sorted = held([P, P], F32, "base_sorted")
         nc.vector.tensor_copy(
             out=base_sorted[:].rearrange("p (t h i) -> p t h i", t=PACK, i=4),
             in_=base_rows[:].rearrange("p (h t i) -> p t h i", t=PACK, i=4),
         )
-
-        early_rows = held([P, 2 * S + 2 * H], U8, "early_rows")
-        sort_rows(early_rows[:, 2 * S:], wa_rows[:])
-        nc.vector.tensor_copy(out=early_rows[:, 0:2 * S].bitcast(I32), in_=picked_rows[:].bitcast(I32))
-        move_rows(nc.sync, early_planes, early_rows, 0)
-        base_cols = held([P, P], F32, "base_cols", "wa_rows")
+        base_cols = held([P, P], F32, "base_cols")
         nc.vector.transpose(out=base_cols[:], in_=base_sorted[:])
         inv_root = held([P, 2 * PACK], F32, "inv_root")
         nc.scalar.activation(out=inv_root[:], in_=base_cols[:, 0:P:16], func=ACT.Abs_reciprocal_sqrt)
@@ -125,10 +120,6 @@ def tile_list_tint_adjustment_kernel(
         nc.scalar.activation(out=inv_base[:], in_=inv_root[:], func=ACT.Square)
         load_ws(0, 0)
         load_ws(0, 1)
-        nc.sync.dma_start(out=wp_rows[ROW0:P:8, :].bitcast(I32), in_=wp_scales[0].bitcast(I32))
-        load_ws(1, 0)
-        nc.sync.dma_start(out=wp_raw[:], in_=wp_words[0].rearrange("p c i -> p (c i)").bitcast(I32))
-        load_ws(1, 1)
 
         def picked_plane(x, cols):
             return early_planes[:, x * S + cols.start:x * S + cols.stop] if x < 2 else late_planes[LATE0:P, cols]
@@ -157,12 +148,14 @@ def tile_list_tint_adjustment_kernel(
                 in_=wa_raw[:, :, b * (KP // 2):(b + 1) * (KP // 2)].rearrange("p a (h t w) -> p a t h w", t=PACK, w=2),
             )
 
-        def sort_wp(b):
-            wp_codes[b] = held([P, KP], I32, f"wp_codes{b}")
+        def sort_wp():
+            both = held([P, H], I32, "wp_codes")
             nc.vector.tensor_copy(
-                out=wp_codes[b][:].rearrange("p (t h i) -> p h t i", t=PACK, i=4),
-                in_=wp_raw[:, b * KP:(b + 1) * KP].rearrange("p (h t i) -> p h t i", t=PACK, i=4),
+                out=both[:].rearrange("p (b t h i) -> p b h t i", b=2, t=PACK, i=4),
+                in_=wp_raw[:].rearrange("p (b h t i) -> p b h t i", b=2, t=PACK, i=4),
             )
+            for b in range(2):
+                wp_codes[b] = both[:, b * KP:(b + 1) * KP]
 
         absorbed = [held([P, PACK, S], F32, f"absorbed{b}") for b in range(2)]
         everything = slice(0, S)
@@ -188,16 +181,22 @@ def tile_list_tint_adjustment_kernel(
         unread = bank(7, [P, S])
         for x in range(4):
             nc.tensor.matmul_mx(
-                out=unread[:], lhsT=windows[0][:, 0:P].bitcast(E4M3), lhsT_scale=early_rows[:, 0:P],
+                out=unread[:], lhsT=windows[0][:, 0:P].bitcast(E4M3), lhsT_scale=early_rows[:, 2 * S:2 * S + P],
                 rhs=windows[0][:, 0:S].bitcast(E4M3), rhs_scale=early_rows[:, 0:S], start=True, stop=True,
             )
         sort_wa(0)
         absorption(0)
         sort_wa(1)
         picked_rows2 = held([P, S], U8, "picked_rows2", "wa_raw")
-        late_rows = held([P, S + H], U8, "late_rows")
         nc.vector.tensor_copy(out=picked_rows2[:], in_=tab_rows[2][:].indirect(lists2[:]))
-        nc.vector.tensor_copy(out=late_rows[:, 0:S].bitcast(I32), in_=picked_rows2[:].bitcast(I32))
+        wp_rows = held([P, H], U8, "wp_rows", "tab_rows2")
+        late_planes = held([P, S + H], U8, "late_planes", "early_rows")
+        for cleared in (wp_rows, late_planes):
+            nc.vector.memset(cleared[:].bitcast(I32), 0)
+        load_ws(1, 0)
+        nc.sync.dma_start(out=wp_rows[ROW0:P:8, :].bitcast(I32), in_=wp_scales[0].bitcast(I32))
+        nc.sync.dma_start(out=wp_raw[:], in_=wp_words[0].rearrange("p c i -> p (c i)").bitcast(I32))
+        load_ws(1, 1)
         load_window(2, 0, T)
 
         ws_rounded, ws_codes, ws_plane = {}, {}, {}
@@ -222,18 +221,18 @@ def tile_list_tint_adjustment_kernel(
                 ws_codes[b, a, t0 + s] = codes[:, s * P:(s + 1) * P]
                 ws_plane[b, a, t0 + s] = plane[:, s * P:(s + 1) * P]
 
-        def round_wc(b, x, copy):
-            wc_rounded[b, x] = held([P, PACK * N // 2], BF16, f"wc_rounded{b}{x}")
-            copy(
-                out=wc_rounded[b, x][:].rearrange("p (c i t) -> p c t i", t=PACK, i=4),
-                in_=wc_raw[b][:, :, x * (N // 2):(x + 1) * (N // 2)].rearrange("p t (c i) -> p c t i", i=4),
+        def round_wc(b):
+            wc_rounded[b] = held([P, PACK * N], BF16, f"wc_rounded{b}")
+            nc.vector.tensor_copy(
+                out=wc_rounded[b][:].rearrange("p (c i t) -> p c t i", t=PACK, i=4),
+                in_=wc_raw[b][:].rearrange("p t (c i) -> p c t i", i=4),
             )
 
-        def quantize_wc(b, x):
-            codes, plane = quantize(wc_rounded[b, x], N // 2, f"wc{b}{x}")
-            for s in range(2):
-                wc_codes[b, 2 * x + s] = codes[:, s * P:(s + 1) * P]
-                wc_plane[b, 2 * x + s] = plane[:, s * P:(s + 1) * P]
+        def quantize_wc(b, tag):
+            codes, plane = quantize(wc_rounded[b], N, f"wc{b}", tag)
+            for n in range(PACK):
+                wc_codes[b, n] = codes[:, n * P:(n + 1) * P]
+                wc_plane[b, n] = plane[:, n * P:(n + 1) * P]
 
         squares = [held([P, PACK, S], F32, f"squares{b}") for b in range(2)]
 
@@ -306,15 +305,17 @@ def tile_list_tint_adjustment_kernel(
                 in_=result[:],
             )
 
-        round_ws(0, 0, 0, 2)
-        round_ws(0, 0, 2, 2)
-        quantize_ws(0, 0, 0, 2)
-        quantize_ws(0, 0, 2, 2)
+        round_ws(0, 0, 0, PACK)
+        late_rows = held([P, S + H], U8, "late_rows", "ws_raw00")
+        nc.vector.tensor_copy(out=late_rows[:, 0:S].bitcast(I32), in_=picked_rows2[:].bitcast(I32))
+        quantize_ws(0, 0, 0, PACK)
         round_ws(0, 1, 0, 1)
+        round_ws(0, 1, 1, 1)
+        quantize_ws(0, 1, 0, 1)
+        round_ws(0, 1, 2, 2)
+        quantize_ws(0, 1, 1, 1)
+        quantize_ws(0, 1, 2, 2)
         for t in range(PACK):
-            if t + 1 < PACK:
-                round_ws(0, 1, t + 1, 1)
-            quantize_ws(0, 1, t, 1)
             scattering(0, t)
             if t > 1:
                 square_root(squares[0][:, t - 2, :])
@@ -328,6 +329,7 @@ def tile_list_tint_adjustment_kernel(
             for t in range(PACK):
                 nc.sync.dma_start(out=wc_raw[b][:, t, :], in_=rows[t])
 
+        quot = [held([P, PACK, QUARTER], F32, f"quot{q}") for q in range(4)]
         inverse_root(squares[0][:, PACK - 1, :], squares[0][:, PACK - 1, :])
         for t in (PACK - 2, PACK - 1):
             square_root(squares[0][:, t, :])
@@ -339,30 +341,27 @@ def tile_list_tint_adjustment_kernel(
             slot_quot.append(held([P, S], F32, f"slot_quot{t}", tag)[:])
             divide(slot_quot[t], absorbed[0][:, t, :], squares[0][:, t, :])
 
-        for a in range(2):
-            round_ws(1, a, 0, 2)
-            round_ws(1, a, 2, 2)
-            quantize_ws(1, a, 0, 2)
-            quantize_ws(1, a, 2, 2)
-            if a == 0:
-                sort_wp(0)
-                sort_wp(1)
-            divide_slot("ws_raw11" if a else "wp_raw")
+        round_ws(1, 0, 0, PACK)
+        sort_wp()
+        quantize_ws(1, 0, 0, PACK)
+        divide_slot("wp_raw")
+        round_ws(1, 1, 0, 2)
+        round_ws(1, 1, 2, 2)
+        quantize_ws(1, 1, 0, 2)
+        quantize_ws(1, 1, 2, 2)
+        divide_slot("ws_raw11")
         for t in range(PACK):
             scattering(1, t)
         gather(2)
         last_two = held([P, 2, S], F32, "last_two", "window2")
-        for t in (2, 3):
-            slot_quot.append(last_two[:, t - 2, :])
-            divide(slot_quot[t], absorbed[0][:, t, :], squares[0][:, t, :])
+        slot_quot.extend([last_two[:, 0, :], last_two[:, 1, :]])
+        divide(last_two[:], pair(absorbed[0], 1), pair(squares[0], 1))
         diffs0 = held([P, PACK, S], F32, "diffs_all")
         for t in range(PACK):
             panel = bank(t, [P, S])
             panel_pass(panel[:], 0, t, everything)
             nc.vector.tensor_tensor(out=diffs0[:, t, :], in0=panel[:], in1=slot_quot[t], op=ALU.subtract)
 
-        all_quot = held([P, 4, PACK, QUARTER], F32, "all_quot", None)
-        quot = [all_quot[:, q] for q in range(4)]
         for q in range(4 + 1):
             if q < 4:
                 inverse_root(quot[q][:], squares[1][:, :, cols_of(q)])
@@ -371,30 +370,25 @@ def tile_list_tint_adjustment_kernel(
             if q in (2, 4):
                 distance(0, (q - 2) * QUARTER, diffs0[:, :, (q - 2) * QUARTER:q * QUARTER])
         for b in range(2):
-            for x in range(2):
-                if (b, x) not in wc_rounded:
-                    round_wc(b, x, nc.vector.tensor_copy)
-            for x in range(2):
-                quantize_wc(b, x)
-        quotient = held([P, PACK, S], F32, "quotient", "window1")
+            round_wc(b)
+        quantize_wc(0, "window1")
+        quantize_wc(1, None)
+        quotient = held([P, PACK, S], F32, "quotient", "wc_rounded0")
         for q in range(4):
             divide(quotient[:, :, cols_of(q)], absorbed[1][:, :, cols_of(q)], quot[q][:])
-            if q == 3:
-                quantize_d(1, QUARTER, QUARTER)
             panel = bank(PACK + q, [P, PACK, QUARTER])
             for t in range(PACK):
                 panel_pass(panel[:, t, :], 1, t, cols_of(q))
             diffs[q] = held([P, PACK, QUARTER], F32, f"diffs{q}")
             nc.vector.tensor_tensor(out=diffs[q][:], in0=panel[:], in1=quotient[:, :, cols_of(q)], op=ALU.subtract)
             if q < 2:
-                quantize_d(0, q * HALF, HALF, f"wc_rounded1{q}")
+                quantize_d(0, q * HALF, HALF, "wc_rounded1" if q == 0 else "quot0")
             distance(1, q * QUARTER, diffs[q][:])
-            if q == 2:
-                quantize_d(1, 0, QUARTER)
-                second_stage(0, 0, PACK, 0, nc.scalar.copy)
-        second_stage(1, 0, PACK, 1, nc.scalar.copy)
+            if q > 1:
+                quantize_d(1, (q - 2) * QUARTER, QUARTER)
+                second_stage(q - 2, 0, PACK, q - 2, nc.scalar.copy)
         quantize_d(1, 2 * QUARTER, QUARTER)
         quantize_d(1, 3 * QUARTER, QUARTER)
         second_stage(2, 0, PACK, 2, nc.vector.tensor_copy)
         second_stage(3, 0, 2, 3, nc.vector.tensor_copy)
-        second_stage(3, 2, 2, 6, nc.scalar.copy)
+        second_stage(3, 2, 2, 4, nc.scalar.copy)

@@ -23,6 +23,7 @@ BANK = 512
 HALF = S // 2
 ROW0 = 4
 LATE0 = 8
+SHARE = 384
 QUARTER = S // 4
 
 
@@ -221,11 +222,10 @@ def tile_list_tint_adjustment_kernel(
                 ws_codes[b, a, t0 + s] = codes[:, s * P:(s + 1) * P]
                 ws_plane[b, a, t0 + s] = plane[:, s * P:(s + 1) * P]
 
-        def round_wc(b):
-            wc_rounded[b] = held([P, PACK * N], BF16, f"wc_rounded{b}")
+        def round_wc(b, n0):
             nc.vector.tensor_copy(
-                out=wc_rounded[b][:].rearrange("p (c i t) -> p c t i", t=PACK, i=4),
-                in_=wc_raw[b][:].rearrange("p t (c i) -> p c t i", i=4),
+                out=wc_rounded[b][:, n0 * PACK:].rearrange("p (c i t) -> p c t i", t=PACK, i=4),
+                in_=wc_raw[b][:, :, n0:].rearrange("p t (c i) -> p c t i", i=4),
             )
 
         def quantize_wc(b, tag):
@@ -367,13 +367,21 @@ def tile_list_tint_adjustment_kernel(
                 inverse_root(quot[q][:], squares[1][:, :, cols_of(q)])
             if q > 0:
                 square_root(quot[q - 1][:])
-            if q in (2, 4):
-                distance(0, (q - 2) * QUARTER, diffs0[:, :, (q - 2) * QUARTER:q * QUARTER])
+            if q == 2:
+                for j0 in (0, HALF):
+                    distance(0, j0, diffs0[:, :, j0:j0 + HALF])
         for b in range(2):
-            round_wc(b)
+            wc_rounded[b] = held([P, PACK * N], BF16, f"wc_rounded{b}", None if b else "squares0")
+        nc.gpsimd.tensor_scalar(
+            out=wc_rounded[0][:, 0:PACK * SHARE].rearrange("p (c t) -> p c t", t=PACK),
+            in0=wc_raw[0][:, :, 0:SHARE].rearrange("p t c -> p c t"),
+            scalar1=1.0, scalar2=0.0, op0=ALU.mult, op1=ALU.add,
+        )
+        round_wc(0, SHARE)
+        round_wc(1, 0)
         quantize_wc(0, "window1")
         quantize_wc(1, None)
-        quotient = held([P, PACK, S], F32, "quotient", "wc_rounded0")
+        quotient = held([P, PACK, S], F32, "quotient", "squares0")
         for q in range(4):
             divide(quotient[:, :, cols_of(q)], absorbed[1][:, :, cols_of(q)], quot[q][:])
             panel = bank(PACK + q, [P, PACK, QUARTER])

@@ -1,6 +1,7 @@
 from contextlib import ExitStack
 
 import concourse.mybir as mybir
+from concourse.masks import make_identity
 
 K, K2, H, N, T, S = 1024, 512, 1024, 512, 2048, 512
 FLOPS = 2 * S * (2 * K * H + K2 * H + H * N)
@@ -23,7 +24,6 @@ BANK = 512
 HALF = S // 2
 ROW0 = 4
 LATE0 = 8
-SHARE = 384
 QUARTER = S // 4
 
 
@@ -50,17 +50,17 @@ def tile_list_tint_adjustment_kernel(
         table_lists = [lists, lists, lists2]
 
         tab_rows = [held([P, T], U8, f"tab_rows{x}") for x in range(3)]
-        wa_rows = held([P, 2 * H], U8, "wa_rows")
         base_rows = held([P, P], F32, "base_rows")
-        early_planes = held([P, 2 * S + 2 * H], U8, "early_planes")
-        for cleared in (tab_rows[0], tab_rows[1], wa_rows):
+        early_planes = held([P, 2 * S], U8, "early_planes")
+        wa_planes = held([P, 2 * H], U8, "wa_planes")
+        for cleared in (tab_rows[0], tab_rows[1], wa_planes):
             nc.vector.memset(cleared[:].bitcast(I32), 0)
         nc.vector.memset(base_rows[:], 0.0)
-        for cleared in (early_planes, tab_rows[2]):
+        for cleared in (tab_rows[2], early_planes):
             nc.vector.memset(cleared[:].bitcast(I32), 0)
 
         windows = [held([P, T], I32, f"window{x}") for x in range(3)]
-        wa_raw = held([P, 2, H // 2], I32, "wa_raw")
+        wa_raw = [held([P, 2, KP // 2], I32, f"wa_raw{b}") for b in range(2)]
         wp_raw = held([P, H], I32, "wp_raw")
         ws_raw = {(b, a): held([P, PACK, KP], F32, f"ws_raw{b}{a}") for b in range(2) for a in range(2)}
         wc_raw = {}
@@ -75,6 +75,10 @@ def tile_list_tint_adjustment_kernel(
         def load_ws(b, a):
             rows = ws[a * KP:(a + 1) * KP, b * KP:(b + 1) * KP]
             nc.sync.dma_start(out=ws_raw[b, a][:], in_=rows.rearrange("(p j) c -> p j c", j=PACK))
+
+        def load_wa(b):
+            columns = wa_words.bitcast(I32)[:, :, b * (KP // 2):(b + 1) * (KP // 2)]
+            nc.sync.dma_start(out=wa_raw[b][:], in_=columns.rearrange("a p c -> p a c"))
 
         def move_rows(queue, planes, rows, first):
             for r in range(4):
@@ -91,43 +95,27 @@ def tile_list_tint_adjustment_kernel(
         load_window(0, 0, T // 4)
         load_rows(nc.sync, 0)
         load_rows(nc.sync, 1)
-        nc.sync.dma_start(
-            out=wa_rows[ROW0:P:8, :].bitcast(I32).rearrange("q (a c) -> q a c", a=2),
-            in_=wa_scales.bitcast(I32).rearrange("a q c -> q a c"),
-        )
         load_window(0, T // 4, T - T // 4)
+        for r in range(4):
+            nc.sync.dma_start(
+                out=wa_planes[r:P:32, :].bitcast(I32).rearrange("d (a c) -> d a c", a=2),
+                in_=wa_scales[:, r:16:4, :].bitcast(I32).rearrange("a d c -> d a c"),
+            )
         nc.sync.dma_start(out=base_rows[0:P:16, :], in_=base.rearrange("(b d x) -> d b x", b=2, d=4))
-        load_window(1, 0, T)
-        nc.sync.dma_start(out=wa_raw[:], in_=wa_words.bitcast(I32).rearrange("a p c -> p a c"))
         load_rows(nc.sync, 2)
+        load_window(1, 0, T)
+        load_wa(0)
 
         picked_rows = held([P, 2 * S], U8, "picked_rows")
         for x in range(2):
             nc.vector.tensor_copy(out=picked_rows[:, x * S:(x + 1) * S], in_=tab_rows[x][:].indirect(lists[:]))
-        early_rows = held([P, 2 * S + 2 * H], U8, "early_rows")
-        sort_rows(early_rows[:, 2 * S:], wa_rows[:])
-        nc.vector.tensor_copy(out=early_rows[:, 0:2 * S].bitcast(I32), in_=picked_rows[:].bitcast(I32))
-        move_rows(nc.sync, early_planes, early_rows, 0)
-        base_sorted = held([P, P], F32, "base_sorted")
-        nc.vector.tensor_copy(
-            out=base_sorted[:].rearrange("p (t h i) -> p t h i", t=PACK, i=4),
-            in_=base_rows[:].rearrange("p (h t i) -> p t h i", t=PACK, i=4),
-        )
-        base_cols = held([P, P], F32, "base_cols")
-        nc.vector.transpose(out=base_cols[:], in_=base_sorted[:])
-        inv_root = held([P, 2 * PACK], F32, "inv_root")
-        nc.scalar.activation(out=inv_root[:], in_=base_cols[:, 0:P:16], func=ACT.Abs_reciprocal_sqrt)
-        inv_base = held([P, 2 * PACK], F32, "inv_base")
-        nc.scalar.activation(out=inv_base[:], in_=inv_root[:], func=ACT.Square)
+        move_rows(nc.sync, early_planes, picked_rows, 0)
+        load_wa(1)
         load_ws(0, 0)
         load_ws(0, 1)
 
         def picked_plane(x, cols):
             return early_planes[:, x * S + cols.start:x * S + cols.stop] if x < 2 else late_planes[LATE0:P, cols]
-
-        def wa_plane(b, a, t):
-            c0 = 2 * S + a * H + b * KP + t * P
-            return early_planes[:, c0:c0 + P]
 
         def wp_plane(b, t):
             c0 = S + b * KP + t * P
@@ -138,16 +126,20 @@ def tile_list_tint_adjustment_kernel(
         def gather(x):
             nc.vector.tensor_copy(out=picked[x][:], in_=windows[x][:].bitcast(U32).indirect(table_lists[x][:]))
 
+        identity = held([P, P], F32, "identity", "tab_rows1")
+        make_identity(nc, identity[:])
         gather(0)
+        base_sorted = held([P, P], F32, "base_sorted")
+        nc.vector.tensor_copy(
+            out=base_sorted[:].rearrange("p (t h i) -> p t h i", t=PACK, i=4),
+            in_=base_rows[:].rearrange("p (h t i) -> p t h i", t=PACK, i=4),
+        )
+        base_cols = held([P, P], F32, "base_cols")
+        nc.vector.transpose(out=base_cols[:], in_=base_sorted[:])
+        inv_root = held([P, PACK], F32, "inv_root")
+        nc.scalar.activation(out=inv_root[:], in_=base_cols[:, 0:P:32], func=ACT.Abs_reciprocal_sqrt)
 
         wa_codes, wp_codes = {}, {}
-
-        def sort_wa(b):
-            wa_codes[b] = held([P, 2, KP // 2], I32, f"wa_codes{b}")
-            nc.vector.tensor_copy(
-                out=wa_codes[b][:].rearrange("p a (t h w) -> p a t h w", t=PACK, w=2),
-                in_=wa_raw[:, :, b * (KP // 2):(b + 1) * (KP // 2)].rearrange("p a (h t w) -> p a t h w", t=PACK, w=2),
-            )
 
         def sort_wp():
             both = held([P, H], I32, "wp_codes")
@@ -158,40 +150,43 @@ def tile_list_tint_adjustment_kernel(
             for b in range(2):
                 wp_codes[b] = both[:, b * KP:(b + 1) * KP]
 
-        absorbed = [held([P, PACK, S], F32, f"absorbed{b}") for b in range(2)]
+        absorbed = [held([P, 4, KP], F32, f"absorbed{b}") for b in range(2)]
         everything = slice(0, S)
 
-        def absorb_pass(absorb, b, a, t):
-            nc.tensor.matmul_mx(
-                out=absorb[:],
-                lhsT=wa_codes[b][:, a, t * (P // 2):(t + 1) * (P // 2)].bitcast(U8).bitcast(E2M1),
-                lhsT_scale=wa_plane(b, a, t),
-                rhs=picked[a][:].bitcast(E4M3), rhs_scale=picked_plane(a, everything),
-                start=(a == 0), stop=(a == 1),
-            )
+        def cols_of(q):
+            return slice(q * QUARTER, (q + 1) * QUARTER)
 
         def absorption(b):
-            banks = [bank(PACK * b + t, [P, S]) for t in range(PACK)]
-            for t in range(PACK):
-                absorb_pass(banks[t], b, 0, t)
-                absorb_pass(banks[t], b, 1, t)
-                col = 2 * t + b
-                nc.scalar.activation(out=absorbed[b][:, t, :], in_=banks[t][:], func=ACT.Abs, scale=inv_base[:, col:col + 1])
+            for c in range(4):
+                absorb = bank(PACK * b + c, [P, KP])
+                for a in range(2):
+                    nc.tensor.matmul_mx(
+                        out=absorb[:],
+                        lhsT=picked[a][:, cols_of(c)].bitcast(E4M3), lhsT_scale=picked_plane(a, cols_of(c)),
+                        rhs=wa_raw[b][:, a, :].bitcast(U8).bitcast(E2M1),
+                        rhs_scale=wa_planes[:, a * H + b * KP:a * H + (b + 1) * KP],
+                        start=(a == 0), stop=(a == 1),
+                    )
+                nc.scalar.activation(
+                    out=absorbed[b][:, c, :].rearrange("p (t h i) -> p h t i", t=PACK, i=4),
+                    in_=absorb[:].rearrange("p (h t i) -> p h t i", t=PACK, i=4), func=ACT.Abs,
+                )
+
+        def turn(target, b, c, t):
+            nc.tensor.transpose(target, absorbed[b][:, c, t * P:(t + 1) * P], identity[:])
 
         gather(1)
         unread = bank(7, [P, S])
         for x in range(4):
             nc.tensor.matmul_mx(
-                out=unread[:], lhsT=windows[0][:, 0:P].bitcast(E4M3), lhsT_scale=early_rows[:, 2 * S:2 * S + P],
-                rhs=windows[0][:, 0:S].bitcast(E4M3), rhs_scale=early_rows[:, 0:S], start=True, stop=True,
+                out=unread[:], lhsT=picked[0][:, 0:P].bitcast(E4M3), lhsT_scale=picked_rows[:, 0:P],
+                rhs=picked[0][:].bitcast(E4M3), rhs_scale=picked_rows[:, 0:S], start=True, stop=True,
             )
-        sort_wa(0)
         absorption(0)
-        sort_wa(1)
-        picked_rows2 = held([P, S], U8, "picked_rows2", "wa_raw")
+        picked_rows2 = held([P, S], U8, "picked_rows2", "window1")
         nc.vector.tensor_copy(out=picked_rows2[:], in_=tab_rows[2][:].indirect(lists2[:]))
         wp_rows = held([P, H], U8, "wp_rows", "tab_rows2")
-        late_planes = held([P, S + H], U8, "late_planes", "early_rows")
+        late_planes = held([P, S + H], U8, "late_planes", "picked_rows")
         for cleared in (wp_rows, late_planes):
             nc.vector.memset(cleared[:].bitcast(I32), 0)
         load_ws(1, 0)
@@ -222,17 +217,14 @@ def tile_list_tint_adjustment_kernel(
                 ws_codes[b, a, t0 + s] = codes[:, s * P:(s + 1) * P]
                 ws_plane[b, a, t0 + s] = plane[:, s * P:(s + 1) * P]
 
-        def round_wc(b, n0):
-            nc.vector.tensor_copy(
-                out=wc_rounded[b][:, n0 * PACK:].rearrange("p (c i t) -> p c t i", t=PACK, i=4),
-                in_=wc_raw[b][:, :, n0:].rearrange("p t (c i) -> p c t i", i=4),
-            )
-
-        def quantize_wc(b, tag):
-            codes, plane = quantize(wc_rounded[b], N, f"wc{b}", tag)
-            for n in range(PACK):
-                wc_codes[b, n] = codes[:, n * P:(n + 1) * P]
-                wc_plane[b, n] = plane[:, n * P:(n + 1) * P]
+        def quantize_wc(b, n0, n1, codes=None):
+            if codes is None:
+                codes = held([P, n1 - n0], U32, f"wc{b}_codes")[:]
+            plane = held([P, n1 - n0], U8, f"wc{b}_plane")
+            nc.vector.quantize_mx(out=codes.bitcast(E4M3), scales=plane[:], in_=wc_rounded[b][:, n0 * PACK:n1 * PACK])
+            for n in range(n0 // P, n1 // P):
+                wc_codes[b, n] = codes[:, n * P - n0:(n + 1) * P - n0]
+                wc_plane[b, n] = plane[:, n * P - n0:(n + 1) * P - n0]
 
         squares = [held([P, PACK, S], F32, f"squares{b}") for b in range(2)]
 
@@ -245,21 +237,19 @@ def tile_list_tint_adjustment_kernel(
                     rhs=picked[a][:].bitcast(E4M3), rhs_scale=picked_plane(a, everything),
                     start=(a == 0), stop=(a == 1),
                 )
-            col = 2 * t + b
-            nc.scalar.activation(out=squares[b][:, t, :], in_=scat[:], func=ACT.Square, scale=inv_root[:, col:col + 1])
+            scale = inv_root[:, t:t + 1] if b == 0 else 1.0
+            nc.scalar.activation(out=squares[b][:, t, :], in_=scat[:], func=ACT.Square, scale=scale)
 
 
-        def cols_of(q):
-            return slice(q * QUARTER, (q + 1) * QUARTER)
+        def inverse_root(b, t):
+            nc.scalar.activation(out=squares[b][:, t, :], in_=squares[b][:, t, :], func=ACT.Abs_reciprocal_sqrt, bias=1.0)
 
-        def pair(tile, x):
-            return tile[:, 2 * x:2 * x + 2, :]
+        def inverse_root_half(t, h):
+            part = squares[1][:, t, h * HALF:(h + 1) * HALF]
+            nc.scalar.activation(out=part, in_=part, func=ACT.Abs_reciprocal_sqrt, bias=base_cols[:, 32 * t + 16:32 * t + 17])
 
-        def inverse_root(target, source):
-            nc.scalar.activation(out=target, in_=source, func=ACT.Abs_reciprocal_sqrt, bias=1.0)
-
-        def square_root(target):
-            nc.scalar.activation(out=target, in_=target, func=ACT.Square)
+        def square_slot(t):
+            nc.scalar.activation(out=squares[0][:, t, :], in_=squares[0][:, t, :], func=ACT.Square, scale=inv_root[:, t:t + 1])
 
         def divide(target, numerator, inverse):
             nc.vector.tensor_tensor(out=target, in0=numerator, in1=inverse, op=ALU.mult)
@@ -274,15 +264,18 @@ def tile_list_tint_adjustment_kernel(
                 start=True, stop=True,
             )
 
-        def distance(b, j0, source):
-            dist[b, j0] = held([P, source.shape[2] * PACK], BF16, f"dist{b}{j0}")
+        def distance(b, j0, source, target=None):
+            dist[b, j0] = held([P, PACK * QUARTER], BF16, f"dist{b}{j0}")[:] if target is None else target
             nc.scalar.activation(
                 out=dist[b, j0][:].rearrange("p (c i t) -> p c t i", t=PACK, i=4),
                 in_=source.rearrange("p t (c i) -> p c t i", i=4), func=ACT.Abs,
             )
 
-        def quantize_d(b, j0, width, tag=None):
-            codes, plane = quantize(dist[b, j0], width, f"d{b}{j0}", tag)
+        def quantize_d(b, j0, width, codes=None):
+            if codes is None:
+                codes = held([P, width], U32, f"d{b}{j0}_codes")[:]
+            plane = held([P, width], U8, f"d{b}{j0}_plane")
+            nc.vector.quantize_mx(out=codes.bitcast(E4M3), scales=plane[:], in_=dist[b, j0][:])
             for c0 in range(0, width, QUARTER):
                 d_codes[b, j0 + c0] = codes[:, c0:c0 + QUARTER]
                 d_plane[b, j0 + c0] = plane[:, c0:c0 + QUARTER]
@@ -312,15 +305,17 @@ def tile_list_tint_adjustment_kernel(
         round_ws(0, 1, 0, 1)
         round_ws(0, 1, 1, 1)
         quantize_ws(0, 1, 0, 1)
-        round_ws(0, 1, 2, 2)
+        round_ws(0, 1, 2, 1)
         quantize_ws(0, 1, 1, 1)
-        quantize_ws(0, 1, 2, 2)
+        round_ws(0, 1, 3, 1)
+        quantize_ws(0, 1, 2, 1)
+        quantize_ws(0, 1, 3, 1)
         for t in range(PACK):
             scattering(0, t)
             if t > 1:
-                square_root(squares[0][:, t - 2, :])
+                square_slot(t - 2)
             if t > 0:
-                inverse_root(squares[0][:, t - 1, :], squares[0][:, t - 1, :])
+                inverse_root(0, t - 1)
         sort_rows(late_rows[:, S:], wp_rows[:])
         move_rows(nc.sync, late_planes, late_rows, LATE0)
         for b in range(2):
@@ -329,74 +324,106 @@ def tile_list_tint_adjustment_kernel(
             for t in range(PACK):
                 nc.sync.dma_start(out=wc_raw[b][:, t, :], in_=rows[t])
 
-        quot = [held([P, PACK, QUARTER], F32, f"quot{q}") for q in range(4)]
-        inverse_root(squares[0][:, PACK - 1, :], squares[0][:, PACK - 1, :])
+        inverse_root(0, PACK - 1)
         for t in (PACK - 2, PACK - 1):
-            square_root(squares[0][:, t, :])
+            square_slot(t)
         absorption(1)
         slot_quot = []
 
-        def divide_slot(tag):
+        def divide_slot(target):
             t = len(slot_quot)
-            slot_quot.append(held([P, S], F32, f"slot_quot{t}", tag)[:])
-            divide(slot_quot[t], absorbed[0][:, t, :], squares[0][:, t, :])
+            numerator = bank(t, [P, S])
+            for c in range(4):
+                turn(numerator[:, cols_of(c)], 0, c, t)
+            slot_quot.append(target)
+            divide(target, numerator[:], squares[0][:, t, :])
 
         round_ws(1, 0, 0, PACK)
         sort_wp()
         quantize_ws(1, 0, 0, PACK)
-        divide_slot("wp_raw")
+        divide_slot(held([P, S], F32, "slot_quot0", "wp_raw")[:])
         round_ws(1, 1, 0, 2)
         round_ws(1, 1, 2, 2)
         quantize_ws(1, 1, 0, 2)
         quantize_ws(1, 1, 2, 2)
-        divide_slot("ws_raw11")
+        divide_slot(held([P, S], F32, "slot_quot1", "ws_raw11")[:])
         for t in range(PACK):
             scattering(1, t)
         gather(2)
-        last_two = held([P, 2, S], F32, "last_two", "window2")
-        slot_quot.extend([last_two[:, 0, :], last_two[:, 1, :]])
-        divide(last_two[:], pair(absorbed[0], 1), pair(squares[0], 1))
+        behind_gather = held([P, T], F32, "behind_gather", "window2")
+        divide_slot(behind_gather[:, 0:S])
+        divide_slot(behind_gather[:, S:2 * S])
         diffs0 = held([P, PACK, S], F32, "diffs_all")
         for t in range(PACK):
             panel = bank(t, [P, S])
             panel_pass(panel[:], 0, t, everything)
             nc.vector.tensor_tensor(out=diffs0[:, t, :], in0=panel[:], in1=slot_quot[t], op=ALU.subtract)
 
-        for q in range(4 + 1):
-            if q < 4:
-                inverse_root(quot[q][:], squares[1][:, :, cols_of(q)])
-            if q > 0:
-                square_root(quot[q - 1][:])
-            if q == 2:
-                for j0 in (0, HALF):
-                    distance(0, j0, diffs0[:, :, j0:j0 + HALF])
+        def round_wc(b, n0, n1):
+            nc.gpsimd.tensor_scalar(
+                out=wc_rounded[b][:, n0 * PACK:n1 * PACK].rearrange("p (c t) -> p c t", t=PACK),
+                in0=wc_raw[b][:, :, n0:n1].rearrange("p t c -> p c t"),
+                scalar1=1.0, scalar2=0.0, op0=ALU.mult, op1=ALU.add,
+            )
+
+        wc_rounded[0] = behind_gather[:, 2 * S:].bitcast(BF16)
+        wc_rounded[1] = held([P, PACK * N], BF16, "wc_rounded1")[:]
         for b in range(2):
-            wc_rounded[b] = held([P, PACK * N], BF16, f"wc_rounded{b}", None if b else "squares0")
-        nc.gpsimd.tensor_scalar(
-            out=wc_rounded[0][:, 0:PACK * SHARE].rearrange("p (c t) -> p c t", t=PACK),
-            in0=wc_raw[0][:, :, 0:SHARE].rearrange("p t c -> p c t"),
-            scalar1=1.0, scalar2=0.0, op0=ALU.mult, op1=ALU.add,
-        )
-        round_wc(0, SHARE)
-        round_wc(1, 0)
-        quantize_wc(0, "window1")
-        quantize_wc(1, None)
-        quotient = held([P, PACK, S], F32, "quotient", "squares0")
-        for q in range(4):
-            divide(quotient[:, :, cols_of(q)], absorbed[1][:, :, cols_of(q)], quot[q][:])
+            round_wc(b, 0, N)
+        quot = [held([P, PACK, QUARTER], F32, f"quot{q}") for q in range(4)]
+
+        def square_quarter(q):
+            nc.scalar.activation(out=quot[q][:], in_=squares[1][:, :, cols_of(q)], func=ACT.Square)
+
+        for t in range(PACK):
+            inverse_root_half(t, 0)
+        inverse_root_half(0, 1)
+        square_quarter(0)
+        square_quarter(1)
+        for t in range(1, PACK):
+            inverse_root_half(t, 1)
+        square_quarter(2)
+        square_quarter(3)
+        rounded0 = held([P, PACK * S], BF16, "rounded0", "squares1")
+        distance(0, 0, diffs0[:, :, 0:HALF], rounded0[:, 0:PACK * HALF])
+        products = {}
+
+        def divide_quarter(q, tag=None):
+            numerator = bank(q, [P, PACK, QUARTER])
+            for t in range(PACK):
+                turn(numerator[:, t, :], 1, q, t)
+            products[q] = held([P, PACK, QUARTER], F32, f"product{q}", tag)
+            divide(products[q][:], numerator[:], quot[q][:])
+
+        def subtract_quarter(q, tag=None):
             panel = bank(PACK + q, [P, PACK, QUARTER])
             for t in range(PACK):
                 panel_pass(panel[:, t, :], 1, t, cols_of(q))
-            diffs[q] = held([P, PACK, QUARTER], F32, f"diffs{q}")
-            nc.vector.tensor_tensor(out=diffs[q][:], in0=panel[:], in1=quotient[:, :, cols_of(q)], op=ALU.subtract)
-            if q < 2:
-                quantize_d(0, q * HALF, HALF, "wc_rounded1" if q == 0 else "quot0")
+            diffs[q] = held([P, PACK, QUARTER], F32, f"diffs{q}", tag)
+            nc.vector.tensor_tensor(out=diffs[q][:], in0=panel[:], in1=products[q][:], op=ALU.subtract)
             distance(1, q * QUARTER, diffs[q][:])
-            if q > 1:
-                quantize_d(1, (q - 2) * QUARTER, QUARTER)
-                second_stage(q - 2, 0, PACK, q - 2, nc.scalar.copy)
+
+        divide_quarter(0)
+        divide_quarter(1)
+        subtract_quarter(0)
+        subtract_quarter(1)
+        divide_quarter(2)
+        divide_quarter(3)
+        distance(0, HALF, diffs0[:, :, HALF:S], rounded0[:, PACK * HALF:])
+        codes = held([P, N + HALF], U32, "late_codes", "window1")
+        quantize_wc(0, 0, N, codes[:, 0:N])
+        quantize_d(0, 0, HALF, codes[:, N:])
+        quantize_wc(1, 0, N)
+        subtract_quarter(2, "wc_rounded1")
+        first_half = held([P, HALF], U32, "d1_codes", "window2")
+        quantize_d(1, 0, QUARTER, first_half[:, 0:QUARTER])
+        quantize_d(1, QUARTER, QUARTER, first_half[:, QUARTER:])
+        subtract_quarter(3, "dist1128")
+        quantize_d(0, HALF, HALF, held([P, HALF], U32, "d0h_codes", "product2")[:])
         quantize_d(1, 2 * QUARTER, QUARTER)
+        second_stage(0, 0, PACK, 0, nc.vector.tensor_copy)
         quantize_d(1, 3 * QUARTER, QUARTER)
-        second_stage(2, 0, PACK, 2, nc.vector.tensor_copy)
+        second_stage(1, 0, PACK, 1, nc.vector.tensor_copy)
+        second_stage(2, 0, PACK, 2, nc.scalar.copy)
         second_stage(3, 0, 2, 3, nc.vector.tensor_copy)
         second_stage(3, 2, 2, 4, nc.scalar.copy)

@@ -24,6 +24,7 @@ BANK = 512
 HALF = S // 2
 ROW0 = 4
 LATE0 = 8
+SHARE = 384
 QUARTER = S // 4
 
 
@@ -217,11 +218,11 @@ def tile_list_tint_adjustment_kernel(
                 ws_codes[b, a, t0 + s] = codes[:, s * P:(s + 1) * P]
                 ws_plane[b, a, t0 + s] = plane[:, s * P:(s + 1) * P]
 
-        def quantize_wc(b, n0, n1, codes=None):
+        def quantize_wc(b, n0, n1, rounded, codes=None):
             if codes is None:
-                codes = held([P, n1 - n0], U32, f"wc{b}_codes")[:]
-            plane = held([P, n1 - n0], U8, f"wc{b}_plane")
-            nc.vector.quantize_mx(out=codes.bitcast(E4M3), scales=plane[:], in_=wc_rounded[b][:, n0 * PACK:n1 * PACK])
+                codes = held([P, n1 - n0], U32, f"wc{b}{n0}_codes")[:]
+            plane = held([P, n1 - n0], U8, f"wc{b}{n0}_plane")
+            nc.vector.quantize_mx(out=codes.bitcast(E4M3), scales=plane[:], in_=rounded)
             for n in range(n0 // P, n1 // P):
                 wc_codes[b, n] = codes[:, n * P - n0:(n + 1) * P - n0]
                 wc_plane[b, n] = plane[:, n * P - n0:(n + 1) * P - n0]
@@ -367,9 +368,9 @@ def tile_list_tint_adjustment_kernel(
             )
 
         wc_rounded[0] = behind_gather[:, 2 * S:].bitcast(BF16)
-        wc_rounded[1] = held([P, PACK * N], BF16, "wc_rounded1")[:]
-        for b in range(2):
-            round_wc(b, 0, N)
+        wc_rounded[1] = held([P, PACK * SHARE], BF16, "wc_rounded1")[:]
+        round_wc(0, 0, N)
+        round_wc(1, 0, SHARE)
         quot = [held([P, PACK, QUARTER], F32, f"quot{q}") for q in range(4)]
 
         def square_quarter(q):
@@ -387,6 +388,7 @@ def tile_list_tint_adjustment_kernel(
         rounded0 = held([P, PACK * S], BF16, "rounded0", "squares1")
         distance(0, 0, diffs0[:, :, 0:HALF], rounded0[:, 0:PACK * HALF])
         products = {}
+        diffs1 = held([P, PACK, HALF], F32, "diffs1")
 
         def divide_quarter(q, tag=None):
             numerator = bank(q, [P, PACK, QUARTER])
@@ -399,9 +401,12 @@ def tile_list_tint_adjustment_kernel(
             panel = bank(PACK + q, [P, PACK, QUARTER])
             for t in range(PACK):
                 panel_pass(panel[:, t, :], 1, t, cols_of(q))
-            diffs[q] = held([P, PACK, QUARTER], F32, f"diffs{q}", tag)
-            nc.vector.tensor_tensor(out=diffs[q][:], in0=panel[:], in1=products[q][:], op=ALU.subtract)
-            distance(1, q * QUARTER, diffs[q][:])
+            target = diffs1[:, :, cols_of(q)] if q < 2 else held([P, PACK, QUARTER], F32, f"diffs{q}", tag)[:]
+            nc.vector.tensor_tensor(out=target, in0=panel[:], in1=products[q][:], op=ALU.subtract)
+            if q == 1:
+                distance(1, 0, diffs1[:], held([P, PACK * HALF], BF16, "rounded1")[:])
+            if q > 1:
+                distance(1, q * QUARTER, target)
 
         divide_quarter(0)
         divide_quarter(1)
@@ -410,15 +415,21 @@ def tile_list_tint_adjustment_kernel(
         divide_quarter(2)
         divide_quarter(3)
         distance(0, HALF, diffs0[:, :, HALF:S], rounded0[:, PACK * HALF:])
+        rest = held([P, PACK * (N - SHARE)], BF16, "wc_rest", "quot3")
+        nc.vector.tensor_copy(
+            out=rest[:].rearrange("p (c i t) -> p c t i", t=PACK, i=4),
+            in_=wc_raw[1][:, :, SHARE:].rearrange("p t (c i) -> p c t i", i=4),
+        )
+        subtract_quarter(2)
         codes = held([P, N + HALF], U32, "late_codes", "window1")
-        quantize_wc(0, 0, N, codes[:, 0:N])
+        quantize_wc(0, 0, N, wc_rounded[0], codes[:, 0:N])
         quantize_d(0, 0, HALF, codes[:, N:])
-        quantize_wc(1, 0, N)
-        subtract_quarter(2, "wc_rounded1")
-        first_half = held([P, HALF], U32, "d1_codes", "window2")
-        quantize_d(1, 0, QUARTER, first_half[:, 0:QUARTER])
-        quantize_d(1, QUARTER, QUARTER, first_half[:, QUARTER:])
-        subtract_quarter(3, "dist1128")
+        quantize_wc(1, SHARE, N, rest[:])
+        shared = held([P, SHARE], U32, "wc10_codes", "quot3")
+        quantize_wc(1, 0, HALF, wc_rounded[1][:, 0:PACK * HALF], shared[:, 0:HALF])
+        quantize_wc(1, HALF, SHARE, wc_rounded[1][:, PACK * HALF:], shared[:, HALF:])
+        quantize_d(1, 0, HALF, held([P, HALF], U32, "d1_codes", "window2")[:])
+        subtract_quarter(3, "rounded1")
         quantize_d(0, HALF, HALF, held([P, HALF], U32, "d0h_codes", "product2")[:])
         quantize_d(1, 2 * QUARTER, QUARTER)
         second_stage(0, 0, PACK, 0, nc.vector.tensor_copy)

@@ -24,7 +24,9 @@ BANK = 512
 HALF = S // 2
 ROW0 = 4
 LATE0 = 8
-SHARE = 384
+VSQ = 1
+FIRST_PIECE = T // 4
+SECOND_PIECE = 5 * T // 8
 QUARTER = S // 4
 
 
@@ -43,77 +45,80 @@ def tile_list_tint_adjustment_kernel(
         def bank(number, shape):
             return psum.tile(shape, F32, name="bank%d" % number, tag="bank%d" % number)
 
+        def cols_of(q):
+            return slice(q * QUARTER, (q + 1) * QUARTER)
+
+        def half(h):
+            return slice(h * HALF, (h + 1) * HALF)
+
+        everything = slice(0, S)
         lists = keep.tile([P, S // 16], U16, name="lists")
         lists2 = keep.tile([P, S // 16], U16, name="lists2")
 
-        table_words = [tab_words[0], tab_words[1], tab2_words[0]]
-        table_scales = [tab_scales[0], tab_scales[1], tab2_scales[0]]
-        table_lists = [lists, lists, lists2]
-
-        tab_rows = [held([P, T], U8, f"tab_rows{x}") for x in range(3)]
+        tab_rows = held([P, T], U8, "tab_rows")
+        tab2_rows = held([P, T], U8, "tab2_rows")
+        wp_rows = held([P, H], U8, "wp_rows")
         base_rows = held([P, P], F32, "base_rows")
         early_planes = held([P, 2 * S], U8, "early_planes")
         wa_planes = held([P, 2 * H], U8, "wa_planes")
-        for cleared in (tab_rows[0], tab_rows[1], wa_planes):
+        late_planes = held([P, S + H], U8, "late_planes")
+        for cleared in (tab_rows, wa_planes):
             nc.vector.memset(cleared[:].bitcast(I32), 0)
         nc.vector.memset(base_rows[:], 0.0)
-        for cleared in (tab_rows[2], early_planes):
+        for cleared in (early_planes, tab2_rows, wp_rows, late_planes):
             nc.vector.memset(cleared[:].bitcast(I32), 0)
+        identity = held([P, P], F32, "identity", "tab_rows")
 
+        table_words = [tab_words[0], tab_words[1], tab2_words[0]]
+        table_lists = [lists, lists, lists2]
         windows = [held([P, T], I32, f"window{x}") for x in range(3)]
-        wa_raw = [held([P, 2, KP // 2], I32, f"wa_raw{b}") for b in range(2)]
+        wa_all = held([P, 2, KP], I32, "wa_all")
         wp_raw = held([P, H], I32, "wp_raw")
         ws_raw = {(b, a): held([P, PACK, KP], F32, f"ws_raw{b}{a}") for b in range(2) for a in range(2)}
-        wc_raw = {}
+        picked = [held([P, S], U32, f"picked{x}") for x in range(3)]
+        picked_rows = held([P, S], U8, "picked_rows")
+        picked_rows2 = held([P, S], U8, "picked_rows2")
+        late_rows = held([P, S + H], U8, "late_rows")
 
-        def load_window(x, c0, count):
+        def load_window(x, c0, c1):
             words = table_words[x].rearrange("p t i -> p (t i)").bitcast(I32)
-            nc.sync.dma_start(out=windows[x][:, c0:c0 + count], in_=words[:, c0:c0 + count])
-
-        def load_rows(queue, x):
-            queue.dma_start(out=tab_rows[x][ROW0:P:8, :].bitcast(I32), in_=table_scales[x].bitcast(I32))
+            nc.sync.dma_start(out=windows[x][:, c0:c1], in_=words[:, c0:c1])
 
         def load_ws(b, a):
             rows = ws[a * KP:(a + 1) * KP, b * KP:(b + 1) * KP]
             nc.sync.dma_start(out=ws_raw[b, a][:], in_=rows.rearrange("(p j) c -> p j c", j=PACK))
 
-        def load_wa(b):
-            columns = wa_words.bitcast(I32)[:, :, b * (KP // 2):(b + 1) * (KP // 2)]
-            nc.sync.dma_start(out=wa_raw[b][:], in_=columns.rearrange("a p c -> p a c"))
-
-        def move_rows(queue, planes, rows, first):
-            for r in range(4):
-                queue.dma_start(out=planes[first + r:P:32, :].bitcast(I32), in_=rows[ROW0 + 8 * r:P:32, :].bitcast(I32))
-
-        def sort_rows(sorted_rows, rows):
-            nc.vector.tensor_copy(
-                out=sorted_rows.bitcast(I32).rearrange("p (s t g e) -> p s g t e", t=PACK, g=8, e=4),
-                in_=rows.bitcast(I32).rearrange("p (s g e t) -> p s g t e", t=PACK, g=8, e=4),
-            )
+        def gather(x):
+            nc.vector.tensor_copy(out=picked[x][:], in_=windows[x][:].bitcast(U32).indirect(table_lists[x][:]))
 
         nc.sync.dma_start(lists[:], offs)
-        nc.sync.dma_start(lists2[:], offs2)
-        load_window(0, 0, T // 4)
-        load_rows(nc.sync, 0)
-        load_rows(nc.sync, 1)
-        load_window(0, T // 4, T - T // 4)
+        load_window(0, 0, FIRST_PIECE)
+        nc.sync.dma_start(
+            out=tab_rows[0:P:4, :].bitcast(I32), in_=tab_scales.bitcast(I32).rearrange("a q c -> q a c"))
+        load_window(0, FIRST_PIECE, T)
         for r in range(4):
             nc.sync.dma_start(
                 out=wa_planes[r:P:32, :].bitcast(I32).rearrange("d (a c) -> d a c", a=2),
                 in_=wa_scales[:, r:16:4, :].bitcast(I32).rearrange("a d c -> d a c"),
             )
         nc.sync.dma_start(out=base_rows[0:P:16, :], in_=base.rearrange("(b d x) -> d b x", b=2, d=4))
-        load_rows(nc.sync, 2)
         load_window(1, 0, T)
-        load_wa(0)
-
-        picked_rows = held([P, 2 * S], U8, "picked_rows")
-        for x in range(2):
-            nc.vector.tensor_copy(out=picked_rows[:, x * S:(x + 1) * S], in_=tab_rows[x][:].indirect(lists[:]))
-        move_rows(nc.sync, early_planes, picked_rows, 0)
-        load_wa(1)
+        nc.vector.tensor_copy(out=picked_rows[:], in_=tab_rows[:].indirect(lists[:]))
+        for d in (0, 2, 1, 3):
+            nc.sync.dma_start(
+                out=early_planes[32 * d:32 * d + 4, :].bitcast(I32).rearrange("r (a c) -> r a c", a=2),
+                in_=picked_rows[32 * d:32 * (d + 1):4, :].bitcast(I32),
+            )
+        nc.sync.dma_start(out=wa_all[:], in_=wa_words.bitcast(I32).rearrange("a p c -> p a c"))
+        nc.sync.dma_start(lists2[:], offs2)
+        nc.sync.dma_start(out=tab2_rows[ROW0:P:8, :].bitcast(I32), in_=tab2_scales[0].bitcast(I32))
         load_ws(0, 0)
+        nc.sync.dma_start(out=wp_rows[ROW0:P:8, :].bitcast(I32), in_=wp_scales[0].bitcast(I32))
         load_ws(0, 1)
+        load_ws(1, 0)
+        load_ws(1, 1)
+        nc.sync.dma_start(out=wp_raw[:], in_=wp_words[0].rearrange("p c i -> p (c i)").bitcast(I32))
+        load_window(2, 0, T)
 
         def picked_plane(x, cols):
             return early_planes[:, x * S + cols.start:x * S + cols.stop] if x < 2 else late_planes[LATE0:P, cols]
@@ -122,12 +127,6 @@ def tile_list_tint_adjustment_kernel(
             c0 = S + b * KP + t * P
             return late_planes[LATE0:P, c0:c0 + P]
 
-        picked = [held([P, S], U32, f"picked{x}") for x in range(3)]
-
-        def gather(x):
-            nc.vector.tensor_copy(out=picked[x][:], in_=windows[x][:].bitcast(U32).indirect(table_lists[x][:]))
-
-        identity = held([P, P], F32, "identity", "tab_rows1")
         make_identity(nc, identity[:])
         gather(0)
         base_sorted = held([P, P], F32, "base_sorted")
@@ -139,65 +138,41 @@ def tile_list_tint_adjustment_kernel(
         nc.vector.transpose(out=base_cols[:], in_=base_sorted[:])
         inv_root = held([P, PACK], F32, "inv_root")
         nc.scalar.activation(out=inv_root[:], in_=base_cols[:, 0:P:32], func=ACT.Abs_reciprocal_sqrt)
-
-        wa_codes, wp_codes = {}, {}
-
-        def sort_wp():
-            both = held([P, H], I32, "wp_codes")
-            nc.vector.tensor_copy(
-                out=both[:].rearrange("p (b t h i) -> p b h t i", b=2, t=PACK, i=4),
-                in_=wp_raw[:].rearrange("p (b h t i) -> p b h t i", b=2, t=PACK, i=4),
-            )
-            for b in range(2):
-                wp_codes[b] = both[:, b * KP:(b + 1) * KP]
+        inv_base = held([P, PACK], F32, "inv_base")
+        nc.scalar.activation(out=inv_base[:], in_=inv_root[:], func=ACT.Square)
+        gather(1)
 
         absorbed = [held([P, 4, KP], F32, f"absorbed{b}") for b in range(2)]
-        everything = slice(0, S)
-
-        def cols_of(q):
-            return slice(q * QUARTER, (q + 1) * QUARTER)
 
         def absorption(b):
-            for c in range(4):
-                absorb = bank(PACK * b + c, [P, KP])
-                for a in range(2):
-                    nc.tensor.matmul_mx(
-                        out=absorb[:],
-                        lhsT=picked[a][:, cols_of(c)].bitcast(E4M3), lhsT_scale=picked_plane(a, cols_of(c)),
-                        rhs=wa_raw[b][:, a, :].bitcast(U8).bitcast(E2M1),
-                        rhs_scale=wa_planes[:, a * H + b * KP:a * H + (b + 1) * KP],
-                        start=(a == 0), stop=(a == 1),
-                    )
-                nc.scalar.activation(
-                    out=absorbed[b][:, c, :].rearrange("p (t h i) -> p h t i", t=PACK, i=4),
-                    in_=absorb[:].rearrange("p (h t i) -> p h t i", t=PACK, i=4), func=ACT.Abs,
+            sums = [bank(PACK * b + c, [P, KP]) for c in range(4)]
+
+            def absorption_pass(c, a):
+                nc.tensor.matmul_mx(
+                    out=sums[c][:],
+                    lhsT=picked[a][:, cols_of(c)].bitcast(E4M3), lhsT_scale=picked_plane(a, cols_of(c)),
+                    rhs=wa_all[:, a, b * (KP // 2):(b + 1) * (KP // 2)].bitcast(U8).bitcast(E2M1),
+                    rhs_scale=wa_planes[:, a * H + b * KP:a * H + (b + 1) * KP],
+                    start=(a == 0), stop=(a == 1),
                 )
+
+            for c in range(4):
+                absorption_pass(c, 0)
+                absorption_pass(c, 1)
+                nc.scalar.activation(
+                    out=absorbed[b][:, c, :].rearrange("p (t h i) -> p t h i", t=PACK, i=4),
+                    in_=sums[c][:].rearrange("p (h t i) -> p t h i", t=PACK, i=4), func=ACT.Abs,
+                )
+
+        absorption(0)
+        absorption(1)
+        nc.vector.tensor_copy(out=picked_rows2[:], in_=tab2_rows[:].indirect(lists2[:]))
+        nc.vector.tensor_copy(out=late_rows[:, 0:S].bitcast(I32), in_=picked_rows2[:].bitcast(I32))
 
         def turn(target, b, c, t):
             nc.tensor.transpose(target, absorbed[b][:, c, t * P:(t + 1) * P], identity[:])
 
-        gather(1)
-        unread = bank(7, [P, S])
-        for x in range(4):
-            nc.tensor.matmul_mx(
-                out=unread[:], lhsT=picked[0][:, 0:P].bitcast(E4M3), lhsT_scale=picked_rows[:, 0:P],
-                rhs=picked[0][:].bitcast(E4M3), rhs_scale=picked_rows[:, 0:S], start=True, stop=True,
-            )
-        absorption(0)
-        picked_rows2 = held([P, S], U8, "picked_rows2", "window1")
-        nc.vector.tensor_copy(out=picked_rows2[:], in_=tab_rows[2][:].indirect(lists2[:]))
-        wp_rows = held([P, H], U8, "wp_rows", "tab_rows2")
-        late_planes = held([P, S + H], U8, "late_planes", "picked_rows")
-        for cleared in (wp_rows, late_planes):
-            nc.vector.memset(cleared[:].bitcast(I32), 0)
-        load_ws(1, 0)
-        nc.sync.dma_start(out=wp_rows[ROW0:P:8, :].bitcast(I32), in_=wp_scales[0].bitcast(I32))
-        nc.sync.dma_start(out=wp_raw[:], in_=wp_words[0].rearrange("p c i -> p (c i)").bitcast(I32))
-        load_ws(1, 1)
-        load_window(2, 0, T)
-
-        ws_rounded, ws_codes, ws_plane = {}, {}, {}
-        wc_rounded, wc_codes, wc_plane = {}, {}, {}
+        ws_rounded, ws_codes, ws_plane, whole = {}, {}, {}, {}
 
         def round_ws(b, a, t0, slots):
             ws_rounded[b, a, t0] = held([P, slots * KP], BF16, f"ws_rounded{b}{a}{t0}")
@@ -209,232 +184,266 @@ def tile_list_tint_adjustment_kernel(
         def quantize(rounded, width, name, tag=None):
             codes = held([P, width], U32, name + "_codes", tag)
             plane = held([P, width], U8, name + "_plane")
-            nc.vector.quantize_mx(out=codes[:].bitcast(E4M3), scales=plane[:], in_=rounded[:])
+            nc.vector.quantize_mx(out=codes[:].bitcast(E4M3), scales=plane[:], in_=rounded)
             return codes, plane
 
         def quantize_ws(b, a, t0, slots):
-            codes, plane = quantize(ws_rounded[b, a, t0], slots * P, f"ws{b}{a}{t0}")
+            codes, plane = quantize(ws_rounded[b, a, t0][:], slots * P, f"ws{b}{a}{t0}")
+            whole[b, a, t0] = (codes, plane)
             for s in range(slots):
                 ws_codes[b, a, t0 + s] = codes[:, s * P:(s + 1) * P]
                 ws_plane[b, a, t0 + s] = plane[:, s * P:(s + 1) * P]
 
-        def quantize_wc(b, n0, n1, rounded, codes=None):
-            if codes is None:
-                codes = held([P, n1 - n0], U32, f"wc{b}{n0}_codes")[:]
-            plane = held([P, n1 - n0], U8, f"wc{b}{n0}_plane")
-            nc.vector.quantize_mx(out=codes.bitcast(E4M3), scales=plane[:], in_=rounded)
-            for n in range(n0 // P, n1 // P):
-                wc_codes[b, n] = codes[:, n * P - n0:(n + 1) * P - n0]
-                wc_plane[b, n] = plane[:, n * P - n0:(n + 1) * P - n0]
+        def prepare_ws(b, a, slots):
+            starts = list(range(0, PACK, slots))
+            round_ws(b, a, starts[0], slots)
+            for before, t0 in zip(starts, starts[1:]):
+                round_ws(b, a, t0, slots)
+                quantize_ws(b, a, before, slots)
+            quantize_ws(b, a, starts[-1], slots)
 
         squares = [held([P, PACK, S], F32, f"squares{b}") for b in range(2)]
+        scat = {}
 
         def scattering(b, t):
-            scat = bank(PACK * b + t, [P, S])
+            scat[b, t] = bank(PACK * b + t, [P, S])
             for a in range(2):
                 nc.tensor.matmul_mx(
-                    out=scat[:],
+                    out=scat[b, t][:],
                     lhsT=ws_codes[b, a, t].bitcast(E4M3), lhsT_scale=ws_plane[b, a, t],
                     rhs=picked[a][:].bitcast(E4M3), rhs_scale=picked_plane(a, everything),
                     start=(a == 0), stop=(a == 1),
                 )
-            scale = inv_root[:, t:t + 1] if b == 0 else 1.0
-            nc.scalar.activation(out=squares[b][:, t, :], in_=scat[:], func=ACT.Square, scale=scale)
-
-
-        def inverse_root(b, t):
-            nc.scalar.activation(out=squares[b][:, t, :], in_=squares[b][:, t, :], func=ACT.Abs_reciprocal_sqrt, bias=1.0)
-
-        def inverse_root_half(t, h):
-            part = squares[1][:, t, h * HALF:(h + 1) * HALF]
-            nc.scalar.activation(out=part, in_=part, func=ACT.Abs_reciprocal_sqrt, bias=base_cols[:, 32 * t + 16:32 * t + 17])
-
-        def square_slot(t):
-            nc.scalar.activation(out=squares[0][:, t, :], in_=squares[0][:, t, :], func=ACT.Square, scale=inv_root[:, t:t + 1])
-
-        def divide(target, numerator, inverse):
-            nc.vector.tensor_tensor(out=target, in0=numerator, in1=inverse, op=ALU.mult)
-
-        diffs, dist, d_codes, d_plane = {}, {}, {}, {}
 
         def panel_pass(target, b, t, cols):
+            c0 = b * KP + t * P
             nc.tensor.matmul_mx(
                 out=target,
-                lhsT=wp_codes[b][:, t * P:(t + 1) * P].bitcast(E4M3), lhsT_scale=wp_plane(b, t),
+                lhsT=wp_codes[:, c0:c0 + P].bitcast(E4M3), lhsT_scale=wp_plane(b, t),
                 rhs=picked[2][:, cols].bitcast(E4M3), rhs_scale=picked_plane(2, cols),
                 start=True, stop=True,
             )
 
-        def distance(b, j0, source, target=None):
-            dist[b, j0] = held([P, PACK * QUARTER], BF16, f"dist{b}{j0}")[:] if target is None else target
-            nc.scalar.activation(
-                out=dist[b, j0][:].rearrange("p (c i t) -> p c t i", t=PACK, i=4),
-                in_=source.rearrange("p t (c i) -> p c t i", i=4), func=ACT.Abs,
-            )
-
-        def quantize_d(b, j0, width, codes=None):
-            if codes is None:
-                codes = held([P, width], U32, f"d{b}{j0}_codes")[:]
-            plane = held([P, width], U8, f"d{b}{j0}_plane")
-            nc.vector.quantize_mx(out=codes.bitcast(E4M3), scales=plane[:], in_=dist[b, j0][:])
-            for c0 in range(0, width, QUARTER):
-                d_codes[b, j0 + c0] = codes[:, c0:c0 + QUARTER]
-                d_plane[b, j0 + c0] = plane[:, c0:c0 + QUARTER]
-
-        def second_stage(q, n0, count, number, copy):
-            j0 = q * QUARTER
-            acc = bank(number, [P, count, QUARTER])
-            for b in range(2):
-                for n in range(n0, n0 + count):
-                    nc.tensor.matmul_mx(
-                        out=acc[:, n - n0, :],
-                        lhsT=wc_codes[b, n].bitcast(E4M3), lhsT_scale=wc_plane[b, n],
-                        rhs=d_codes[b, j0].bitcast(E4M3), rhs_scale=d_plane[b, j0],
-                        start=(b == 0 and n == n0), stop=(b == 1 and n == n0 + count - 1),
-                    )
-            result = held([P, count, QUARTER], F32, f"result{q}{n0}")
-            copy(out=result[:], in_=acc[:])
-            nc.sync.dma_start(
-                out=out[n0 * P:(n0 + count) * P, j0:j0 + QUARTER].rearrange("(n p) j -> p n j", p=P),
-                in_=result[:],
-            )
-
         round_ws(0, 0, 0, PACK)
-        late_rows = held([P, S + H], U8, "late_rows", "ws_raw00")
-        nc.vector.tensor_copy(out=late_rows[:, 0:S].bitcast(I32), in_=picked_rows2[:].bitcast(I32))
+        nc.vector.tensor_copy(
+            out=late_rows[:, S:].bitcast(I32).rearrange("p (s t g e) -> p s g t e", t=PACK, g=8, e=4),
+            in_=wp_rows[:].bitcast(I32).rearrange("p (s g e t) -> p s g t e", t=PACK, g=8, e=4),
+        )
         quantize_ws(0, 0, 0, PACK)
-        round_ws(0, 1, 0, 1)
-        round_ws(0, 1, 1, 1)
-        quantize_ws(0, 1, 0, 1)
-        round_ws(0, 1, 2, 1)
-        quantize_ws(0, 1, 1, 1)
-        round_ws(0, 1, 3, 1)
-        quantize_ws(0, 1, 2, 1)
-        quantize_ws(0, 1, 3, 1)
-        for t in range(PACK):
-            scattering(0, t)
-            if t > 1:
-                square_slot(t - 2)
-            if t > 0:
-                inverse_root(0, t - 1)
-        sort_rows(late_rows[:, S:], wp_rows[:])
-        move_rows(nc.sync, late_planes, late_rows, LATE0)
+        for r in range(4):
+            nc.sync.dma_start(
+                out=late_planes[LATE0 + r:P:32, :].bitcast(I32), in_=late_rows[ROW0 + 8 * r:P:32, :].bitcast(I32))
+        wc_raw = {}
         for b in range(2):
-            wc_raw[b] = held([P, PACK, N], F32, f"wc_raw{b}", f"window{b}")
+            wc_raw[b] = held([P, PACK, N], F32, f"wc_raw{b}")
             rows = wc[b * KP:(b + 1) * KP, :].rearrange("(h t i) n -> t h i n", t=PACK, i=4)
             for t in range(PACK):
                 nc.sync.dma_start(out=wc_raw[b][:, t, :], in_=rows[t])
+        prepare_ws(0, 1, 1)
 
-        inverse_root(0, PACK - 1)
+        def square_sum(t):
+            nc.scalar.activation(out=squares[0][:, t, :], in_=scat[0, t][:], func=ACT.Square, scale=inv_root[:, t:t + 1])
+
+        def inverse_root(t):
+            nc.scalar.activation(out=squares[0][:, t, :], in_=squares[0][:, t, :], func=ACT.Abs_reciprocal_sqrt, bias=1.0)
+
+        def square_root_slot(t):
+            if t >= VSQ:
+                nc.scalar.activation(out=squares[0][:, t, :], in_=squares[0][:, t, :], func=ACT.Square, scale=inv_root[:, t:t + 1])
+
+        reciprocal = {t: squares[0][:, t, :] for t in range(PACK)}
+
+        def square_on_vector(t):
+            part = squares[0][:, t, :]
+            reciprocal[t] = held([P, S], F32, f"reciprocal{t}", "ws_raw10")[:]
+            nc.vector.scalar_tensor_tensor(
+                out=reciprocal[t], in0=part, scalar=inv_base[:, t:t + 1], in1=part, op0=ALU.mult, op1=ALU.mult)
+
+        for t in range(PACK):
+            scattering(0, t)
+            square_sum(t)
+            if t >= 2:
+                square_root_slot(t - 2)
+            if t >= 1:
+                inverse_root(t - 1)
+        inverse_root(PACK - 1)
         for t in (PACK - 2, PACK - 1):
-            square_slot(t)
-        absorption(1)
-        slot_quot = []
+            square_root_slot(t)
 
-        def divide_slot(target):
-            t = len(slot_quot)
+        slot_quot = {}
+
+        def divide_slot(t, target):
             numerator = bank(t, [P, S])
             for c in range(4):
                 turn(numerator[:, cols_of(c)], 0, c, t)
-            slot_quot.append(target)
-            divide(target, numerator[:], squares[0][:, t, :])
+            slot_quot[t] = target
+            nc.vector.tensor_tensor(out=target, in0=numerator[:], in1=reciprocal[t], op=ALU.mult)
 
-        round_ws(1, 0, 0, PACK)
-        sort_wp()
-        quantize_ws(1, 0, 0, PACK)
-        divide_slot(held([P, S], F32, "slot_quot0", "wp_raw")[:])
-        round_ws(1, 1, 0, 2)
-        round_ws(1, 1, 2, 2)
-        quantize_ws(1, 1, 0, 2)
-        quantize_ws(1, 1, 2, 2)
-        divide_slot(held([P, S], F32, "slot_quot1", "ws_raw11")[:])
+        prepare_ws(1, 0, 2)
+        square_on_vector(0)
+        prepare_ws(1, 1, 2)
         for t in range(PACK):
             scattering(1, t)
+        wp_codes = held([P, H], I32, "wp_codes", "ws_rounded112")
+        nc.gpsimd.tensor_copy(
+            out=wp_codes[:].rearrange("p (b t h i) -> p b t h i", b=2, t=PACK, i=4),
+            in_=wp_raw[:].rearrange("p (b h t i) -> p b t h i", b=2, t=PACK, i=4),
+        )
+        first_quot = held([P, PACK - 1, S], F32, "first_quot", "ws_raw11")
+        for t in range(PACK - 1):
+            divide_slot(t, first_quot[:, t, :])
         gather(2)
-        behind_gather = held([P, T], F32, "behind_gather", "window2")
-        divide_slot(behind_gather[:, 0:S])
-        divide_slot(behind_gather[:, S:2 * S])
-        diffs0 = held([P, PACK, S], F32, "diffs_all")
+        divide_slot(PACK - 1, held([P, S], F32, "last_quot", "window2")[:])
+        diffs0 = held([P, PACK, S], F32, "diffs0")
         for t in range(PACK):
             panel = bank(t, [P, S])
             panel_pass(panel[:], 0, t, everything)
             nc.vector.tensor_tensor(out=diffs0[:, t, :], in0=panel[:], in1=slot_quot[t], op=ALU.subtract)
 
-        def round_wc(b, n0, n1):
+        wc_rounded = {}
+
+        def round_wc(engine, b, n0, n1, tag=None):
+            wc_rounded[b, n0] = held([P, PACK * (n1 - n0)], BF16, f"wc_rounded{b}{n0}", tag)
+            if engine is nc.vector:
+                nc.vector.tensor_copy(
+                    out=wc_rounded[b, n0][:].rearrange("p (c i t) -> p c t i", t=PACK, i=4),
+                    in_=wc_raw[b][:, :, n0:n1].rearrange("p t (c i) -> p c t i", i=4),
+                )
+                return
             nc.gpsimd.tensor_scalar(
-                out=wc_rounded[b][:, n0 * PACK:n1 * PACK].rearrange("p (c t) -> p c t", t=PACK),
+                out=wc_rounded[b, n0][:].rearrange("p (c t) -> p c t", t=PACK),
                 in0=wc_raw[b][:, :, n0:n1].rearrange("p t c -> p c t"),
                 scalar1=1.0, scalar2=0.0, op0=ALU.mult, op1=ALU.add,
             )
 
-        wc_rounded[0] = behind_gather[:, 2 * S:].bitcast(BF16)
-        wc_rounded[1] = held([P, PACK * SHARE], BF16, "wc_rounded1")[:]
-        round_wc(0, 0, N)
-        round_wc(1, 0, SHARE)
-        quot = [held([P, PACK, QUARTER], F32, f"quot{q}") for q in range(4)]
+        round_wc(nc.gpsimd, 0, 0, N)
+        round_wc(nc.gpsimd, 1, 0, N)
+        inverse = [held([P, PACK, QUARTER], F32, f"inverse{q}") for q in range(4)]
+        products, diffs1 = {}, {}
+
+        def square_half(t, h):
+            nc.scalar.activation(out=squares[1][:, t, half(h)], in_=scat[1, t][:, half(h)], func=ACT.Square)
+
+        def inverse_root_half(t, h):
+            part = squares[1][:, t, half(h)]
+            nc.scalar.activation(
+                out=part, in_=part, func=ACT.Abs_reciprocal_sqrt, bias=base_cols[:, 32 * t + 16:32 * t + 17])
 
         def square_quarter(q):
-            nc.scalar.activation(out=quot[q][:], in_=squares[1][:, :, cols_of(q)], func=ACT.Square)
+            nc.scalar.activation(out=inverse[q][:], in_=squares[1][:, :, cols_of(q)], func=ACT.Square)
 
-        for t in range(PACK):
-            inverse_root_half(t, 0)
-        inverse_root_half(0, 1)
-        square_quarter(0)
-        square_quarter(1)
-        for t in range(1, PACK):
-            inverse_root_half(t, 1)
-        square_quarter(2)
-        square_quarter(3)
-        rounded0 = held([P, PACK * S], BF16, "rounded0", "squares1")
-        distance(0, 0, diffs0[:, :, 0:HALF], rounded0[:, 0:PACK * HALF])
-        products = {}
-        diffs1 = held([P, PACK, HALF], F32, "diffs1")
-
-        def divide_quarter(q, tag=None):
-            numerator = bank(q, [P, PACK, QUARTER])
+        def divide_quarter(q, number):
+            numerator = bank(number, [P, PACK, QUARTER])
             for t in range(PACK):
                 turn(numerator[:, t, :], 1, q, t)
-            products[q] = held([P, PACK, QUARTER], F32, f"product{q}", tag)
-            divide(products[q][:], numerator[:], quot[q][:])
+            products[q] = held([P, PACK, QUARTER], F32, f"product{q}")
+            nc.vector.tensor_tensor(out=products[q][:], in0=numerator[:], in1=inverse[q][:], op=ALU.mult)
 
-        def subtract_quarter(q, tag=None):
-            panel = bank(PACK + q, [P, PACK, QUARTER])
+        def subtract_quarter(q, number):
+            panel = bank(number, [P, PACK, QUARTER])
             for t in range(PACK):
                 panel_pass(panel[:, t, :], 1, t, cols_of(q))
-            target = diffs1[:, :, cols_of(q)] if q < 2 else held([P, PACK, QUARTER], F32, f"diffs{q}", tag)[:]
-            nc.vector.tensor_tensor(out=target, in0=panel[:], in1=products[q][:], op=ALU.subtract)
-            if q == 1:
-                distance(1, 0, diffs1[:], held([P, PACK * HALF], BF16, "rounded1")[:])
-            if q > 1:
-                distance(1, q * QUARTER, target)
+            diffs1[q] = held([P, PACK, QUARTER], F32, f"diffs1{q}")
+            nc.vector.tensor_tensor(out=diffs1[q][:], in0=panel[:], in1=products[q][:], op=ALU.subtract)
 
-        divide_quarter(0)
-        divide_quarter(1)
-        subtract_quarter(0)
-        subtract_quarter(1)
-        divide_quarter(2)
-        divide_quarter(3)
-        distance(0, HALF, diffs0[:, :, HALF:S], rounded0[:, PACK * HALF:])
-        rest = held([P, PACK * (N - SHARE)], BF16, "wc_rest", "quot3")
-        nc.vector.tensor_copy(
-            out=rest[:].rearrange("p (c i t) -> p c t i", t=PACK, i=4),
-            in_=wc_raw[1][:, :, SHARE:].rearrange("p t (c i) -> p c t i", i=4),
-        )
-        subtract_quarter(2)
-        codes = held([P, N + HALF], U32, "late_codes", "window1")
-        quantize_wc(0, 0, N, wc_rounded[0], codes[:, 0:N])
-        quantize_d(0, 0, HALF, codes[:, N:])
-        quantize_wc(1, SHARE, N, rest[:])
-        shared = held([P, SHARE], U32, "wc10_codes", "quot3")
-        quantize_wc(1, 0, HALF, wc_rounded[1][:, 0:PACK * HALF], shared[:, 0:HALF])
-        quantize_wc(1, HALF, SHARE, wc_rounded[1][:, PACK * HALF:], shared[:, HALF:])
-        quantize_d(1, 0, HALF, held([P, HALF], U32, "d1_codes", "window2")[:])
-        subtract_quarter(3, "rounded1")
-        quantize_d(0, HALF, HALF, held([P, HALF], U32, "d0h_codes", "product2")[:])
-        quantize_d(1, 2 * QUARTER, QUARTER)
-        second_stage(0, 0, PACK, 0, nc.vector.tensor_copy)
-        quantize_d(1, 3 * QUARTER, QUARTER)
-        second_stage(1, 0, PACK, 1, nc.vector.tensor_copy)
-        second_stage(2, 0, PACK, 2, nc.scalar.copy)
-        second_stage(3, 0, 2, 3, nc.vector.tensor_copy)
-        second_stage(3, 2, 2, 4, nc.scalar.copy)
+        d_codes, wc_codes, wc_plane = [{}, {}], {}, {}
+
+        def distance(target, source):
+            nc.scalar.activation(
+                out=target.rearrange("p (c i t) -> p c t i", t=PACK, i=4),
+                in_=source.rearrange("p t (c i) -> p c t i", i=4), func=ACT.Abs,
+            )
+
+        def distance_on_vector(target, source):
+            walk = source.rearrange("p t (c i) -> p c t i", i=4)
+            for c0 in range(0, 32, 32):
+                nc.vector.scalar_tensor_tensor(
+                    out=target.rearrange("p (c i t) -> p c t i", t=PACK, i=4), in0=walk, scalar=-1.0, in1=walk,
+                    op0=ALU.mult, op1=ALU.max,
+                )
+
+        def quantize_d(b, j0, width, rounded):
+            codes, plane = quantize(rounded, width, f"d{b}{j0}")
+            d_codes[b][j0] = (codes, plane, width)
+
+        def quantize_wc(b, n0, n1, first=None):
+            first = n0 if first is None else first
+            codes, plane = quantize(wc_rounded[b, first][:, PACK * (n0 - first):PACK * (n1 - first)], n1 - n0, f"wc{b}{n0}")
+            for n in range(n0 // P, n1 // P):
+                wc_codes[b, n] = codes[:, n * P - n0:(n + 1) * P - n0]
+                wc_plane[b, n] = plane[:, n * P - n0:(n + 1) * P - n0]
+
+        def second_stage(j0, width, n0, count, number, copy):
+            acc = bank(number, [P, count, width])
+            passes = [(b, c0, n) for b in range(2) for c0 in d_codes[b] if j0 <= c0 < j0 + width
+                      for n in range(n0, n0 + count)]
+            for number_of_pass, (b, c0, n) in enumerate(passes):
+                codes, plane, columns = d_codes[b][c0]
+                nc.tensor.matmul_mx(
+                    out=acc[:, n - n0, c0 - j0:c0 - j0 + columns],
+                    lhsT=wc_codes[b, n].bitcast(E4M3), lhsT_scale=wc_plane[b, n],
+                    rhs=codes[:].bitcast(E4M3), rhs_scale=plane[:],
+                    start=(number_of_pass == 0), stop=(number_of_pass == len(passes) - 1),
+                )
+            result = held([P, count, width], F32, f"result{j0}{n0}")
+            copy(out=result[:], in_=acc[:])
+            nc.sync.dma_start(
+                out=out[n0 * P:(n0 + count) * P, j0:j0 + width].rearrange("(n p) j -> p n j", p=P),
+                in_=result[:],
+            )
+
+        rounded = [held([P, PACK * S], BF16, f"rounded{b}") for b in range(2)]
+
+        def rounded_cols(b, j0, width):
+            return rounded[b][:, PACK * j0:PACK * (j0 + width)]
+
+        square_half(0, 0)
+        square_half(1, 0)
+        square_half(2, 0)
+        square_half(3, 0)
+        inverse_root_half(0, 0)
+        inverse_root_half(1, 0)
+        inverse_root_half(2, 0)
+        inverse_root_half(3, 0)
+        square_half(0, 1)
+        square_quarter(0)
+        square_quarter(1)
+        square_half(1, 1)
+        square_half(2, 1)
+        square_half(3, 1)
+        inverse_root_half(0, 1)
+        inverse_root_half(1, 1)
+        inverse_root_half(2, 1)
+        inverse_root_half(3, 1)
+        distance(rounded_cols(0, 0 * QUARTER, QUARTER), diffs0[:, :, cols_of(0)])
+        square_quarter(2)
+        square_quarter(3)
+        divide_quarter(0, 0)
+        divide_quarter(1, 1)
+        subtract_quarter(0, 2)
+        subtract_quarter(1, 3)
+        divide_quarter(2, 0)
+        divide_quarter(3, 1)
+        subtract_quarter(2, 2)
+        subtract_quarter(3, 3)
+        distance(rounded_cols(0, 1 * QUARTER, QUARTER), diffs0[:, :, cols_of(1)])
+        distance(rounded_cols(1, 0 * QUARTER, QUARTER), diffs1[0][:])
+        distance(rounded_cols(1, 1 * QUARTER, QUARTER), diffs1[1][:])
+        distance(rounded_cols(0, HALF, HALF), diffs0[:, :, half(1)])
+        distance(rounded_cols(1, 2 * QUARTER, QUARTER), diffs1[2][:])
+        distance(rounded_cols(1, 3 * QUARTER, QUARTER), diffs1[3][:])
+        quantize_wc(0, 0, HALF, 0)
+        quantize_d(0, 0, HALF, rounded_cols(0, 0, HALF))
+        quantize_wc(1, 0, HALF, 0)
+        quantize_d(1, 0, HALF, rounded_cols(1, 0, HALF))
+        quantize_wc(0, HALF, N, 0)
+        quantize_wc(1, HALF, N, 0)
+        quantize_d(0, HALF, HALF, rounded_cols(0, HALF, HALF))
+        quantize_d(1, 2 * QUARTER, QUARTER, rounded_cols(1, 2 * QUARTER, QUARTER))
+        second_stage(0, HALF, 0, 2, 4, nc.vector.tensor_copy)
+        quantize_d(1, 3 * QUARTER, QUARTER, rounded_cols(1, 3 * QUARTER, QUARTER))
+        second_stage(0, HALF, 2, 2, 5, nc.scalar.copy)
+        second_stage(HALF, HALF, 0, 1, 6, nc.vector.tensor_copy)
+        second_stage(HALF, HALF, 1, 1, 7, nc.scalar.copy)
+        second_stage(HALF, HALF, 2, 1, 0, nc.vector.tensor_copy)
+        second_stage(HALF, HALF, 3, 1, 2, nc.scalar.copy)

@@ -72,7 +72,7 @@ def tile_list_tint_adjustment_kernel(
         table_words = [tab_words[0], tab_words[1], tab2_words[0]]
         table_lists = [lists, lists, lists2]
         windows = [held([P, T], I32, f"window{x}") for x in range(3)]
-        wa_all = held([P, 2, KP], I32, "wa_all")
+        wa_raw = [held([P, 2, KP // 2], I32, f"wa_raw{b}") for b in range(2)]
         wp_raw = held([P, H], I32, "wp_raw")
         ws_raw = {(b, a): held([P, PACK, KP], F32, f"ws_raw{b}{a}") for b in range(2) for a in range(2)}
         picked = [held([P, S], U32, f"picked{x}") for x in range(3)]
@@ -87,6 +87,10 @@ def tile_list_tint_adjustment_kernel(
         def load_ws(b, a):
             rows = ws[a * KP:(a + 1) * KP, b * KP:(b + 1) * KP]
             nc.sync.dma_start(out=ws_raw[b, a][:], in_=rows.rearrange("(p j) c -> p j c", j=PACK))
+
+        def load_wa(b):
+            columns = wa_words.bitcast(I32)[:, :, b * (KP // 2):(b + 1) * (KP // 2)]
+            nc.sync.dma_start(out=wa_raw[b][:], in_=columns.rearrange("a p c -> p a c"))
 
         def gather(x):
             nc.vector.tensor_copy(out=picked[x][:], in_=windows[x][:].bitcast(U32).indirect(table_lists[x][:]))
@@ -109,7 +113,8 @@ def tile_list_tint_adjustment_kernel(
                 out=early_planes[32 * d:32 * d + 4, :].bitcast(I32).rearrange("r (a c) -> r a c", a=2),
                 in_=picked_rows[32 * d:32 * (d + 1):4, :].bitcast(I32),
             )
-        nc.sync.dma_start(out=wa_all[:], in_=wa_words.bitcast(I32).rearrange("a p c -> p a c"))
+        load_wa(0)
+        load_wa(1)
         nc.sync.dma_start(lists2[:], offs2)
         nc.sync.dma_start(out=tab2_rows[ROW0:P:8, :].bitcast(I32), in_=tab2_scales[0].bitcast(I32))
         load_ws(0, 0)
@@ -151,7 +156,7 @@ def tile_list_tint_adjustment_kernel(
                 nc.tensor.matmul_mx(
                     out=sums[c][:],
                     lhsT=picked[a][:, cols_of(c)].bitcast(E4M3), lhsT_scale=picked_plane(a, cols_of(c)),
-                    rhs=wa_all[:, a, b * (KP // 2):(b + 1) * (KP // 2)].bitcast(U8).bitcast(E2M1),
+                    rhs=wa_raw[b][:, a, :].bitcast(U8).bitcast(E2M1),
                     rhs_scale=wa_planes[:, a * H + b * KP:a * H + (b + 1) * KP],
                     start=(a == 0), stop=(a == 1),
                 )
@@ -321,8 +326,8 @@ def tile_list_tint_adjustment_kernel(
         inverse = [held([P, PACK, QUARTER], F32, f"inverse{q}") for q in range(4)]
         products, diffs1 = {}, {}
 
-        def square_half(t, h):
-            nc.scalar.activation(out=squares[1][:, t, half(h)], in_=scat[1, t][:, half(h)], func=ACT.Square)
+        def square_whole(t):
+            nc.scalar.activation(out=squares[1][:, t, :], in_=scat[1, t][:], func=ACT.Square)
 
         def inverse_root_half(t, h):
             part = squares[1][:, t, half(h)]
@@ -397,21 +402,17 @@ def tile_list_tint_adjustment_kernel(
         def rounded_cols(b, j0, width):
             return rounded[b][:, PACK * j0:PACK * (j0 + width)]
 
-        square_half(0, 0)
-        square_half(1, 0)
-        square_half(2, 0)
-        square_half(3, 0)
+        square_whole(0)
+        square_whole(1)
+        square_whole(2)
+        square_whole(3)
         inverse_root_half(0, 0)
         inverse_root_half(1, 0)
         inverse_root_half(2, 0)
         inverse_root_half(3, 0)
-        square_half(0, 1)
+        inverse_root_half(0, 1)
         square_quarter(0)
         square_quarter(1)
-        square_half(1, 1)
-        square_half(2, 1)
-        square_half(3, 1)
-        inverse_root_half(0, 1)
         inverse_root_half(1, 1)
         inverse_root_half(2, 1)
         inverse_root_half(3, 1)
@@ -432,18 +433,22 @@ def tile_list_tint_adjustment_kernel(
         distance(rounded_cols(0, HALF, HALF), diffs0[:, :, half(1)])
         distance(rounded_cols(1, 2 * QUARTER, QUARTER), diffs1[2][:])
         distance(rounded_cols(1, 3 * QUARTER, QUARTER), diffs1[3][:])
-        quantize_wc(0, 0, HALF, 0)
+        quantize_wc(0, 0, 128, 0)
         quantize_d(0, 0, HALF, rounded_cols(0, 0, HALF))
-        quantize_wc(1, 0, HALF, 0)
+        quantize_wc(1, 0, 128, 0)
         quantize_d(1, 0, HALF, rounded_cols(1, 0, HALF))
-        quantize_wc(0, HALF, N, 0)
-        quantize_wc(1, HALF, N, 0)
+        quantize_wc(0, 128, 256, 0)
+        quantize_wc(1, 128, 256, 0)
+        quantize_wc(0, 256, 512, 0)
+        second_stage(0, HALF, 0, 1, 4, nc.vector.tensor_copy)
+        quantize_wc(1, 256, 512, 0)
+        second_stage(0, HALF, 1, 1, 5, nc.vector.tensor_copy)
         quantize_d(0, HALF, HALF, rounded_cols(0, HALF, HALF))
         quantize_d(1, 2 * QUARTER, QUARTER, rounded_cols(1, 2 * QUARTER, QUARTER))
-        second_stage(0, HALF, 0, 2, 4, nc.vector.tensor_copy)
         quantize_d(1, 3 * QUARTER, QUARTER, rounded_cols(1, 3 * QUARTER, QUARTER))
-        second_stage(0, HALF, 2, 2, 5, nc.scalar.copy)
-        second_stage(HALF, HALF, 0, 1, 6, nc.vector.tensor_copy)
-        second_stage(HALF, HALF, 1, 1, 7, nc.scalar.copy)
-        second_stage(HALF, HALF, 2, 1, 0, nc.vector.tensor_copy)
-        second_stage(HALF, HALF, 3, 1, 2, nc.scalar.copy)
+        second_stage(0, HALF, 2, 1, 6, nc.scalar.copy)
+        second_stage(0, HALF, 3, 1, 7, nc.vector.tensor_copy)
+        second_stage(HALF, HALF, 0, 1, 0, nc.scalar.copy)
+        second_stage(HALF, HALF, 1, 1, 3, nc.vector.tensor_copy)
+        second_stage(HALF, HALF, 2, 1, 2, nc.scalar.copy)
+        second_stage(HALF, HALF, 3, 1, 1, nc.vector.tensor_copy)

@@ -106,6 +106,7 @@ def tile_list_tint_adjustment_kernel(
                 in_=wa_scales[:, r:16:4, :].bitcast(I32).rearrange("a d c -> d a c"),
             )
         nc.sync.dma_start(out=base_rows[0:P:16, :], in_=base.rearrange("(b d x) -> d b x", b=2, d=4))
+        nc.sync.dma_start(lists2[:], offs2)
         load_window(1, 0, T)
         nc.vector.tensor_copy(out=picked_rows[:], in_=tab_rows[:].indirect(lists[:]))
         for d in (0, 2, 1, 3):
@@ -115,7 +116,6 @@ def tile_list_tint_adjustment_kernel(
             )
         load_wa(0)
         load_wa(1)
-        nc.sync.dma_start(lists2[:], offs2)
         nc.sync.dma_start(out=tab2_rows[ROW0:P:8, :].bitcast(I32), in_=tab2_scales[0].bitcast(I32))
         load_ws(0, 0)
         nc.sync.dma_start(out=wp_rows[ROW0:P:8, :].bitcast(I32), in_=wp_scales[0].bitcast(I32))

@@ -341,7 +341,7 @@ def tile_list_tint_adjustment_kernel(
             numerator = bank(number, [P, PACK, QUARTER])
             for t in range(PACK):
                 turn(numerator[:, t, :], 1, q, t)
-            products[q] = held([P, PACK, QUARTER], F32, f"product{q}")
+            products[q] = held([P, PACK, QUARTER], F32, f"product{q}", ("ws_raw11", "window2", None, None)[q])
             nc.vector.tensor_tensor(out=products[q][:], in0=numerator[:], in1=inverse[q][:], op=ALU.mult)
 
         def subtract_quarter(q, number):
@@ -419,10 +419,10 @@ def tile_list_tint_adjustment_kernel(
         distance(rounded_cols(0, 0 * QUARTER, QUARTER), diffs0[:, :, cols_of(0)])
         square_quarter(2)
         square_quarter(3)
-        divide_quarter(0, 0)
-        divide_quarter(1, 1)
-        subtract_quarter(0, 2)
-        subtract_quarter(1, 3)
+        divide_quarter(0, 4)
+        divide_quarter(1, 5)
+        subtract_quarter(0, 6)
+        subtract_quarter(1, 7)
         divide_quarter(2, 0)
         divide_quarter(3, 1)
         subtract_quarter(2, 2)

@@ -433,6 +433,13 @@ def tile_list_tint_adjustment_kernel(
         distance(rounded_cols(0, HALF, HALF), diffs0[:, :, half(1)])
         distance(rounded_cols(1, 2 * QUARTER, QUARTER), diffs1[2][:])
         distance(rounded_cols(1, 3 * QUARTER, QUARTER), diffs1[3][:])
+        warm_codes, warm_plane = whole[0, 0, 0]
+        unread = bank(0, [P, S])
+        for x in range(4):
+            nc.tensor.matmul_mx(
+                out=unread[:], lhsT=ws_codes[1, 0, 0].bitcast(E4M3), lhsT_scale=ws_plane[1, 0, 0],
+                rhs=warm_codes[:].bitcast(E4M3), rhs_scale=warm_plane[:], start=True, stop=True,
+            )
         quantize_wc(0, 0, 128, 0)
         quantize_d(0, 0, HALF, rounded_cols(0, 0, HALF))
         quantize_wc(1, 0, 128, 0)

@@ -72,7 +72,7 @@ def tile_list_tint_adjustment_kernel(
         table_words = [tab_words[0], tab_words[1], tab2_words[0]]
         table_lists = [lists, lists, lists2]
         windows = [held([P, T], I32, f"window{x}") for x in range(3)]
-        wa_raw = [held([P, 2, KP // 2], I32, f"wa_raw{b}") for b in range(2)]
+        wa_all = held([P, 2, KP], I32, "wa_all")
         wp_raw = held([P, H], I32, "wp_raw")
         ws_raw = {(b, a): held([P, PACK, KP], F32, f"ws_raw{b}{a}") for b in range(2) for a in range(2)}
         picked = [held([P, S], U32, f"picked{x}") for x in range(3)]
@@ -88,10 +88,6 @@ def tile_list_tint_adjustment_kernel(
             rows = ws[a * KP:(a + 1) * KP, b * KP:(b + 1) * KP]
             nc.sync.dma_start(out=ws_raw[b, a][:], in_=rows.rearrange("(p j) c -> p j c", j=PACK))
 
-        def load_wa(b):
-            columns = wa_words.bitcast(I32)[:, :, b * (KP // 2):(b + 1) * (KP // 2)]
-            nc.sync.dma_start(out=wa_raw[b][:], in_=columns.rearrange("a p c -> p a c"))
-
         def gather(x):
             nc.vector.tensor_copy(out=picked[x][:], in_=windows[x][:].bitcast(U32).indirect(table_lists[x][:]))
 
@@ -106,7 +102,6 @@ def tile_list_tint_adjustment_kernel(
                 in_=wa_scales[:, r:16:4, :].bitcast(I32).rearrange("a d c -> d a c"),
             )
         nc.sync.dma_start(out=base_rows[0:P:16, :], in_=base.rearrange("(b d x) -> d b x", b=2, d=4))
-        nc.sync.dma_start(lists2[:], offs2)
         load_window(1, 0, T)
         nc.vector.tensor_copy(out=picked_rows[:], in_=tab_rows[:].indirect(lists[:]))
         for d in (0, 2, 1, 3):
@@ -114,8 +109,8 @@ def tile_list_tint_adjustment_kernel(
                 out=early_planes[32 * d:32 * d + 4, :].bitcast(I32).rearrange("r (a c) -> r a c", a=2),
                 in_=picked_rows[32 * d:32 * (d + 1):4, :].bitcast(I32),
             )
-        load_wa(0)
-        load_wa(1)
+        nc.sync.dma_start(out=wa_all[:], in_=wa_words.bitcast(I32).rearrange("a p c -> p a c"))
+        nc.sync.dma_start(lists2[:], offs2)
         nc.sync.dma_start(out=tab2_rows[ROW0:P:8, :].bitcast(I32), in_=tab2_scales[0].bitcast(I32))
         load_ws(0, 0)
         nc.sync.dma_start(out=wp_rows[ROW0:P:8, :].bitcast(I32), in_=wp_scales[0].bitcast(I32))
@@ -156,7 +151,7 @@ def tile_list_tint_adjustment_kernel(
                 nc.tensor.matmul_mx(
                     out=sums[c][:],
                     lhsT=picked[a][:, cols_of(c)].bitcast(E4M3), lhsT_scale=picked_plane(a, cols_of(c)),
-                    rhs=wa_raw[b][:, a, :].bitcast(U8).bitcast(E2M1),
+                    rhs=wa_all[:, a, b * (KP // 2):(b + 1) * (KP // 2)].bitcast(U8).bitcast(E2M1),
                     rhs_scale=wa_planes[:, a * H + b * KP:a * H + (b + 1) * KP],
                     start=(a == 0), stop=(a == 1),
                 )
@@ -440,22 +435,20 @@ def tile_list_tint_adjustment_kernel(
                 out=unread[:], lhsT=ws_codes[1, 0, 0].bitcast(E4M3), lhsT_scale=ws_plane[1, 0, 0],
                 rhs=warm_codes[:].bitcast(E4M3), rhs_scale=warm_plane[:], start=True, stop=True,
             )
-        quantize_wc(0, 0, 128, 0)
+        quantize_wc(0, 0, 256, 0)
         quantize_d(0, 0, HALF, rounded_cols(0, 0, HALF))
-        quantize_wc(1, 0, 128, 0)
+        quantize_wc(1, 0, 256, 0)
         quantize_d(1, 0, HALF, rounded_cols(1, 0, HALF))
-        quantize_wc(0, 128, 256, 0)
-        quantize_wc(1, 128, 256, 0)
         quantize_wc(0, 256, 512, 0)
-        second_stage(0, HALF, 0, 1, 4, nc.vector.tensor_copy)
         quantize_wc(1, 256, 512, 0)
-        second_stage(0, HALF, 1, 1, 5, nc.vector.tensor_copy)
         quantize_d(0, HALF, HALF, rounded_cols(0, HALF, HALF))
         quantize_d(1, 2 * QUARTER, QUARTER, rounded_cols(1, 2 * QUARTER, QUARTER))
         quantize_d(1, 3 * QUARTER, QUARTER, rounded_cols(1, 3 * QUARTER, QUARTER))
+        second_stage(0, HALF, 0, 1, 4, nc.scalar.copy)
+        second_stage(0, HALF, 1, 1, 5, nc.vector.tensor_copy)
         second_stage(0, HALF, 2, 1, 6, nc.scalar.copy)
         second_stage(0, HALF, 3, 1, 7, nc.vector.tensor_copy)
         second_stage(HALF, HALF, 0, 1, 0, nc.scalar.copy)
-        second_stage(HALF, HALF, 1, 1, 3, nc.vector.tensor_copy)
+        second_stage(HALF, HALF, 1, 1, 1, nc.vector.tensor_copy)
         second_stage(HALF, HALF, 2, 1, 2, nc.scalar.copy)
-        second_stage(HALF, HALF, 3, 1, 1, nc.vector.tensor_copy)
+        second_stage(HALF, HALF, 3, 1, 3, nc.vector.tensor_copy)

@@ -319,7 +319,8 @@ def tile_list_tint_adjustment_kernel(
         round_wc(nc.gpsimd, 0, 0, N)
         round_wc(nc.gpsimd, 1, 0, N)
         inverse = [held([P, PACK, QUARTER], F32, f"inverse{q}") for q in range(4)]
-        products, diffs1 = {}, {}
+        products = {}
+        diffs1 = held([P, PACK, S], F32, "diffs1")
 
         def square_whole(t):
             nc.scalar.activation(out=squares[1][:, t, :], in_=scat[1, t][:], func=ACT.Square)
@@ -343,8 +344,7 @@ def tile_list_tint_adjustment_kernel(
             panel = bank(number, [P, PACK, QUARTER])
             for t in range(PACK):
                 panel_pass(panel[:, t, :], 1, t, cols_of(q))
-            diffs1[q] = held([P, PACK, QUARTER], F32, f"diffs1{q}")
-            nc.vector.tensor_tensor(out=diffs1[q][:], in0=panel[:], in1=products[q][:], op=ALU.subtract)
+            nc.vector.tensor_tensor(out=diffs1[:, :, cols_of(q)], in0=panel[:], in1=products[q][:], op=ALU.subtract)
 
         d_codes, wc_codes, wc_plane = [{}, {}], {}, {}
 
@@ -423,11 +423,10 @@ def tile_list_tint_adjustment_kernel(
         subtract_quarter(2, 2)
         subtract_quarter(3, 3)
         distance(rounded_cols(0, 1 * QUARTER, QUARTER), diffs0[:, :, cols_of(1)])
-        distance(rounded_cols(1, 0 * QUARTER, QUARTER), diffs1[0][:])
-        distance(rounded_cols(1, 1 * QUARTER, QUARTER), diffs1[1][:])
+        distance(rounded_cols(1, 0, HALF), diffs1[:, :, 0:0 + HALF])
         distance(rounded_cols(0, HALF, HALF), diffs0[:, :, half(1)])
-        distance(rounded_cols(1, 2 * QUARTER, QUARTER), diffs1[2][:])
-        distance(rounded_cols(1, 3 * QUARTER, QUARTER), diffs1[3][:])
+        distance(rounded_cols(1, HALF, QUARTER), diffs1[:, :, HALF:HALF + QUARTER])
+        distance(rounded_cols(1, 3 * QUARTER, QUARTER), diffs1[:, :, 3 * QUARTER:3 * QUARTER + QUARTER])
         warm_codes, warm_plane = whole[0, 0, 0]
         unread = bank(0, [P, S])
         for x in range(4):
@@ -435,20 +434,19 @@ def tile_list_tint_adjustment_kernel(
                 out=unread[:], lhsT=ws_codes[1, 0, 0].bitcast(E4M3), lhsT_scale=ws_plane[1, 0, 0],
                 rhs=warm_codes[:].bitcast(E4M3), rhs_scale=warm_plane[:], start=True, stop=True,
             )
-        quantize_wc(0, 0, 256, 0)
+        quantize_wc(0, 0, 512, 0)
         quantize_d(0, 0, HALF, rounded_cols(0, 0, HALF))
         quantize_wc(1, 0, 256, 0)
         quantize_d(1, 0, HALF, rounded_cols(1, 0, HALF))
-        quantize_wc(0, 256, 512, 0)
         quantize_wc(1, 256, 512, 0)
         quantize_d(0, HALF, HALF, rounded_cols(0, HALF, HALF))
         quantize_d(1, 2 * QUARTER, QUARTER, rounded_cols(1, 2 * QUARTER, QUARTER))
         quantize_d(1, 3 * QUARTER, QUARTER, rounded_cols(1, 3 * QUARTER, QUARTER))
         second_stage(0, HALF, 0, 1, 4, nc.scalar.copy)
-        second_stage(0, HALF, 1, 1, 5, nc.vector.tensor_copy)
-        second_stage(0, HALF, 2, 1, 6, nc.scalar.copy)
-        second_stage(0, HALF, 3, 1, 7, nc.vector.tensor_copy)
-        second_stage(HALF, HALF, 0, 1, 0, nc.scalar.copy)
-        second_stage(HALF, HALF, 1, 1, 1, nc.vector.tensor_copy)
-        second_stage(HALF, HALF, 2, 1, 2, nc.scalar.copy)
-        second_stage(HALF, HALF, 3, 1, 3, nc.vector.tensor_copy)
+        second_stage(0, HALF, 1, 1, 5, nc.scalar.copy)
+        second_stage(0, HALF, 2, 1, 6, nc.vector.tensor_copy)
+        second_stage(0, HALF, 3, 1, 7, nc.scalar.copy)
+        second_stage(HALF, HALF, 0, 1, 0, nc.vector.tensor_copy)
+        second_stage(HALF, HALF, 1, 1, 1, nc.scalar.copy)
+        second_stage(HALF, HALF, 2, 1, 2, nc.vector.tensor_copy)
+        second_stage(HALF, HALF, 3, 1, 3, nc.scalar.copy)

@@ -72,7 +72,7 @@ def tile_list_tint_adjustment_kernel(
         table_words = [tab_words[0], tab_words[1], tab2_words[0]]
         table_lists = [lists, lists, lists2]
         windows = [held([P, T], I32, f"window{x}") for x in range(3)]
-        wa_all = held([P, 2, KP], I32, "wa_all")
+        wa_raw = [held([P, KP], I32, f"wa_raw{a}") for a in range(2)]
         wp_raw = held([P, H], I32, "wp_raw")
         ws_raw = {(b, a): held([P, PACK, KP], F32, f"ws_raw{b}{a}") for b in range(2) for a in range(2)}
         picked = [held([P, S], U32, f"picked{x}") for x in range(3)]
@@ -102,6 +102,7 @@ def tile_list_tint_adjustment_kernel(
                 in_=wa_scales[:, r:16:4, :].bitcast(I32).rearrange("a d c -> d a c"),
             )
         nc.sync.dma_start(out=base_rows[0:P:16, :], in_=base.rearrange("(b d x) -> d b x", b=2, d=4))
+        nc.sync.dma_start(lists2[:], offs2)
         load_window(1, 0, T)
         nc.vector.tensor_copy(out=picked_rows[:], in_=tab_rows[:].indirect(lists[:]))
         for d in (0, 2, 1, 3):
@@ -109,8 +110,8 @@ def tile_list_tint_adjustment_kernel(
                 out=early_planes[32 * d:32 * d + 4, :].bitcast(I32).rearrange("r (a c) -> r a c", a=2),
                 in_=picked_rows[32 * d:32 * (d + 1):4, :].bitcast(I32),
             )
-        nc.sync.dma_start(out=wa_all[:], in_=wa_words.bitcast(I32).rearrange("a p c -> p a c"))
-        nc.sync.dma_start(lists2[:], offs2)
+        for a in range(2):
+            nc.sync.dma_start(out=wa_raw[a][:], in_=wa_words[a].bitcast(I32))
         nc.sync.dma_start(out=tab2_rows[ROW0:P:8, :].bitcast(I32), in_=tab2_scales[0].bitcast(I32))
         load_ws(0, 0)
         nc.sync.dma_start(out=wp_rows[ROW0:P:8, :].bitcast(I32), in_=wp_scales[0].bitcast(I32))
@@ -138,8 +139,8 @@ def tile_list_tint_adjustment_kernel(
         nc.vector.transpose(out=base_cols[:], in_=base_sorted[:])
         inv_root = held([P, PACK], F32, "inv_root")
         nc.scalar.activation(out=inv_root[:], in_=base_cols[:, 0:P:32], func=ACT.Abs_reciprocal_sqrt)
-        inv_base = held([P, PACK], F32, "inv_base")
-        nc.scalar.activation(out=inv_base[:], in_=inv_root[:], func=ACT.Square)
+        inv_base = held([P, 1], F32, "inv_base")
+        nc.scalar.activation(out=inv_base[:], in_=inv_root[:, 0:1], func=ACT.Square)
         gather(1)
 
         absorbed = [held([P, 4, KP], F32, f"absorbed{b}") for b in range(2)]
@@ -151,7 +152,7 @@ def tile_list_tint_adjustment_kernel(
                 nc.tensor.matmul_mx(
                     out=sums[c][:],
                     lhsT=picked[a][:, cols_of(c)].bitcast(E4M3), lhsT_scale=picked_plane(a, cols_of(c)),
-                    rhs=wa_all[:, a, b * (KP // 2):(b + 1) * (KP // 2)].bitcast(U8).bitcast(E2M1),
+                    rhs=wa_raw[a][:, b * (KP // 2):(b + 1) * (KP // 2)].bitcast(U8).bitcast(E2M1),
                     rhs_scale=wa_planes[:, a * H + b * KP:a * H + (b + 1) * KP],
                     start=(a == 0), stop=(a == 1),
                 )

@@ -65,7 +65,7 @@ def tile_list_tint_adjustment_kernel(
         for cleared in (tab_rows, wa_planes):
             nc.vector.memset(cleared[:].bitcast(I32), 0)
         nc.vector.memset(base_rows[:], 0.0)
-        for cleared in (early_planes, tab2_rows, wp_rows, late_planes):
+        for cleared in (tab2_rows, early_planes, wp_rows, late_planes):
             nc.vector.memset(cleared[:].bitcast(I32), 0)
         identity = held([P, P], F32, "identity", "tab_rows")
 
@@ -77,7 +77,6 @@ def tile_list_tint_adjustment_kernel(
         ws_raw = {(b, a): held([P, PACK, KP], F32, f"ws_raw{b}{a}") for b in range(2) for a in range(2)}
         picked = [held([P, S], U32, f"picked{x}") for x in range(3)]
         picked_rows = held([P, S], U8, "picked_rows")
-        picked_rows2 = held([P, S], U8, "picked_rows2")
         late_rows = held([P, S + H], U8, "late_rows")
 
         def load_window(x, c0, c1):
@@ -88,13 +87,15 @@ def tile_list_tint_adjustment_kernel(
             rows = ws[a * KP:(a + 1) * KP, b * KP:(b + 1) * KP]
             nc.sync.dma_start(out=ws_raw[b, a][:], in_=rows.rearrange("(p j) c -> p j c", j=PACK))
 
-        def gather(x):
-            nc.vector.tensor_copy(out=picked[x][:], in_=windows[x][:].bitcast(U32).indirect(table_lists[x][:]))
+        def gather(x, cols=everything):
+            entries = table_lists[x][:, cols.start // 16:cols.stop // 16]
+            nc.vector.tensor_copy(out=picked[x][:, cols], in_=windows[x][:].bitcast(U32).indirect(entries))
 
-        nc.sync.dma_start(lists[:], offs)
         load_window(0, 0, FIRST_PIECE)
+        nc.sync.dma_start(lists[:], offs)
         nc.sync.dma_start(
             out=tab_rows[0:P:4, :].bitcast(I32), in_=tab_scales.bitcast(I32).rearrange("a q c -> q a c"))
+        nc.sync.dma_start(lists2[:], offs2)
         load_window(0, FIRST_PIECE, T)
         for r in range(4):
             nc.sync.dma_start(
@@ -102,7 +103,7 @@ def tile_list_tint_adjustment_kernel(
                 in_=wa_scales[:, r:16:4, :].bitcast(I32).rearrange("a d c -> d a c"),
             )
         nc.sync.dma_start(out=base_rows[0:P:16, :], in_=base.rearrange("(b d x) -> d b x", b=2, d=4))
-        nc.sync.dma_start(lists2[:], offs2)
+        nc.sync.dma_start(out=tab2_rows[ROW0:P:8, :].bitcast(I32), in_=tab2_scales[0].bitcast(I32))
         load_window(1, 0, T)
         nc.vector.tensor_copy(out=picked_rows[:], in_=tab_rows[:].indirect(lists[:]))
         for d in (0, 2, 1, 3):
@@ -112,7 +113,6 @@ def tile_list_tint_adjustment_kernel(
             )
         for a in range(2):
             nc.sync.dma_start(out=wa_raw[a][:], in_=wa_words[a].bitcast(I32))
-        nc.sync.dma_start(out=tab2_rows[ROW0:P:8, :].bitcast(I32), in_=tab2_scales[0].bitcast(I32))
         load_ws(0, 0)
         nc.sync.dma_start(out=wp_rows[ROW0:P:8, :].bitcast(I32), in_=wp_scales[0].bitcast(I32))
         load_ws(0, 1)
@@ -141,25 +141,27 @@ def tile_list_tint_adjustment_kernel(
         nc.scalar.activation(out=inv_root[:], in_=base_cols[:, 0:P:32], func=ACT.Abs_reciprocal_sqrt)
         inv_base = held([P, 1], F32, "inv_base")
         nc.scalar.activation(out=inv_base[:], in_=inv_root[:, 0:1], func=ACT.Square)
-        gather(1)
+        gather(1, half(0))
+        gather(1, half(1))
 
         absorbed = [held([P, 4, KP], F32, f"absorbed{b}") for b in range(2)]
 
         def absorption(b):
             sums = [bank(PACK * b + c, [P, KP]) for c in range(4)]
 
-            def absorption_pass(c, a):
+            def absorption_pass(c, a, first):
                 nc.tensor.matmul_mx(
                     out=sums[c][:],
                     lhsT=picked[a][:, cols_of(c)].bitcast(E4M3), lhsT_scale=picked_plane(a, cols_of(c)),
                     rhs=wa_raw[a][:, b * (KP // 2):(b + 1) * (KP // 2)].bitcast(U8).bitcast(E2M1),
                     rhs_scale=wa_planes[:, a * H + b * KP:a * H + (b + 1) * KP],
-                    start=(a == 0), stop=(a == 1),
+                    start=first, stop=not first,
                 )
 
             for c in range(4):
-                absorption_pass(c, 0)
-                absorption_pass(c, 1)
+                opening = 0 if (b, c) == (0, 0) else 1
+                absorption_pass(c, opening, True)
+                absorption_pass(c, 1 - opening, False)
                 nc.scalar.activation(
                     out=absorbed[b][:, c, :].rearrange("p (t h i) -> p t h i", t=PACK, i=4),
                     in_=sums[c][:].rearrange("p (h t i) -> p t h i", t=PACK, i=4), func=ACT.Abs,
@@ -167,6 +169,7 @@ def tile_list_tint_adjustment_kernel(
 
         absorption(0)
         absorption(1)
+        picked_rows2 = held([P, S], U8, "picked_rows2", "window1")
         nc.vector.tensor_copy(out=picked_rows2[:], in_=tab2_rows[:].indirect(lists2[:]))
         nc.vector.tensor_copy(out=late_rows[:, 0:S].bitcast(I32), in_=picked_rows2[:].bitcast(I32))
 
@@ -208,12 +211,13 @@ def tile_list_tint_adjustment_kernel(
 
         def scattering(b, t):
             scat[b, t] = bank(PACK * b + t, [P, S])
-            for a in range(2):
+            order = (0, 1) if (b, t) == (0, 0) or b == 1 else (1, 0)
+            for a in order:
                 nc.tensor.matmul_mx(
                     out=scat[b, t][:],
                     lhsT=ws_codes[b, a, t].bitcast(E4M3), lhsT_scale=ws_plane[b, a, t],
                     rhs=picked[a][:].bitcast(E4M3), rhs_scale=picked_plane(a, everything),
-                    start=(a == 0), stop=(a == 1),
+                    start=(a == order[0]), stop=(a == order[1]),
                 )
 
         def panel_pass(target, b, t, cols):

@@ -290,7 +290,7 @@ def tile_list_tint_adjustment_kernel(
         for t in range(PACK):
             scattering(1, t)
         wp_codes = held([P, H], I32, "wp_codes", "ws_rounded112")
-        nc.gpsimd.tensor_copy(
+        nc.vector.tensor_copy(
             out=wp_codes[:].rearrange("p (b t h i) -> p b t h i", b=2, t=PACK, i=4),
             in_=wp_raw[:].rearrange("p (b h t i) -> p b t h i", b=2, t=PACK, i=4),
         )

from contextlib import ExitStack

import concourse.mybir as mybir
from concourse.masks import make_identity

K, K2, H, N, T, S = 1024, 512, 1024, 512, 2048, 512
FLOPS = 2 * S * (2 * K * H + K2 * H + H * N)

F32 = mybir.dt.float32
BF16 = mybir.dt.bfloat16
I32 = mybir.dt.int32
U32 = mybir.dt.uint32
U16 = mybir.dt.uint16
U8 = mybir.dt.uint8
E4M3 = mybir.dt.float8_e4m3fn_x4
E2M1 = mybir.dt.float4_e2m1fn_x4
ACT = mybir.ActivationFunctionType
ALU = mybir.AluOpType

P = 128
PACK = 4
KP = P * PACK
BANK = 512
HALF = S // 2
ROW0 = 4
LATE0 = 8
VSQ = 1
FIRST_PIECE = T // 4
SECOND_PIECE = 5 * T // 8
QUARTER = S // 4


def tile_list_tint_adjustment_kernel(
    tc, tab_words, tab_scales, tab2_words, tab2_scales, offs, offs2,
    wa_words, wa_scales, ws, base, wp_words, wp_scales, wc, out,
):
    nc = tc.nc
    with ExitStack() as ctx:
        keep = ctx.enter_context(tc.tile_pool(name="keep", bufs=1))
        psum = ctx.enter_context(tc.psum_pool(name="psum", bufs=1))

        def held(shape, dtype, name, tag=None):
            return keep.tile(shape, dtype, name=name, tag=tag or name, align_bytes=64)

        def bank(number, shape):
            return psum.tile(shape, F32, name="bank%d" % number, tag="bank%d" % number)

        def cols_of(q):
            return slice(q * QUARTER, (q + 1) * QUARTER)

        def half(h):
            return slice(h * HALF, (h + 1) * HALF)

        everything = slice(0, S)
        lists = keep.tile([P, S // 16], U16, name="lists")
        lists2 = keep.tile([P, S // 16], U16, name="lists2")

        tab_rows = held([P, T], U8, "tab_rows")
        tab2_rows = held([P, T], U8, "tab2_rows")
        wp_rows = held([P, H], U8, "wp_rows")
        base_rows = held([P, P], F32, "base_rows")
        early_planes = held([P, 2 * S], U8, "early_planes")
        wa_planes = held([P, 2 * H], U8, "wa_planes")
        late_planes = held([P, S + H], U8, "late_planes")
        for cleared in (tab_rows, wa_planes):
            nc.vector.memset(cleared[:].bitcast(I32), 0)
        nc.vector.memset(base_rows[:], 0.0)
        for cleared in (tab2_rows, early_planes, wp_rows, late_planes):
            nc.vector.memset(cleared[:].bitcast(I32), 0)
        identity = held([P, P], F32, "identity", "tab_rows")

        table_words = [tab_words[0], tab_words[1], tab2_words[0]]
        table_lists = [lists, lists, lists2]
        windows = [held([P, T], I32, f"window{x}") for x in range(3)]
        wa_raw = [held([P, KP], I32, f"wa_raw{a}") for a in range(2)]
        wp_raw = held([P, H], I32, "wp_raw")
        ws_raw = {(b, a): held([P, PACK, KP], F32, f"ws_raw{b}{a}") for b in range(2) for a in range(2)}
        picked = [held([P, S], U32, f"picked{x}") for x in range(3)]
        picked_rows = held([P, S], U8, "picked_rows")
        late_rows = held([P, S + H], U8, "late_rows")

        def load_window(x, c0, c1):
            words = table_words[x].rearrange("p t i -> p (t i)").bitcast(I32)
            nc.sync.dma_start(out=windows[x][:, c0:c1], in_=words[:, c0:c1])

        def load_ws(b, a):
            rows = ws[a * KP:(a + 1) * KP, b * KP:(b + 1) * KP]
            nc.sync.dma_start(out=ws_raw[b, a][:], in_=rows.rearrange("(p j) c -> p j c", j=PACK))

        def gather(x, cols=everything):
            entries = table_lists[x][:, cols.start // 16:cols.stop // 16]
            nc.vector.tensor_copy(out=picked[x][:, cols], in_=windows[x][:].bitcast(U32).indirect(entries))

        load_window(0, 0, FIRST_PIECE)
        nc.sync.dma_start(lists[:], offs)
        nc.sync.dma_start(
            out=tab_rows[0:P:4, :].bitcast(I32), in_=tab_scales.bitcast(I32).rearrange("a q c -> q a c"))
        nc.sync.dma_start(lists2[:], offs2)
        load_window(0, FIRST_PIECE, T)
        for r in range(4):
            nc.sync.dma_start(
                out=wa_planes[r:P:32, :].bitcast(I32).rearrange("d (a c) -> d a c", a=2),
                in_=wa_scales[:, r:16:4, :].bitcast(I32).rearrange("a d c -> d a c"),
            )
        nc.sync.dma_start(out=base_rows[0:P:16, :], in_=base.rearrange("(b d x) -> d b x", b=2, d=4))
        nc.sync.dma_start(out=tab2_rows[ROW0:P:8, :].bitcast(I32), in_=tab2_scales[0].bitcast(I32))
        load_window(1, 0, T)
        nc.vector.tensor_copy(out=picked_rows[:], in_=tab_rows[:].indirect(lists[:]))
        for d in (0, 2, 1, 3):
            nc.sync.dma_start(
                out=early_planes[32 * d:32 * d + 4, :].bitcast(I32).rearrange("r (a c) -> r a c", a=2),
                in_=picked_rows[32 * d:32 * (d + 1):4, :].bitcast(I32),
            )
        for a in range(2):
            nc.sync.dma_start(out=wa_raw[a][:], in_=wa_words[a].bitcast(I32))
        load_ws(0, 0)
        nc.sync.dma_start(out=wp_rows[ROW0:P:8, :].bitcast(I32), in_=wp_scales[0].bitcast(I32))
        load_ws(0, 1)
        load_ws(1, 0)
        load_ws(1, 1)
        nc.sync.dma_start(out=wp_raw[:], in_=wp_words[0].rearrange("p c i -> p (c i)").bitcast(I32))
        load_window(2, 0, T)

        def picked_plane(x, cols):
            return early_planes[:, x * S + cols.start:x * S + cols.stop] if x < 2 else late_planes[LATE0:P, cols]

        def wp_plane(b, t):
            c0 = S + b * KP + t * P
            return late_planes[LATE0:P, c0:c0 + P]

        make_identity(nc, identity[:])
        gather(0)
        base_sorted = held([P, P], F32, "base_sorted")
        nc.vector.tensor_copy(
            out=base_sorted[:].rearrange("p (t h i) -> p t h i", t=PACK, i=4),
            in_=base_rows[:].rearrange("p (h t i) -> p t h i", t=PACK, i=4),
        )
        base_cols = held([P, P], F32, "base_cols")
        nc.vector.transpose(out=base_cols[:], in_=base_sorted[:])
        inv_root = held([P, PACK], F32, "inv_root")
        nc.scalar.activation(out=inv_root[:], in_=base_cols[:, 0:P:32], func=ACT.Abs_reciprocal_sqrt)
        inv_base = held([P, 1], F32, "inv_base")
        nc.scalar.activation(out=inv_base[:], in_=inv_root[:, 0:1], func=ACT.Square)
        gather(1, half(0))
        gather(1, half(1))

        absorbed = [held([P, 4, KP], F32, f"absorbed{b}") for b in range(2)]

        def absorption(b):
            sums = [bank(PACK * b + c, [P, KP]) for c in range(4)]

            def absorption_pass(c, a, first):
                nc.tensor.matmul_mx(
                    out=sums[c][:],
                    lhsT=picked[a][:, cols_of(c)].bitcast(E4M3), lhsT_scale=picked_plane(a, cols_of(c)),
                    rhs=wa_raw[a][:, b * (KP // 2):(b + 1) * (KP // 2)].bitcast(U8).bitcast(E2M1),
                    rhs_scale=wa_planes[:, a * H + b * KP:a * H + (b + 1) * KP],
                    start=first, stop=not first,
                )

            for c in range(4):
                opening = 0 if (b, c) == (0, 0) else 1
                absorption_pass(c, opening, True)
                absorption_pass(c, 1 - opening, False)
                nc.scalar.activation(
                    out=absorbed[b][:, c, :].rearrange("p (t h i) -> p t h i", t=PACK, i=4),
                    in_=sums[c][:].rearrange("p (h t i) -> p t h i", t=PACK, i=4), func=ACT.Abs,
                )

        absorption(0)
        absorption(1)
        picked_rows2 = held([P, S], U8, "picked_rows2", "window1")
        nc.vector.tensor_copy(out=picked_rows2[:], in_=tab2_rows[:].indirect(lists2[:]))
        nc.vector.tensor_copy(out=late_rows[:, 0:S].bitcast(I32), in_=picked_rows2[:].bitcast(I32))

        def turn(target, b, c, t):
            nc.tensor.transpose(target, absorbed[b][:, c, t * P:(t + 1) * P], identity[:])

        ws_rounded, ws_codes, ws_plane, whole = {}, {}, {}, {}

        def round_ws(b, a, t0, slots):
            ws_rounded[b, a, t0] = held([P, slots * KP], BF16, f"ws_rounded{b}{a}{t0}")
            nc.vector.tensor_copy(
                out=ws_rounded[b, a, t0][:].rearrange("p (t h i j) -> p t h j i", t=slots, i=4, j=PACK),
                in_=ws_raw[b, a][:].rearrange("p j (h t i) -> p t h j i", t=PACK, i=4)[:, t0:t0 + slots],
            )

        def quantize(rounded, width, name, tag=None):
            codes = held([P, width], U32, name + "_codes", tag)
            plane = held([P, width], U8, name + "_plane")
            nc.vector.quantize_mx(out=codes[:].bitcast(E4M3), scales=plane[:], in_=rounded)
            return codes, plane

        def quantize_ws(b, a, t0, slots):
            codes, plane = quantize(ws_rounded[b, a, t0][:], slots * P, f"ws{b}{a}{t0}")
            whole[b, a, t0] = (codes, plane)
            for s in range(slots):
                ws_codes[b, a, t0 + s] = codes[:, s * P:(s + 1) * P]
                ws_plane[b, a, t0 + s] = plane[:, s * P:(s + 1) * P]

        def prepare_ws(b, a, slots):
            starts = list(range(0, PACK, slots))
            round_ws(b, a, starts[0], slots)
            for before, t0 in zip(starts, starts[1:]):
                round_ws(b, a, t0, slots)
                quantize_ws(b, a, before, slots)
            quantize_ws(b, a, starts[-1], slots)

        squares = [held([P, PACK, S], F32, f"squares{b}") for b in range(2)]
        scat = {}

        def scattering(b, t):
            scat[b, t] = bank(PACK * b + t, [P, S])
            order = (0, 1) if (b, t) == (0, 0) or b == 1 else (1, 0)
            for a in order:
                nc.tensor.matmul_mx(
                    out=scat[b, t][:],
                    lhsT=ws_codes[b, a, t].bitcast(E4M3), lhsT_scale=ws_plane[b, a, t],
                    rhs=picked[a][:].bitcast(E4M3), rhs_scale=picked_plane(a, everything),
                    start=(a == order[0]), stop=(a == order[1]),
                )

        def panel_pass(target, b, t, cols):
            c0 = b * KP + t * P
            nc.tensor.matmul_mx(
                out=target,
                lhsT=wp_codes[:, c0:c0 + P].bitcast(E4M3), lhsT_scale=wp_plane(b, t),
                rhs=picked[2][:, cols].bitcast(E4M3), rhs_scale=picked_plane(2, cols),
                start=True, stop=True,
            )

        round_ws(0, 0, 0, PACK)
        nc.vector.tensor_copy(
            out=late_rows[:, S:].bitcast(I32).rearrange("p (s t g e) -> p s g t e", t=PACK, g=8, e=4),
            in_=wp_rows[:].bitcast(I32).rearrange("p (s g e t) -> p s g t e", t=PACK, g=8, e=4),
        )
        quantize_ws(0, 0, 0, PACK)
        for r in range(4):
            nc.sync.dma_start(
                out=late_planes[LATE0 + r:P:32, :].bitcast(I32), in_=late_rows[ROW0 + 8 * r:P:32, :].bitcast(I32))
        wc_raw = {}
        for b in range(2):
            wc_raw[b] = held([P, PACK, N], F32, f"wc_raw{b}")
            rows = wc[b * KP:(b + 1) * KP, :].rearrange("(h t i) n -> t h i n", t=PACK, i=4)
            for t in range(PACK):
                nc.sync.dma_start(out=wc_raw[b][:, t, :], in_=rows[t])
        prepare_ws(0, 1, 1)

        def square_sum(t):
            nc.scalar.activation(out=squares[0][:, t, :], in_=scat[0, t][:], func=ACT.Square, scale=inv_root[:, t:t + 1])

        def inverse_root(t):
            nc.scalar.activation(out=squares[0][:, t, :], in_=squares[0][:, t, :], func=ACT.Abs_reciprocal_sqrt, bias=1.0)

        def square_root_slot(t):
            if t >= VSQ:
                nc.scalar.activation(out=squares[0][:, t, :], in_=squares[0][:, t, :], func=ACT.Square, scale=inv_root[:, t:t + 1])

        reciprocal = {t: squares[0][:, t, :] for t in range(PACK)}

        def square_on_vector(t):
            part = squares[0][:, t, :]
            reciprocal[t] = held([P, S], F32, f"reciprocal{t}", "ws_raw10")[:]
            nc.vector.scalar_tensor_tensor(
                out=reciprocal[t], in0=part, scalar=inv_base[:, t:t + 1], in1=part, op0=ALU.mult, op1=ALU.mult)

        for t in range(PACK):
            scattering(0, t)
            square_sum(t)
            if t >= 2:
                square_root_slot(t - 2)
            if t >= 1:
                inverse_root(t - 1)
        inverse_root(PACK - 1)
        for t in (PACK - 2, PACK - 1):
            square_root_slot(t)

        slot_quot = {}

        def divide_slot(t, target):
            numerator = bank(t, [P, S])
            for c in range(4):
                turn(numerator[:, cols_of(c)], 0, c, t)
            slot_quot[t] = target
            nc.vector.tensor_tensor(out=target, in0=numerator[:], in1=reciprocal[t], op=ALU.mult)

        prepare_ws(1, 0, 2)
        square_on_vector(0)
        prepare_ws(1, 1, 2)
        for t in range(PACK):
            scattering(1, t)
        wp_codes = held([P, H], I32, "wp_codes", "ws_rounded112")
        nc.vector.tensor_copy(
            out=wp_codes[:].rearrange("p (b t h i) -> p b t h i", b=2, t=PACK, i=4),
            in_=wp_raw[:].rearrange("p (b h t i) -> p b t h i", b=2, t=PACK, i=4),
        )
        first_quot = held([P, PACK - 1, S], F32, "first_quot", "ws_raw11")
        for t in range(PACK - 1):
            divide_slot(t, first_quot[:, t, :])
        gather(2)
        divide_slot(PACK - 1, held([P, S], F32, "last_quot", "window2")[:])
        diffs0 = held([P, PACK, S], F32, "diffs0")
        for t in range(PACK):
            panel = bank(t, [P, S])
            panel_pass(panel[:], 0, t, everything)
            nc.vector.tensor_tensor(out=diffs0[:, t, :], in0=panel[:], in1=slot_quot[t], op=ALU.subtract)

        wc_rounded = {}

        def round_wc(engine, b, n0, n1, tag=None):
            wc_rounded[b, n0] = held([P, PACK * (n1 - n0)], BF16, f"wc_rounded{b}{n0}", tag)
            if engine is nc.vector:
                nc.vector.tensor_copy(
                    out=wc_rounded[b, n0][:].rearrange("p (c i t) -> p c t i", t=PACK, i=4),
                    in_=wc_raw[b][:, :, n0:n1].rearrange("p t (c i) -> p c t i", i=4),
                )
                return
            nc.gpsimd.tensor_scalar(
                out=wc_rounded[b, n0][:].rearrange("p (c t) -> p c t", t=PACK),
                in0=wc_raw[b][:, :, n0:n1].rearrange("p t c -> p c t"),
                scalar1=1.0, scalar2=0.0, op0=ALU.mult, op1=ALU.add,
            )

        round_wc(nc.gpsimd, 0, 0, N)
        round_wc(nc.gpsimd, 1, 0, N)
        inverse = [held([P, PACK, QUARTER], F32, f"inverse{q}") for q in range(4)]
        products = {}
        diffs1 = held([P, PACK, S], F32, "diffs1")

        def square_whole(t):
            nc.scalar.activation(out=squares[1][:, t, :], in_=scat[1, t][:], func=ACT.Square)

        def inverse_root_half(t, h):
            part = squares[1][:, t, half(h)]
            nc.scalar.activation(
                out=part, in_=part, func=ACT.Abs_reciprocal_sqrt, bias=base_cols[:, 32 * t + 16:32 * t + 17])

        def square_quarter(q):
            nc.scalar.activation(out=inverse[q][:], in_=squares[1][:, :, cols_of(q)], func=ACT.Square)

        def divide_quarter(q, number):
            numerator = bank(number, [P, PACK, QUARTER])
            for t in range(PACK):
                turn(numerator[:, t, :], 1, q, t)
            products[q] = held([P, PACK, QUARTER], F32, f"product{q}", ("ws_raw11", "window2", None, None)[q])
            nc.vector.tensor_tensor(out=products[q][:], in0=numerator[:], in1=inverse[q][:], op=ALU.mult)

        def subtract_quarter(q, number):
            panel = bank(number, [P, PACK, QUARTER])
            for t in range(PACK):
                panel_pass(panel[:, t, :], 1, t, cols_of(q))
            nc.vector.tensor_tensor(out=diffs1[:, :, cols_of(q)], in0=panel[:], in1=products[q][:], op=ALU.subtract)

        d_codes, wc_codes, wc_plane = [{}, {}], {}, {}

        def distance(target, source):
            nc.scalar.activation(
                out=target.rearrange("p (c i t) -> p c t i", t=PACK, i=4),
                in_=source.rearrange("p t (c i) -> p c t i", i=4), func=ACT.Abs,
            )

        def distance_on_vector(target, source):
            walk = source.rearrange("p t (c i) -> p c t i", i=4)
            for c0 in range(0, 32, 32):
                nc.vector.scalar_tensor_tensor(
                    out=target.rearrange("p (c i t) -> p c t i", t=PACK, i=4), in0=walk, scalar=-1.0, in1=walk,
                    op0=ALU.mult, op1=ALU.max,
                )

        def quantize_d(b, j0, width, rounded):
            codes, plane = quantize(rounded, width, f"d{b}{j0}")
            d_codes[b][j0] = (codes, plane, width)

        def quantize_wc(b, n0, n1, first=None):
            first = n0 if first is None else first
            codes, plane = quantize(wc_rounded[b, first][:, PACK * (n0 - first):PACK * (n1 - first)], n1 - n0, f"wc{b}{n0}")
            for n in range(n0 // P, n1 // P):
                wc_codes[b, n] = codes[:, n * P - n0:(n + 1) * P - n0]
                wc_plane[b, n] = plane[:, n * P - n0:(n + 1) * P - n0]

        def second_stage(j0, width, n0, count, number, copy):
            acc = bank(number, [P, count, width])
            passes = [(b, c0, n) for b in range(2) for c0 in d_codes[b] if j0 <= c0 < j0 + width
                      for n in range(n0, n0 + count)]
            for number_of_pass, (b, c0, n) in enumerate(passes):
                codes, plane, columns = d_codes[b][c0]
                nc.tensor.matmul_mx(
                    out=acc[:, n - n0, c0 - j0:c0 - j0 + columns],
                    lhsT=wc_codes[b, n].bitcast(E4M3), lhsT_scale=wc_plane[b, n],
                    rhs=codes[:].bitcast(E4M3), rhs_scale=plane[:],
                    start=(number_of_pass == 0), stop=(number_of_pass == len(passes) - 1),
                )
            result = held([P, count, width], F32, f"result{j0}{n0}")
            copy(out=result[:], in_=acc[:])
            nc.sync.dma_start(
                out=out[n0 * P:(n0 + count) * P, j0:j0 + width].rearrange("(n p) j -> p n j", p=P),
                in_=result[:],
            )

        rounded = [held([P, PACK * S], BF16, f"rounded{b}") for b in range(2)]

        def rounded_cols(b, j0, width):
            return rounded[b][:, PACK * j0:PACK * (j0 + width)]

        square_whole(0)
        square_whole(1)
        square_whole(2)
        square_whole(3)
        inverse_root_half(0, 0)
        inverse_root_half(1, 0)
        inverse_root_half(2, 0)
        inverse_root_half(3, 0)
        inverse_root_half(0, 1)
        square_quarter(0)
        square_quarter(1)
        inverse_root_half(1, 1)
        inverse_root_half(2, 1)
        inverse_root_half(3, 1)
        distance(rounded_cols(0, 0 * QUARTER, QUARTER), diffs0[:, :, cols_of(0)])
        square_quarter(2)
        square_quarter(3)
        divide_quarter(0, 4)
        divide_quarter(1, 5)
        subtract_quarter(0, 6)
        subtract_quarter(1, 7)
        divide_quarter(2, 0)
        divide_quarter(3, 1)
        subtract_quarter(2, 2)
        subtract_quarter(3, 3)
        distance(rounded_cols(0, 1 * QUARTER, QUARTER), diffs0[:, :, cols_of(1)])
        distance(rounded_cols(1, 0, HALF), diffs1[:, :, 0:0 + HALF])
        distance(rounded_cols(0, HALF, HALF), diffs0[:, :, half(1)])
        distance(rounded_cols(1, HALF, QUARTER), diffs1[:, :, HALF:HALF + QUARTER])
        distance(rounded_cols(1, 3 * QUARTER, QUARTER), diffs1[:, :, 3 * QUARTER:3 * QUARTER + QUARTER])
        warm_codes, warm_plane = whole[0, 0, 0]
        unread = bank(0, [P, S])
        for x in range(4):
            nc.tensor.matmul_mx(
                out=unread[:], lhsT=ws_codes[1, 0, 0].bitcast(E4M3), lhsT_scale=ws_plane[1, 0, 0],
                rhs=warm_codes[:].bitcast(E4M3), rhs_scale=warm_plane[:], start=True, stop=True,
            )
        quantize_wc(0, 0, 512, 0)
        quantize_d(0, 0, HALF, rounded_cols(0, 0, HALF))
        quantize_wc(1, 0, 256, 0)
        quantize_d(1, 0, HALF, rounded_cols(1, 0, HALF))
        quantize_wc(1, 256, 512, 0)
        quantize_d(0, HALF, HALF, rounded_cols(0, HALF, HALF))
        quantize_d(1, 2 * QUARTER, QUARTER, rounded_cols(1, 2 * QUARTER, QUARTER))
        quantize_d(1, 3 * QUARTER, QUARTER, rounded_cols(1, 3 * QUARTER, QUARTER))
        second_stage(0, HALF, 0, 1, 4, nc.scalar.copy)
        second_stage(0, HALF, 1, 1, 5, nc.scalar.copy)
        second_stage(0, HALF, 2, 1, 6, nc.vector.tensor_copy)
        second_stage(0, HALF, 3, 1, 7, nc.scalar.copy)
        second_stage(HALF, HALF, 0, 1, 0, nc.vector.tensor_copy)
        second_stage(HALF, HALF, 1, 1, 1, nc.scalar.copy)
        second_stage(HALF, HALF, 2, 1, 2, nc.vector.tensor_copy)
        second_stage(HALF, HALF, 3, 1, 3, nc.scalar.copy)
